import numpy as np
import ml_dtypes


def mxq(x, axis, fmt="e4m3"):
    dtype, down = {"e4m3": (ml_dtypes.float8_e4m3fn, 7), "e5m2": (ml_dtypes.float8_e5m2, 14)}[fmt]
    v = np.moveaxis(np.asarray(x, np.float32).astype(ml_dtypes.bfloat16).astype(np.float64), axis, -1)
    blocks = v.reshape(v.shape[:-1] + (-1, 32))
    amax = np.abs(blocks).max(-1, keepdims=True)
    byte = np.maximum(np.where(amax > 0, np.frexp(amax)[1] - 1 + 127, 0) - down, 1)
    scale = np.exp2(byte - 127.0)
    codes = (blocks / scale).astype(np.float32).astype(dtype).astype(np.float64)
    return np.moveaxis((codes * scale).reshape(v.shape), -1, axis)


WIDE = False


def mx_kscale(k):
    if not WIDE:
        return np.ones(k)
    levels = np.array([18, -18])
    if k % 512:
        return np.exp2(np.random.permutation(np.resize(levels, k // 32))).repeat(32)
    a = np.empty((k // 512, 16))
    for p in range(k // 512):
        a[p, :8] = np.random.permutation(np.resize(levels, 8))
        for g in range(8):
            far = levels[np.abs(levels - a[p, g]) >= 10]
            a[p, g + 8] = far[np.random.randint(len(far))]
    return np.exp2(a.ravel()).repeat(32)


def f64(x):
    return np.asarray(x).astype(np.float64)


def striped(idx):
    return np.tile(np.asarray(idx).reshape(-1, 16).T, (8, 1)).astype(np.uint16)


def unstriped(offs):
    return offs[:16].T.reshape(-1).astype(np.int64)


def setup_inputs():
    n = np.random.standard_normal
    uni = np.random.uniform
    idx = np.random.permutation(2048)[:1024]
    bag = np.random.permutation(np.repeat(np.arange(512), 2))
    slot = np.argsort(bag, kind="stable")
    f_m = mx_kscale(512)
    return {
        "vT": (0.5 * n((512, 2048))).astype(np.float32),
        "W": (n((512, 512)) / np.sqrt(512) * f_m[:, None]).astype(np.float32),
        "dz": (n((512, 512)) / f_m[:, None]).astype(np.float32),
        "gy": np.tile(uni(0.75, 1.3, 512), (128, 1)).astype(np.float32),
        "offs": striped(idx),
        "boffs": striped(bag),
        "soffs": striped(slot),
    }


def reference(vT, W, dz, gy, offs, boffs, soffs):
    idx = unstriped(offs)
    bag = unstriped(boffs)
    slot = unstriped(soffs)
    vT_c = f64(vT)[:, idx]
    vT_c_y = vT_c[:, slot]
    s = vT_c_y.reshape(512, 512, 2).sum(-1)
    ds = mxq(f64(W), 0, "e4m3").T @ mxq(f64(dz), 0, "e5m2")
    e = ds + f64(gy)[:1] * s
    e_c = e[:, bag]
    gy_c = f64(gy)[:1][:, bag]
    dv = e_c - gy_c * vT_c
    out = np.zeros((512, 2048))
    out[:, idx] = dv
    return out

@@ -1,0 +1,189 @@
+from contextlib import ExitStack
+
+import concourse.mybir as mybir
+from concourse.masks import make_identity
+
+D, M, X, C, T = 512, 512, 512, 1024, 2048
+FLOPS = 2 * M * D * X
+
+F32 = mybir.dt.float32
+BF16 = mybir.dt.bfloat16
+U32 = mybir.dt.uint32
+U16 = mybir.dt.uint16
+U8 = mybir.dt.uint8
+E4M3X4 = mybir.dt.float8_e4m3fn_x4
+E5M2X4 = mybir.dt.float8_e5m2_x4
+COPY = mybir.ActivationFunctionType.Copy
+ADD = mybir.AluOpType.add
+
+P = 128
+PACK = 4
+BANK = 512
+D_TILES = D // P
+X_BLOCKS = X // P
+C_BLOCKS = C // P
+WINDOW = 1376
+
+
+def tile_attend_gfm_bi_kernel(tc, vT, W, dz, gy, offs, boffs, soffs, out):
+    nc = tc.nc
+    with ExitStack() as ctx:
+        keep = ctx.enter_context(tc.tile_pool(name="keep", bufs=1))
+        ring = ctx.enter_context(tc.tile_pool(name="ring", bufs=2))
+        psum = ctx.enter_context(tc.psum_pool(name="psum", bufs=1))
+
+        bag_list = keep.tile([P, C // 16], U16, name="bag_list")
+        idx_list = keep.tile([P, C // 16], U16, name="idx_list")
+        slot_list = keep.tile([P, C // 16], U16, name="slot_list")
+        gy_win = keep.tile([P, WINDOW], F32, name="gy_win")
+        tables = [keep.tile([P, T], F32, name="table%d" % t) for t in range(D_TILES)]
+        w_raw = keep.tile([P, PACK, D], F32, name="w_raw")
+        dz_raw = keep.tile([P, PACK, X], F32, name="dz_raw")
+
+        nc.sync.dma_start(bag_list[:], boffs)
+        nc.sync.dma_start(gy_win[:, :X], gy)
+        nc.sync.dma_start(idx_list[:], offs)
+        nc.sync.dma_start(tables[0][:], vT[0:P, :])
+        nc.sync.dma_start(slot_list[:], soffs)
+        nc.sync.dma_start(tables[1][:], vT[P : 2 * P, :])
+        nc.sync.dma_start(w_raw[:], W.rearrange("(p j) d -> p j d", j=PACK))
+        nc.sync.dma_start(dz_raw[:], dz.rearrange("(p j) x -> p j x", j=PACK))
+        for t in range(2, D_TILES):
+            nc.sync.dma_start(tables[t][:], vT[t * P : (t + 1) * P, :])
+
+        picked = keep.tile([P, (D_TILES - 1) * C + WINDOW], F32, name="picked")
+        e_all = keep.tile([P, (D_TILES - 1) * X + WINDOW], F32, name="e_all")
+        placed = [keep.tile([P, T], F32, name="placed%d" % k) for k in range(2)]
+        identity = keep.tile([P, P], F32, name="identity")
+
+        nc.vector.memset(gy_win[:, X:], 0.0)
+        nc.vector.memset(picked[:, D_TILES * C :], 0.0)
+        nc.vector.memset(e_all[:, D_TILES * X :], 0.0)
+        nc.vector.memset(placed[0][:], 0.0)
+        make_identity(nc, identity[:])
+        nc.gpsimd.memset(placed[1][:], 0.0)
+
+        def turn(dst, src, start=True, stop=True):
+            nc.tensor.matmul(dst, src, identity[:], start=start, stop=stop, is_transpose=True)
+
+        def block(b):
+            return slice(b * P, (b + 1) * P)
+
+        gy_c = keep.tile([P, C], F32, name="gy_c")
+        nc.vector.tensor_copy(gy_c[:], gy_win[:].indirect(bag_list[:]))
+        gy_col = keep.tile([P, X_BLOCKS], F32, name="gy_col")
+        neg_gy_c_col = keep.tile([P, C_BLOCKS], F32, name="neg_gy_c_col")
+        bank = psum.tile([P, X_BLOCKS, P], F32, name="bank", tag="fwd", bufs=3)
+        for b in range(X_BLOCKS):
+            turn(bank[:, b, :], gy_win[:, block(b)])
+        nc.scalar.copy(gy_col[:], bank[:, :, 0])
+        for h in range(2):
+            bank = psum.tile([P, 4, P], F32, name="bank", tag="fwd", bufs=3)
+            for b in range(4):
+                turn(bank[:, b, :], gy_c[:, block(4 * h + b)])
+            nc.scalar.activation(neg_gy_c_col[:, 4 * h : 4 * h + 4], bank[:, :, 0], COPY, scale=-1.0)
+
+        def picked_at(t):
+            return (D_TILES - 1 - t) * C
+
+        def e_at(t):
+            return (D_TILES - 1 - t) * X
+
+        def gather_table(t):
+            nc.vector.tensor_copy(picked[:, picked_at(t) : picked_at(t) + C], tables[t][:].indirect(idx_list[:]))
+
+        by_sample = [keep.tile([P, C], F32, name="by_sample%d" % t) for t in range(D_TILES)]
+        own_term = [keep.tile([P, C], F32, name="own_term%d" % t) for t in range(D_TILES)]
+
+        def gather_bags(t):
+            nc.vector.tensor_copy(by_sample[t][:], picked[:, picked_at(t) : picked_at(t) + WINDOW].indirect(slot_list[:]))
+
+        def make_own_term(t):
+            for h in range(2):
+                fwd = psum.tile([P, 4, P], F32, name="fwd", tag="fwd", bufs=3)
+                for b in range(4):
+                    at = picked_at(t) + (4 * h + b) * P
+                    turn(fwd[:, b, :], picked[:, at : at + P])
+                scaled = ring.tile([P, 4, P], F32, name="scaled", tag="scaled", bufs=3)
+                for b in range(4):
+                    k = 4 * h + b
+                    nc.scalar.activation(scaled[:, b, :], fwd[:, b, :], COPY, scale=neg_gy_c_col[:, k : k + 1])
+                back = psum.tile([P, 4, P], F32, name="back", tag="back", bufs=3)
+                for b in range(4):
+                    turn(back[:, b, :], scaled[:, b, :])
+                nc.scalar.copy(own_term[t][:, h * BANK : (h + 1) * BANK], back[:].rearrange("p b c -> p (b c)"))
+
+        w_codes = keep.tile([P, D], U32, name="w_codes", align_bytes=64)
+        w_scales = keep.tile([P, D], U8, name="w_scales", align_bytes=64)
+        dz_codes = keep.tile([P, X], U32, name="dz_codes", align_bytes=64)
+        dz_scales = keep.tile([P, X], U8, name="dz_scales", align_bytes=64)
+        ds_t = keep.tile([P, X_BLOCKS, D], F32, name="ds_t")
+
+        def dense_gradient():
+            for raw, codes, scales, fmt, name in (
+                (w_raw, w_codes, w_scales, E4M3X4, "w_grouped"),
+                (dz_raw, dz_codes, dz_scales, E5M2X4, "dz_grouped"),
+            ):
+                grouped = keep.tile([P, BANK, PACK], BF16, name=name, align_bytes=64)
+                nc.scalar.copy(grouped[:], raw[:].rearrange("p j w -> p w j"))
+                nc.vector.quantize_mx(out=codes[:].bitcast(fmt), scales=scales[:], in_=grouped[:].rearrange("p w j -> p (w j)"))
+            for b in range(X_BLOCKS):
+                acc = psum.tile([P, D], F32, name="acc", tag="acc", bufs=2)
+                nc.tensor.matmul_mx(
+                    out=acc[:],
+                    lhsT=dz_codes[:, block(b)].bitcast(E5M2X4),
+                    lhsT_scale=dz_scales[:, block(b)],
+                    rhs=w_codes[:].bitcast(E4M3X4),
+                    rhs_scale=w_scales[:],
+                    start=True,
+                    stop=True,
+                )
+                nc.scalar.copy(ds_t[:, b, :], acc[:])
+
+        def make_e(t):
+            fwd = psum.tile([P, 4, P], F32, name="fwd", tag="fwd", bufs=3)
+            pairs = by_sample[t][:].rearrange("p (x j) -> p j x", j=2)
+            for b in range(X_BLOCKS):
+                turn(fwd[:, b, :], pairs[:, 0, block(b)], start=True, stop=False)
+                turn(fwd[:, b, :], pairs[:, 1, block(b)], start=False, stop=True)
+            scaled = ring.tile([P, 4, P], F32, name="scaled", tag="scaled", bufs=3)
+            for b in range(X_BLOCKS):
+                nc.scalar.activation(scaled[:, b, :], fwd[:, b, :], COPY, scale=gy_col[:, b : b + 1])
+            back = psum.tile([P, 4, P], F32, name="back", tag="back", bufs=3)
+            for b in range(X_BLOCKS):
+                turn(back[:, b, :], ds_t[:, b, block(t)], start=True, stop=False)
+                turn(back[:, b, :], scaled[:, b, :], start=False, stop=True)
+            nc.scalar.copy(e_all[:, e_at(t) : e_at(t) + X], back[:].rearrange("p b c -> p (b c)"))
+
+        e_c = [keep.tile([P, C], F32, name="e_c%d" % t) for t in range(D_TILES)]
+
+        def gather_e(t):
+            nc.vector.tensor_copy(e_c[t][:], e_all[:, e_at(t) : e_at(t) + WINDOW].indirect(bag_list[:]))
+
+        def place(t):
+            window = placed[t % 2]
+            nc.vector.tensor_tensor(window[:].indirect(idx_list[:]), e_c[t][:], own_term[t][:], ADD)
+            rows = out[t * P : (t + 1) * P, :]
+            if t + 1 < D_TILES:
+                nc.sync.dma_start(rows, window[:])
+            else:
+                nc.sync.dma_start(rows[:, : T // 2], window[:, : T // 2])
+                nc.scalar.dma_start(rows[:, T // 2 :], window[:, T // 2 :])
+
+        gather_table(0)
+        gather_table(1)
+        gather_bags(0)
+        make_own_term(0)
+        dense_gradient()
+        make_e(0)
+        for t in range(1, D_TILES):
+            if t + 1 < D_TILES:
+                gather_table(t + 1)
+            gather_bags(t)
+            make_own_term(t)
+            make_e(t)
+        gather_e(0)
+        for t in range(D_TILES):
+            if t + 1 < D_TILES:
+                gather_e(t + 1)
+            place(t)

@@ -36,7 +36,7 @@ def tile_attend_gfm_bi_kernel(tc, vT, W, dz, gy, offs, boffs, soffs, out):
         idx_list = keep.tile([P, C // 16], U16, name="idx_list")
         slot_list = keep.tile([P, C // 16], U16, name="slot_list")
         gy_win = keep.tile([P, WINDOW], F32, name="gy_win")
-        tables = [keep.tile([P, T], F32, name="table%d" % t) for t in range(D_TILES)]
+        tables = [keep.tile([P, T], F32, name="table%d" % t, tag="table%d" % t) for t in range(D_TILES)]
         w_raw = keep.tile([P, PACK, D], F32, name="w_raw")
         dz_raw = keep.tile([P, PACK, X], F32, name="dz_raw")
 
@@ -53,15 +53,12 @@ def tile_attend_gfm_bi_kernel(tc, vT, W, dz, gy, offs, boffs, soffs, out):
 
         picked = keep.tile([P, (D_TILES - 1) * C + WINDOW], F32, name="picked")
         e_all = keep.tile([P, (D_TILES - 1) * X + WINDOW], F32, name="e_all")
-        placed = [keep.tile([P, T], F32, name="placed%d" % k) for k in range(2)]
         identity = keep.tile([P, P], F32, name="identity")
 
         nc.vector.memset(gy_win[:, X:], 0.0)
-        nc.vector.memset(picked[:, D_TILES * C :], 0.0)
-        nc.vector.memset(e_all[:, D_TILES * X :], 0.0)
-        nc.vector.memset(placed[0][:], 0.0)
         make_identity(nc, identity[:])
-        nc.gpsimd.memset(placed[1][:], 0.0)
+        nc.gpsimd.memset(picked[:, D_TILES * C :], 0.0)
+        nc.gpsimd.memset(e_all[:, D_TILES * X :], 0.0)
 
         def turn(dst, src, start=True, stop=True):
             nc.tensor.matmul(dst, src, identity[:], start=start, stop=stop, is_transpose=True)
@@ -73,12 +70,12 @@ def tile_attend_gfm_bi_kernel(tc, vT, W, dz, gy, offs, boffs, soffs, out):
         nc.vector.tensor_copy(gy_c[:], gy_win[:].indirect(bag_list[:]))
         gy_col = keep.tile([P, X_BLOCKS], F32, name="gy_col")
         neg_gy_c_col = keep.tile([P, C_BLOCKS], F32, name="neg_gy_c_col")
-        bank = psum.tile([P, X_BLOCKS, P], F32, name="bank", tag="fwd", bufs=3)
+        bank = psum.tile([P, X_BLOCKS, P], F32, name="bank", tag="bank", bufs=8)
         for b in range(X_BLOCKS):
             turn(bank[:, b, :], gy_win[:, block(b)])
         nc.scalar.copy(gy_col[:], bank[:, :, 0])
         for h in range(2):
-            bank = psum.tile([P, 4, P], F32, name="bank", tag="fwd", bufs=3)
+            bank = psum.tile([P, 4, P], F32, name="bank", tag="bank", bufs=8)
             for b in range(4):
                 turn(bank[:, b, :], gy_c[:, block(4 * h + b)])
             nc.scalar.activation(neg_gy_c_col[:, 4 * h : 4 * h + 4], bank[:, :, 0], COPY, scale=-1.0)
@@ -98,20 +95,34 @@ def tile_attend_gfm_bi_kernel(tc, vT, W, dz, gy, offs, boffs, soffs, out):
         def gather_bags(t):
             nc.vector.tensor_copy(by_sample[t][:], picked[:, picked_at(t) : picked_at(t) + WINDOW].indirect(slot_list[:]))
 
-        def make_own_term(t):
-            for h in range(2):
-                fwd = psum.tile([P, 4, P], F32, name="fwd", tag="fwd", bufs=3)
+        def scale_columns(pair, source, factor, addend, result):
+            scaled = ring.tile([P, 4, 2, P], F32, name="scaled", tag="scaled", bufs=3)
+            for half in range(2):
+                fwd = psum.tile([P, 2, 2, P], F32, name="fwd", tag="bank", bufs=8)
+                for i in range(2):
+                    for u in range(2):
+                        parts = source(2 * pair + u, 2 * half + i)
+                        for n, part in enumerate(parts):
+                            turn(fwd[:, i, u, :], part, start=(n == 0), stop=(n == len(parts) - 1))
+                for i in range(2):
+                    b = 2 * half + i
+                    nc.scalar.activation(scaled[:, b, :, :], fwd[:, i, :, :], COPY, scale=factor(b))
+            for u in range(2):
+                back = psum.tile([P, 4, P], F32, name="back", tag="bank", bufs=8)
                 for b in range(4):
-                    at = picked_at(t) + (4 * h + b) * P
-                    turn(fwd[:, b, :], picked[:, at : at + P])
-                scaled = ring.tile([P, 4, P], F32, name="scaled", tag="scaled", bufs=3)
-                for b in range(4):
-                    k = 4 * h + b
-                    nc.scalar.activation(scaled[:, b, :], fwd[:, b, :], COPY, scale=neg_gy_c_col[:, k : k + 1])
-                back = psum.tile([P, 4, P], F32, name="back", tag="back", bufs=3)
-                for b in range(4):
-                    turn(back[:, b, :], scaled[:, b, :])
-                nc.scalar.copy(own_term[t][:, h * BANK : (h + 1) * BANK], back[:].rearrange("p b c -> p (b c)"))
+                    parts = addend(2 * pair + u, b) + [scaled[:, b, u, :]]
+                    for n, part in enumerate(parts):
+                        turn(back[:, b, :], part, start=(n == 0), stop=(n == len(parts) - 1))
+                nc.scalar.copy(result(2 * pair + u), back[:].rearrange("p b c -> p (b c)"))
+
+        def make_own_term(pair, h):
+            scale_columns(
+                pair,
+                lambda t, b: [picked[:, picked_at(t) + (4 * h + b) * P : picked_at(t) + (4 * h + b + 1) * P]],
+                lambda b: neg_gy_c_col[:, 4 * h + b : 4 * h + b + 1],
+                lambda t, b: [],
+                lambda t: own_term[t][:, h * BANK : (h + 1) * BANK],
+            )
 
         w_codes = keep.tile([P, D], U32, name="w_codes", align_bytes=64)
         w_scales = keep.tile([P, D], U8, name="w_scales", align_bytes=64)
@@ -128,7 +139,7 @@ def tile_attend_gfm_bi_kernel(tc, vT, W, dz, gy, offs, boffs, soffs, out):
                 nc.scalar.copy(grouped[:], raw[:].rearrange("p j w -> p w j"))
                 nc.vector.quantize_mx(out=codes[:].bitcast(fmt), scales=scales[:], in_=grouped[:].rearrange("p w j -> p (w j)"))
             for b in range(X_BLOCKS):
-                acc = psum.tile([P, D], F32, name="acc", tag="acc", bufs=2)
+                acc = psum.tile([P, D], F32, name="acc", tag="bank", bufs=8)
                 nc.tensor.matmul_mx(
                     out=acc[:],
                     lhsT=dz_codes[:, block(b)].bitcast(E5M2X4),
@@ -140,20 +151,14 @@ def tile_attend_gfm_bi_kernel(tc, vT, W, dz, gy, offs, boffs, soffs, out):
                 )
                 nc.scalar.copy(ds_t[:, b, :], acc[:])
 
-        def make_e(t):
-            fwd = psum.tile([P, 4, P], F32, name="fwd", tag="fwd", bufs=3)
-            pairs = by_sample[t][:].rearrange("p (x j) -> p j x", j=2)
-            for b in range(X_BLOCKS):
-                turn(fwd[:, b, :], pairs[:, 0, block(b)], start=True, stop=False)
-                turn(fwd[:, b, :], pairs[:, 1, block(b)], start=False, stop=True)
-            scaled = ring.tile([P, 4, P], F32, name="scaled", tag="scaled", bufs=3)
-            for b in range(X_BLOCKS):
-                nc.scalar.activation(scaled[:, b, :], fwd[:, b, :], COPY, scale=gy_col[:, b : b + 1])
-            back = psum.tile([P, 4, P], F32, name="back", tag="back", bufs=3)
-            for b in range(X_BLOCKS):
-                turn(back[:, b, :], ds_t[:, b, block(t)], start=True, stop=False)
-                turn(back[:, b, :], scaled[:, b, :], start=False, stop=True)
-            nc.scalar.copy(e_all[:, e_at(t) : e_at(t) + X], back[:].rearrange("p b c -> p (b c)"))
+        def make_e(pair):
+            scale_columns(
+                pair,
+                lambda t, b: [by_sample[t][:].rearrange("p (x j) -> p j x", j=2)[:, j, block(b)] for j in range(2)],
+                lambda b: gy_col[:, b : b + 1],
+                lambda t, b: [ds_t[:, b, block(t)]],
+                lambda t: e_all[:, e_at(t) : e_at(t) + X],
+            )
 
         e_c = [keep.tile([P, C], F32, name="e_c%d" % t) for t in range(D_TILES)]
 
@@ -172,16 +177,22 @@ def tile_attend_gfm_bi_kernel(tc, vT, W, dz, gy, offs, boffs, soffs, out):
 
         gather_table(0)
         gather_table(1)
+        placed = [keep.tile([P, T], F32, name="placed%d" % k, tag="table%d" % k) for k in range(2)]
+        for window in placed:
+            nc.gpsimd.memset(window[:], 0.0)
         gather_bags(0)
-        make_own_term(0)
+        gather_bags(1)
         dense_gradient()
         make_e(0)
-        for t in range(1, D_TILES):
-            if t + 1 < D_TILES:
-                gather_table(t + 1)
-            gather_bags(t)
-            make_own_term(t)
-            make_e(t)
+        make_own_term(0, 0)
+        make_own_term(0, 1)
+        gather_table(2)
+        gather_table(3)
+        gather_bags(2)
+        gather_bags(3)
+        make_e(1)
+        make_own_term(1, 0)
+        make_own_term(1, 1)
         gather_e(0)
         for t in range(D_TILES):
             if t + 1 < D_TILES:

@@ -36,26 +36,27 @@ def tile_attend_gfm_bi_kernel(tc, vT, W, dz, gy, offs, boffs, soffs, out):
         idx_list = keep.tile([P, C // 16], U16, name="idx_list")
         slot_list = keep.tile([P, C // 16], U16, name="slot_list")
         gy_win = keep.tile([P, WINDOW], F32, name="gy_win")
-        tables = [keep.tile([P, T], F32, name="table%d" % t, tag="table%d" % t) for t in range(D_TILES)]
+        first_tables = [keep.tile([P, T], F32, name="table%d" % t, tag="table%d" % t) for t in range(2)]
+        last_tables = keep.tile([P, 2, T], F32, name="last_tables")
+        tables = [first_tables[0][:], first_tables[1][:], last_tables[:, 0, :], last_tables[:, 1, :]]
         w_raw = keep.tile([P, PACK, D], F32, name="w_raw")
         dz_raw = keep.tile([P, PACK, X], F32, name="dz_raw")
 
         nc.sync.dma_start(bag_list[:], boffs)
         nc.sync.dma_start(gy_win[:, :X], gy)
         nc.sync.dma_start(idx_list[:], offs)
-        nc.sync.dma_start(tables[0][:], vT[0:P, :])
+        nc.sync.dma_start(tables[0], vT[0:P, :])
+        nc.sync.dma_start(tables[1], vT[P : 2 * P, :])
         nc.sync.dma_start(slot_list[:], soffs)
-        nc.sync.dma_start(tables[1][:], vT[P : 2 * P, :])
         nc.sync.dma_start(w_raw[:], W.rearrange("(p j) d -> p j d", j=PACK))
         nc.sync.dma_start(dz_raw[:], dz.rearrange("(p j) x -> p j x", j=PACK))
-        for t in range(2, D_TILES):
-            nc.sync.dma_start(tables[t][:], vT[t * P : (t + 1) * P, :])
+        nc.sync.dma_start(last_tables[:], vT[2 * P :, :].rearrange("(u p) n -> p u n", p=P))
 
         picked = keep.tile([P, (D_TILES - 1) * C + WINDOW], F32, name="picked")
         e_all = keep.tile([P, (D_TILES - 1) * X + WINDOW], F32, name="e_all")
         identity = keep.tile([P, P], F32, name="identity")
 
-        nc.vector.memset(gy_win[:, X:], 0.0)
+        nc.gpsimd.memset(gy_win[:, X:], 0.0)
         make_identity(nc, identity[:])
         nc.gpsimd.memset(picked[:, D_TILES * C :], 0.0)
         nc.gpsimd.memset(e_all[:, D_TILES * X :], 0.0)
@@ -84,10 +85,10 @@ def tile_attend_gfm_bi_kernel(tc, vT, W, dz, gy, offs, boffs, soffs, out):
             return (D_TILES - 1 - t) * C
 
         def e_at(t):
-            return (D_TILES - 1 - t) * X
+            return ((t + 2) % D_TILES) * X
 
         def gather_table(t):
-            nc.vector.tensor_copy(picked[:, picked_at(t) : picked_at(t) + C], tables[t][:].indirect(idx_list[:]))
+            nc.vector.tensor_copy(picked[:, picked_at(t) : picked_at(t) + C], tables[t].indirect(idx_list[:]))
 
         by_sample = [keep.tile([P, C], F32, name="by_sample%d" % t) for t in range(D_TILES)]
         own_term = [keep.tile([P, C], F32, name="own_term%d" % t) for t in range(D_TILES)]

@@ -23,6 +23,8 @@ D_TILES = D // P
 X_BLOCKS = X // P
 C_BLOCKS = C // P
 WINDOW = 1376
+HALF_WINDOW = 688
+GY_WINDOW = X + 8
 
 
 def tile_attend_gfm_bi_kernel(tc, vT, W, dz, gy, offs, boffs, soffs, out):
@@ -35,8 +37,8 @@ def tile_attend_gfm_bi_kernel(tc, vT, W, dz, gy, offs, boffs, soffs, out):
         bag_list = keep.tile([P, C // 16], U16, name="bag_list")
         idx_list = keep.tile([P, C // 16], U16, name="idx_list")
         slot_list = keep.tile([P, C // 16], U16, name="slot_list")
-        gy_win = keep.tile([P, WINDOW], F32, name="gy_win")
-        first_tables = [keep.tile([P, T], F32, name="table%d" % t, tag="table%d" % t) for t in range(2)]
+        gy_win = keep.tile([P, GY_WINDOW], F32, name="gy_win")
+        first_tables = [keep.tile([P, T], F32, name="table%d" % t) for t in range(2)]
         last_tables = keep.tile([P, 2, T], F32, name="last_tables")
         tables = [first_tables[0][:], first_tables[1][:], last_tables[:, 0, :], last_tables[:, 1, :]]
         w_raw = keep.tile([P, PACK, D], F32, name="w_raw")
@@ -52,14 +54,26 @@ def tile_attend_gfm_bi_kernel(tc, vT, W, dz, gy, offs, boffs, soffs, out):
         nc.sync.dma_start(dz_raw[:], dz.rearrange("(p j) x -> p j x", j=PACK))
         nc.sync.dma_start(last_tables[:], vT[2 * P :, :].rearrange("(u p) n -> p u n", p=P))
 
-        picked = keep.tile([P, (D_TILES - 1) * C + WINDOW], F32, name="picked")
-        e_all = keep.tile([P, (D_TILES - 1) * X + WINDOW], F32, name="e_all")
+        picked = keep.tile([P, D_TILES * C], F32, name="picked")
+        e_all = keep.tile([P, (D_TILES - 1) * X + HALF_WINDOW], F32, name="e_all")
         identity = keep.tile([P, P], F32, name="identity")
 
-        nc.gpsimd.memset(gy_win[:, X:], 0.0)
+        placed = [keep.tile([P, T], F32, name="placed%d" % k) for k in range(2)]
         make_identity(nc, identity[:])
-        nc.gpsimd.memset(picked[:, D_TILES * C :], 0.0)
-        nc.gpsimd.memset(e_all[:, D_TILES * X :], 0.0)
+        nc.vector.memset(gy_win[:, X:], 0.0)
+        nc.vector.memset(e_all[:, D_TILES * X :], 0.0)
+        for window in placed:
+            nc.vector.memset(window[:], 0.0)
+
+        def gather(dst, tile, at, entries, wide, narrow):
+            if at + wide <= tile.shape[1]:
+                nc.vector.tensor_copy(dst[:], tile[:, at : at + wide].indirect(entries[:]))
+            else:
+                for h in range(2):
+                    nc.vector.tensor_copy(
+                        dst[:, h * C // 2 : (h + 1) * C // 2],
+                        tile[:, at : at + narrow].indirect(entries[:, h * C // 32 : (h + 1) * C // 32]),
+                    )
 
         def turn(dst, src, start=True, stop=True):
             nc.tensor.matmul(dst, src, identity[:], start=start, stop=stop, is_transpose=True)
@@ -68,7 +82,7 @@ def tile_attend_gfm_bi_kernel(tc, vT, W, dz, gy, offs, boffs, soffs, out):
             return slice(b * P, (b + 1) * P)
 
         gy_c = keep.tile([P, C], F32, name="gy_c")
-        nc.vector.tensor_copy(gy_c[:], gy_win[:].indirect(bag_list[:]))
+        gather(gy_c, gy_win, 0, bag_list, WINDOW, GY_WINDOW)
         gy_col = keep.tile([P, X_BLOCKS], F32, name="gy_col")
         neg_gy_c_col = keep.tile([P, C_BLOCKS], F32, name="neg_gy_c_col")
         bank = psum.tile([P, X_BLOCKS, P], F32, name="bank", tag="bank", bufs=8)
@@ -94,7 +108,7 @@ def tile_attend_gfm_bi_kernel(tc, vT, W, dz, gy, offs, boffs, soffs, out):
         own_term = [keep.tile([P, C], F32, name="own_term%d" % t) for t in range(D_TILES)]
 
         def gather_bags(t):
-            nc.vector.tensor_copy(by_sample[t][:], picked[:, picked_at(t) : picked_at(t) + WINDOW].indirect(slot_list[:]))
+            gather(by_sample[t], picked, picked_at(t), slot_list, WINDOW, C)
 
         def scale_columns(pair, source, factor, addend, result):
             scaled = ring.tile([P, 4, 2, P], F32, name="scaled", tag="scaled", bufs=3)
@@ -164,7 +178,7 @@ def tile_attend_gfm_bi_kernel(tc, vT, W, dz, gy, offs, boffs, soffs, out):
         e_c = [keep.tile([P, C], F32, name="e_c%d" % t) for t in range(D_TILES)]
 
         def gather_e(t):
-            nc.vector.tensor_copy(e_c[t][:], e_all[:, e_at(t) : e_at(t) + WINDOW].indirect(bag_list[:]))
+            gather(e_c[t], e_all, e_at(t), bag_list, WINDOW, HALF_WINDOW)
 
         def place(t):
             window = placed[t % 2]
@@ -178,9 +192,6 @@ def tile_attend_gfm_bi_kernel(tc, vT, W, dz, gy, offs, boffs, soffs, out):
 
         gather_table(0)
         gather_table(1)
-        placed = [keep.tile([P, T], F32, name="placed%d" % k, tag="table%d" % k) for k in range(2)]
-        for window in placed:
-            nc.gpsimd.memset(window[:], 0.0)
         gather_bags(0)
         gather_bags(1)
         dense_gradient()

@@ -31,7 +31,6 @@ def tile_attend_gfm_bi_kernel(tc, vT, W, dz, gy, offs, boffs, soffs, out):
     nc = tc.nc
     with ExitStack() as ctx:
         keep = ctx.enter_context(tc.tile_pool(name="keep", bufs=1))
-        ring = ctx.enter_context(tc.tile_pool(name="ring", bufs=2))
         psum = ctx.enter_context(tc.psum_pool(name="psum", bufs=1))
 
         bag_list = keep.tile([P, C // 16], U16, name="bag_list")
@@ -42,7 +41,7 @@ def tile_attend_gfm_bi_kernel(tc, vT, W, dz, gy, offs, boffs, soffs, out):
         last_tables = keep.tile([P, 2, T], F32, name="last_tables")
         tables = [first_tables[0][:], first_tables[1][:], last_tables[:, 0, :], last_tables[:, 1, :]]
         w_raw = keep.tile([P, PACK, D], F32, name="w_raw")
-        dz_raw = keep.tile([P, PACK, X], F32, name="dz_raw")
+        dz_raw = keep.tile([P, PACK, X], F32, name="dz_raw", tag="slot_a", align_bytes=64)
 
         nc.sync.dma_start(bag_list[:], boffs)
         nc.sync.dma_start(gy_win[:, :X], gy)
@@ -85,12 +84,12 @@ def tile_attend_gfm_bi_kernel(tc, vT, W, dz, gy, offs, boffs, soffs, out):
         gather(gy_c, gy_win, 0, bag_list, WINDOW, GY_WINDOW)
         gy_col = keep.tile([P, X_BLOCKS], F32, name="gy_col")
         neg_gy_c_col = keep.tile([P, C_BLOCKS], F32, name="neg_gy_c_col")
-        bank = psum.tile([P, X_BLOCKS, P], F32, name="bank", tag="bank", bufs=8)
+        bank = psum.tile([P, X_BLOCKS, P], F32, name="bank", tag="bank0")
         for b in range(X_BLOCKS):
             turn(bank[:, b, :], gy_win[:, block(b)])
         nc.scalar.copy(gy_col[:], bank[:, :, 0])
         for h in range(2):
-            bank = psum.tile([P, 4, P], F32, name="bank", tag="bank", bufs=8)
+            bank = psum.tile([P, 4, P], F32, name="bank", tag="bank%d" % (h + 1))
             for b in range(4):
                 turn(bank[:, b, :], gy_c[:, block(4 * h + b)])
             nc.scalar.activation(neg_gy_c_col[:, 4 * h : 4 * h + 4], bank[:, :, 0], COPY, scale=-1.0)
@@ -99,7 +98,7 @@ def tile_attend_gfm_bi_kernel(tc, vT, W, dz, gy, offs, boffs, soffs, out):
             return (D_TILES - 1 - t) * C
 
         def e_at(t):
-            return ((t + 2) % D_TILES) * X
+            return (D_TILES - 1 - t) * X
 
         def gather_table(t):
             nc.vector.tensor_copy(picked[:, picked_at(t) : picked_at(t) + C], tables[t].indirect(idx_list[:]))
@@ -110,33 +109,32 @@ def tile_attend_gfm_bi_kernel(tc, vT, W, dz, gy, offs, boffs, soffs, out):
         def gather_bags(t):
             gather(by_sample[t], picked, picked_at(t), slot_list, WINDOW, C)
 
-        def scale_columns(pair, source, factor, addend, result):
-            scaled = ring.tile([P, 4, 2, P], F32, name="scaled", tag="scaled", bufs=3)
-            for half in range(2):
-                fwd = psum.tile([P, 2, 2, P], F32, name="fwd", tag="bank", bufs=8)
-                for i in range(2):
-                    for u in range(2):
-                        parts = source(2 * pair + u, 2 * half + i)
-                        for n, part in enumerate(parts):
-                            turn(fwd[:, i, u, :], part, start=(n == 0), stop=(n == len(parts) - 1))
-                for i in range(2):
-                    b = 2 * half + i
-                    nc.scalar.activation(scaled[:, b, :, :], fwd[:, i, :, :], COPY, scale=factor(b))
+        def scale_columns(pair, source, factor, addend, result, slot, fwd_banks, back_banks):
+            scaled = keep.tile([P, 4, 2, P], F32, name="scaled", tag=slot, align_bytes=64)
+            fwd = [psum.tile([P, 2, 2, P], F32, name="fwd", tag="bank%d" % k) for k in fwd_banks]
             for u in range(2):
-                back = psum.tile([P, 4, P], F32, name="back", tag="bank", bufs=8)
+                for b in range(4):
+                    parts = source(2 * pair + u, b)
+                    for n, part in enumerate(parts):
+                        turn(fwd[b // 2][:, b % 2, u, :], part, start=(n == 0), stop=(n == len(parts) - 1))
+            for b in range(4):
+                nc.scalar.activation(scaled[:, b, :, :], fwd[b // 2][:, b % 2, :, :], COPY, scale=factor(b))
+            for u in range(2):
+                back = psum.tile([P, 4, P], F32, name="back", tag="bank%d" % back_banks[u])
                 for b in range(4):
                     parts = addend(2 * pair + u, b) + [scaled[:, b, u, :]]
                     for n, part in enumerate(parts):
                         turn(back[:, b, :], part, start=(n == 0), stop=(n == len(parts) - 1))
                 nc.scalar.copy(result(2 * pair + u), back[:].rearrange("p b c -> p (b c)"))
 
-        def make_own_term(pair, h):
+        def make_own_term(pair, h, *places):
             scale_columns(
                 pair,
                 lambda t, b: [picked[:, picked_at(t) + (4 * h + b) * P : picked_at(t) + (4 * h + b + 1) * P]],
                 lambda b: neg_gy_c_col[:, 4 * h + b : 4 * h + b + 1],
                 lambda t, b: [],
                 lambda t: own_term[t][:, h * BANK : (h + 1) * BANK],
+                *places,
             )
 
         w_codes = keep.tile([P, D], U32, name="w_codes", align_bytes=64)
@@ -148,13 +146,15 @@ def tile_attend_gfm_bi_kernel(tc, vT, W, dz, gy, offs, boffs, soffs, out):
         def dense_gradient():
             for raw, codes, scales, fmt, name in (
                 (w_raw, w_codes, w_scales, E4M3X4, "w_grouped"),
-                (dz_raw, dz_codes, dz_scales, E5M2X4, "dz_grouped"),
+                (dz_raw, dz_codes, dz_scales, E5M2X4, "slot_b"),
             ):
-                grouped = keep.tile([P, BANK, PACK], BF16, name=name, align_bytes=64)
-                nc.scalar.copy(grouped[:], raw[:].rearrange("p j w -> p w j"))
+                grouped = keep.tile([P, BANK, PACK], BF16, name="grouped", tag=name, align_bytes=64)
+                nc.scalar.copy(
+                    grouped[:].rearrange("p (c i) j -> p c j i", i=4), raw[:].rearrange("p j (c i) -> p c j i", i=4)
+                )
                 nc.vector.quantize_mx(out=codes[:].bitcast(fmt), scales=scales[:], in_=grouped[:].rearrange("p w j -> p (w j)"))
             for b in range(X_BLOCKS):
-                acc = psum.tile([P, D], F32, name="acc", tag="bank", bufs=8)
+                acc = psum.tile([P, D], F32, name="acc", tag="bank%d" % (5, 6, 7, 2)[b])
                 nc.tensor.matmul_mx(
                     out=acc[:],
                     lhsT=dz_codes[:, block(b)].bitcast(E5M2X4),
@@ -166,13 +166,14 @@ def tile_attend_gfm_bi_kernel(tc, vT, W, dz, gy, offs, boffs, soffs, out):
                 )
                 nc.scalar.copy(ds_t[:, b, :], acc[:])
 
-        def make_e(pair):
+        def make_e(pair, *places):
             scale_columns(
                 pair,
                 lambda t, b: [by_sample[t][:].rearrange("p (x j) -> p j x", j=2)[:, j, block(b)] for j in range(2)],
                 lambda b: gy_col[:, b : b + 1],
                 lambda t, b: [ds_t[:, b, block(t)]],
                 lambda t: e_all[:, e_at(t) : e_at(t) + X],
+                *places,
             )
 
         e_c = [keep.tile([P, C], F32, name="e_c%d" % t) for t in range(D_TILES)]
@@ -195,18 +196,18 @@ def tile_attend_gfm_bi_kernel(tc, vT, W, dz, gy, offs, boffs, soffs, out):
         gather_bags(0)
         gather_bags(1)
         dense_gradient()
-        make_e(0)
-        make_own_term(0, 0)
-        make_own_term(0, 1)
+        make_e(0, "slot_a", (3, 4), (3, 4))
+        make_own_term(0, 0, "slot_b", (0, 1), (5, 6))
+        make_own_term(0, 1, "slot_a", (7, 2), (0, 1))
         gather_table(2)
         gather_table(3)
         gather_bags(2)
         gather_bags(3)
-        make_e(1)
-        make_own_term(1, 0)
-        make_own_term(1, 1)
-        gather_e(0)
-        for t in range(D_TILES):
-            if t + 1 < D_TILES:
-                gather_e(t + 1)
-            place(t)
+        make_e(1, "slot_b", (0, 1), (3, 4))
+        make_own_term(1, 0, "slot_a", (7, 2), (5, 6))
+        make_own_term(1, 1, "slot_b", (0, 1), (7, 2))
+        for pair in range(2):
+            gather_e(2 * pair)
+            gather_e(2 * pair + 1)
+            place(2 * pair)
+            place(2 * pair + 1)

@@ -19,12 +19,12 @@ ADD = mybir.AluOpType.add
 P = 128
 PACK = 4
 BANK = 512
+STRIPE = 16
 D_TILES = D // P
 X_BLOCKS = X // P
 C_BLOCKS = C // P
 WINDOW = 1376
-HALF_WINDOW = 688
-GY_WINDOW = X + 8
+GY_ROW = P - 1
 
 
 def tile_attend_gfm_bi_kernel(tc, vT, W, dz, gy, offs, boffs, soffs, out):
@@ -33,18 +33,18 @@ def tile_attend_gfm_bi_kernel(tc, vT, W, dz, gy, offs, boffs, soffs, out):
         keep = ctx.enter_context(tc.tile_pool(name="keep", bufs=1))
         psum = ctx.enter_context(tc.psum_pool(name="psum", bufs=1))
 
-        bag_list = keep.tile([P, C // 16], U16, name="bag_list")
-        idx_list = keep.tile([P, C // 16], U16, name="idx_list")
-        slot_list = keep.tile([P, C // 16], U16, name="slot_list")
-        gy_win = keep.tile([P, GY_WINDOW], F32, name="gy_win")
-        first_tables = [keep.tile([P, T], F32, name="table%d" % t) for t in range(2)]
+        bag_list = keep.tile([P, C // STRIPE], U16, name="bag_list")
+        idx_list = keep.tile([P, C // STRIPE], U16, name="idx_list")
+        slot_list = keep.tile([P, C // STRIPE], U16, name="slot_list")
+        gy_win = keep.tile([P, X], F32, name="gy_win")
+        first_tables = [keep.tile([P, T], F32, name="table", tag="table%d" % t) for t in range(2)]
         last_tables = keep.tile([P, 2, T], F32, name="last_tables")
         tables = [first_tables[0][:], first_tables[1][:], last_tables[:, 0, :], last_tables[:, 1, :]]
         w_raw = keep.tile([P, PACK, D], F32, name="w_raw")
-        dz_raw = keep.tile([P, PACK, X], F32, name="dz_raw", tag="slot_a", align_bytes=64)
+        dz_raw = keep.tile([P, PACK, X], F32, name="dz_raw", tag="room_a", align_bytes=64)
 
+        nc.scalar.dma_start(gy_win[GY_ROW:, :], gy[0:1, :])
         nc.sync.dma_start(bag_list[:], boffs)
-        nc.sync.dma_start(gy_win[:, :X], gy)
         nc.sync.dma_start(idx_list[:], offs)
         nc.sync.dma_start(tables[0], vT[0:P, :])
         nc.sync.dma_start(tables[1], vT[P : 2 * P, :])
@@ -54,45 +54,46 @@ def tile_attend_gfm_bi_kernel(tc, vT, W, dz, gy, offs, boffs, soffs, out):
         nc.sync.dma_start(last_tables[:], vT[2 * P :, :].rearrange("(u p) n -> p u n", p=P))
 
         picked = keep.tile([P, D_TILES * C], F32, name="picked")
-        e_all = keep.tile([P, (D_TILES - 1) * X + HALF_WINDOW], F32, name="e_all")
+        e_all = keep.tile([P, D_TILES * X], F32, name="e_all")
         identity = keep.tile([P, P], F32, name="identity")
+        placed_even = keep.tile([P, T], F32, name="placed_even")
 
-        placed = [keep.tile([P, T], F32, name="placed%d" % k) for k in range(2)]
         make_identity(nc, identity[:])
-        nc.vector.memset(gy_win[:, X:], 0.0)
-        nc.vector.memset(e_all[:, D_TILES * X :], 0.0)
-        for window in placed:
-            nc.vector.memset(window[:], 0.0)
+        nc.vector.memset(gy_win[:GY_ROW, :], 0.0)
+        nc.vector.memset(placed_even[:], 0.0)
 
-        def gather(dst, tile, at, entries, wide, narrow):
-            if at + wide <= tile.shape[1]:
-                nc.vector.tensor_copy(dst[:], tile[:, at : at + wide].indirect(entries[:]))
-            else:
-                for h in range(2):
-                    nc.vector.tensor_copy(
-                        dst[:, h * C // 2 : (h + 1) * C // 2],
-                        tile[:, at : at + narrow].indirect(entries[:, h * C // 32 : (h + 1) * C // 32]),
-                    )
+        def gather(dst, tile, at, entries):
+            room = min(tile.shape[1] - at, WINDOW)
+            piece = min(C, (3 * room // 4) // (2 * STRIPE) * (2 * STRIPE))
+            pieces = -(-C // piece)
+            piece = -(-C // (pieces * 2 * STRIPE)) * 2 * STRIPE
+            for lo in range(0, C, piece):
+                hi = min(C, lo + piece)
+                nc.vector.tensor_copy(dst[:, lo:hi], tile[:, at : at + room].indirect(entries[:, lo // STRIPE : hi // STRIPE]))
 
-        def turn(dst, src, start=True, stop=True):
-            nc.tensor.matmul(dst, src, identity[:], start=start, stop=stop, is_transpose=True)
+        def turn(dst, parts):
+            for n, part in enumerate(parts):
+                nc.tensor.matmul(dst, part, identity[:], start=(n == 0), stop=(n == len(parts) - 1), is_transpose=True)
 
         def block(b):
             return slice(b * P, (b + 1) * P)
 
+        def bank_tile(k, shape):
+            return psum.tile(shape, F32, name="bank", tag="bank%d" % k)
+
         gy_c = keep.tile([P, C], F32, name="gy_c")
-        gather(gy_c, gy_win, 0, bag_list, WINDOW, GY_WINDOW)
+        gather(gy_c, gy_win, 0, bag_list)
         gy_col = keep.tile([P, X_BLOCKS], F32, name="gy_col")
         neg_gy_c_col = keep.tile([P, C_BLOCKS], F32, name="neg_gy_c_col")
-        bank = psum.tile([P, X_BLOCKS, P], F32, name="bank", tag="bank0")
+        bank = bank_tile(4, [P, X_BLOCKS, P])
         for b in range(X_BLOCKS):
-            turn(bank[:, b, :], gy_win[:, block(b)])
-        nc.scalar.copy(gy_col[:], bank[:, :, 0])
+            turn(bank[:, b, :], [gy_win[:, block(b)]])
+        nc.scalar.copy(gy_col[:], bank[:, :, GY_ROW])
         for h in range(2):
-            bank = psum.tile([P, 4, P], F32, name="bank", tag="bank%d" % (h + 1))
+            bank = bank_tile(5 + h, [P, 4, P])
             for b in range(4):
-                turn(bank[:, b, :], gy_c[:, block(4 * h + b)])
-            nc.scalar.activation(neg_gy_c_col[:, 4 * h : 4 * h + 4], bank[:, :, 0], COPY, scale=-1.0)
+                turn(bank[:, b, :], [gy_c[:, block(4 * h + b)]])
+            nc.scalar.activation(neg_gy_c_col[:, 4 * h : 4 * h + 4], bank[:, :, GY_ROW], COPY, scale=-1.0)
 
         def picked_at(t):
             return (D_TILES - 1 - t) * C
@@ -107,34 +108,49 @@ def tile_attend_gfm_bi_kernel(tc, vT, W, dz, gy, offs, boffs, soffs, out):
         own_term = [keep.tile([P, C], F32, name="own_term%d" % t) for t in range(D_TILES)]
 
         def gather_bags(t):
-            gather(by_sample[t], picked, picked_at(t), slot_list, WINDOW, C)
+            gather(by_sample[t], picked, picked_at(t), slot_list)
 
-        def scale_columns(pair, source, factor, addend, result, slot, fwd_banks, back_banks):
-            scaled = keep.tile([P, 4, 2, P], F32, name="scaled", tag=slot, align_bytes=64)
-            fwd = [psum.tile([P, 2, 2, P], F32, name="fwd", tag="bank%d" % k) for k in fwd_banks]
+        def turn_and_scale(pair, blocks, source, factors, room, banks):
+            scaled = keep.tile([P, blocks, 2, P], F32, name="scaled", tag=room, align_bytes=64)
+            turned = [bank_tile(k, [P, 2, 2, P]) for k in banks]
             for u in range(2):
-                for b in range(4):
-                    parts = source(2 * pair + u, b)
-                    for n, part in enumerate(parts):
-                        turn(fwd[b // 2][:, b % 2, u, :], part, start=(n == 0), stop=(n == len(parts) - 1))
-            for b in range(4):
-                nc.scalar.activation(scaled[:, b, :, :], fwd[b // 2][:, b % 2, :, :], COPY, scale=factor(b))
+                for b in range(blocks):
+                    turn(turned[b // 2][:, b % 2, u, :], source(2 * pair + u, b))
+            for b in range(blocks):
+                nc.scalar.activation(scaled[:, b, :, :], turned[b // 2][:, b % 2, :, :], COPY, scale=factors[:, b : b + 1])
+            return scaled
+
+        def turn_back(pair, parts, result, banks):
             for u in range(2):
-                back = psum.tile([P, 4, P], F32, name="back", tag="bank%d" % back_banks[u])
+                back = bank_tile(banks[u], [P, 4, P])
                 for b in range(4):
-                    parts = addend(2 * pair + u, b) + [scaled[:, b, u, :]]
-                    for n, part in enumerate(parts):
-                        turn(back[:, b, :], part, start=(n == 0), stop=(n == len(parts) - 1))
+                    turn(back[:, b, :], parts(u, b))
                 nc.scalar.copy(result(2 * pair + u), back[:].rearrange("p b c -> p (b c)"))
 
-        def make_own_term(pair, h, *places):
-            scale_columns(
+        def scale_own(pair, banks):
+            return turn_and_scale(
+                pair, C_BLOCKS, lambda t, b: [picked[:, picked_at(t) + b * P : picked_at(t) + (b + 1) * P]], neg_gy_c_col, "room_a", banks
+            )
+
+        def scale_sums(pair, banks):
+            return turn_and_scale(
                 pair,
-                lambda t, b: [picked[:, picked_at(t) + (4 * h + b) * P : picked_at(t) + (4 * h + b + 1) * P]],
-                lambda b: neg_gy_c_col[:, 4 * h + b : 4 * h + b + 1],
-                lambda t, b: [],
-                lambda t: own_term[t][:, h * BANK : (h + 1) * BANK],
-                *places,
+                X_BLOCKS,
+                lambda t, b: [by_sample[t][:].rearrange("p (x j) -> p j x", j=2)[:, j, block(b)] for j in range(2)],
+                gy_col,
+                "room_b",
+                banks,
+            )
+
+        def finish_own(pair, h, scaled, banks):
+            turn_back(pair, lambda u, b: [scaled[:, 4 * h + b, u, :]], lambda t: own_term[t][:, h * BANK : (h + 1) * BANK], banks)
+
+        def finish_e(pair, scaled, banks):
+            turn_back(
+                pair,
+                lambda u, b: [ds_t[:, b, block(2 * pair + u)], scaled[:, b, u, :]],
+                lambda t: e_all[:, e_at(t) : e_at(t) + X],
+                banks,
             )
 
         w_codes = keep.tile([P, D], U32, name="w_codes", align_bytes=64)
@@ -143,18 +159,20 @@ def tile_attend_gfm_bi_kernel(tc, vT, W, dz, gy, offs, boffs, soffs, out):
         dz_scales = keep.tile([P, X], U8, name="dz_scales", align_bytes=64)
         ds_t = keep.tile([P, X_BLOCKS, D], F32, name="ds_t")
 
-        def dense_gradient():
-            for raw, codes, scales, fmt, name in (
+        def quantise():
+            for raw, codes, scales, fmt, room in (
                 (w_raw, w_codes, w_scales, E4M3X4, "w_grouped"),
-                (dz_raw, dz_codes, dz_scales, E5M2X4, "slot_b"),
+                (dz_raw, dz_codes, dz_scales, E5M2X4, "room_b"),
             ):
-                grouped = keep.tile([P, BANK, PACK], BF16, name="grouped", tag=name, align_bytes=64)
+                grouped = keep.tile([P, BANK, PACK], BF16, name="grouped", tag=room, align_bytes=64)
                 nc.scalar.copy(
                     grouped[:].rearrange("p (c i) j -> p c j i", i=4), raw[:].rearrange("p j (c i) -> p c j i", i=4)
                 )
                 nc.vector.quantize_mx(out=codes[:].bitcast(fmt), scales=scales[:], in_=grouped[:].rearrange("p w j -> p (w j)"))
+
+        def dense_gradient(banks):
             for b in range(X_BLOCKS):
-                acc = psum.tile([P, D], F32, name="acc", tag="bank%d" % (5, 6, 7, 2)[b])
+                acc = bank_tile(banks[b], [P, D])
                 nc.tensor.matmul_mx(
                     out=acc[:],
                     lhsT=dz_codes[:, block(b)].bitcast(E5M2X4),
@@ -166,20 +184,11 @@ def tile_attend_gfm_bi_kernel(tc, vT, W, dz, gy, offs, boffs, soffs, out):
                 )
                 nc.scalar.copy(ds_t[:, b, :], acc[:])
 
-        def make_e(pair, *places):
-            scale_columns(
-                pair,
-                lambda t, b: [by_sample[t][:].rearrange("p (x j) -> p j x", j=2)[:, j, block(b)] for j in range(2)],
-                lambda b: gy_col[:, b : b + 1],
-                lambda t, b: [ds_t[:, b, block(t)]],
-                lambda t: e_all[:, e_at(t) : e_at(t) + X],
-                *places,
-            )
-
-        e_c = [keep.tile([P, C], F32, name="e_c%d" % t) for t in range(D_TILES)]
+        e_c = {}
 
         def gather_e(t):
-            gather(e_c[t], e_all, e_at(t), bag_list, WINDOW, HALF_WINDOW)
+            e_c[t] = keep.tile([P, C], F32, name="e_c", tag="e_c%d" % (t % 2))
+            gather(e_c[t], e_all, e_at(t), bag_list)
 
         def place(t):
             window = placed[t % 2]
@@ -193,19 +202,27 @@ def tile_attend_gfm_bi_kernel(tc, vT, W, dz, gy, offs, boffs, soffs, out):
 
         gather_table(0)
         gather_table(1)
+        placed_odd = keep.tile([P, T], F32, name="placed_odd", tag="table0")
+        nc.gpsimd.memset(placed_odd[:], 0.0)
+        placed = [placed_even, placed_odd]
         gather_bags(0)
         gather_bags(1)
-        dense_gradient()
-        make_e(0, "slot_a", (3, 4), (3, 4))
-        make_own_term(0, 0, "slot_b", (0, 1), (5, 6))
-        make_own_term(0, 1, "slot_a", (7, 2), (0, 1))
+        quantise()
+        own_scaled = scale_own(0, (0, 1, 2, 3))
+        sums_scaled = scale_sums(0, (4, 5))
+        dense_gradient((6, 7, 0, 1))
+        finish_own(0, 0, own_scaled, (2, 3))
+        finish_e(0, sums_scaled, (4, 5))
+        finish_own(0, 1, own_scaled, (0, 1))
         gather_table(2)
         gather_table(3)
         gather_bags(2)
         gather_bags(3)
-        make_e(1, "slot_b", (0, 1), (3, 4))
-        make_own_term(1, 0, "slot_a", (7, 2), (5, 6))
-        make_own_term(1, 1, "slot_b", (0, 1), (7, 2))
+        own_scaled = scale_own(1, (2, 3, 4, 5))
+        sums_scaled = scale_sums(1, (0, 1))
+        finish_own(1, 0, own_scaled, (6, 7))
+        finish_e(1, sums_scaled, (2, 3))
+        finish_own(1, 1, own_scaled, (4, 5))
         for pair in range(2):
             gather_e(2 * pair)
             gather_e(2 * pair + 1)

@@ -56,11 +56,9 @@ def tile_attend_gfm_bi_kernel(tc, vT, W, dz, gy, offs, boffs, soffs, out):
         picked = keep.tile([P, D_TILES * C], F32, name="picked")
         e_all = keep.tile([P, D_TILES * X], F32, name="e_all")
         identity = keep.tile([P, P], F32, name="identity")
-        placed_even = keep.tile([P, T], F32, name="placed_even")
 
         make_identity(nc, identity[:])
         nc.vector.memset(gy_win[:GY_ROW, :], 0.0)
-        nc.vector.memset(placed_even[:], 0.0)
 
         def gather(dst, tile, at, entries):
             room = min(tile.shape[1] - at, WINDOW)
@@ -202,9 +200,9 @@ def tile_attend_gfm_bi_kernel(tc, vT, W, dz, gy, offs, boffs, soffs, out):
 
         gather_table(0)
         gather_table(1)
-        placed_odd = keep.tile([P, T], F32, name="placed_odd", tag="table0")
-        nc.gpsimd.memset(placed_odd[:], 0.0)
-        placed = [placed_even, placed_odd]
+        placed = [keep.tile([P, T], F32, name="placed", tag="table%d" % k) for k in range(2)]
+        for window in placed:
+            nc.gpsimd.memset(window[:], 0.0)
         gather_bags(0)
         gather_bags(1)
         quantise()

@@ -15,6 +15,7 @@ E4M3X4 = mybir.dt.float8_e4m3fn_x4
 E5M2X4 = mybir.dt.float8_e5m2_x4
 COPY = mybir.ActivationFunctionType.Copy
 ADD = mybir.AluOpType.add
+MULT = mybir.AluOpType.mult
 
 P = 128
 PACK = 4
@@ -41,7 +42,7 @@ def tile_attend_gfm_bi_kernel(tc, vT, W, dz, gy, offs, boffs, soffs, out):
         last_tables = keep.tile([P, 2, T], F32, name="last_tables")
         tables = [first_tables[0][:], first_tables[1][:], last_tables[:, 0, :], last_tables[:, 1, :]]
         w_raw = keep.tile([P, PACK, D], F32, name="w_raw")
-        dz_raw = keep.tile([P, PACK, X], F32, name="dz_raw", tag="room_a", align_bytes=64)
+        dz_raw = keep.tile([P, PACK, X], F32, name="dz_raw", tag="room_a")
 
         nc.scalar.dma_start(gy_win[GY_ROW:, :], gy[0:1, :])
         nc.sync.dma_start(bag_list[:], boffs)
@@ -103,7 +104,9 @@ def tile_attend_gfm_bi_kernel(tc, vT, W, dz, gy, offs, boffs, soffs, out):
             nc.vector.tensor_copy(picked[:, picked_at(t) : picked_at(t) + C], tables[t].indirect(idx_list[:]))
 
         by_sample = [keep.tile([P, C], F32, name="by_sample%d" % t) for t in range(D_TILES)]
-        own_term = [keep.tile([P, C], F32, name="own_term%d" % t) for t in range(D_TILES)]
+
+        def make_own(t):
+            nc.gpsimd.tensor_tensor(own_term[:, t * C : (t + 1) * C], picked[:, picked_at(t) : picked_at(t) + C], neg_gy_c[:], MULT)
 
         def gather_bags(t):
             gather(by_sample[t], picked, picked_at(t), slot_list)
@@ -125,11 +128,6 @@ def tile_attend_gfm_bi_kernel(tc, vT, W, dz, gy, offs, boffs, soffs, out):
                     turn(back[:, b, :], parts(u, b))
                 nc.scalar.copy(result(2 * pair + u), back[:].rearrange("p b c -> p (b c)"))
 
-        def scale_own(pair, banks):
-            return turn_and_scale(
-                pair, C_BLOCKS, lambda t, b: [picked[:, picked_at(t) + b * P : picked_at(t) + (b + 1) * P]], neg_gy_c_col, "room_a", banks
-            )
-
         def scale_sums(pair, banks):
             return turn_and_scale(
                 pair,
@@ -139,9 +137,6 @@ def tile_attend_gfm_bi_kernel(tc, vT, W, dz, gy, offs, boffs, soffs, out):
                 "room_b",
                 banks,
             )
-
-        def finish_own(pair, h, scaled, banks):
-            turn_back(pair, lambda u, b: [scaled[:, 4 * h + b, u, :]], lambda t: own_term[t][:, h * BANK : (h + 1) * BANK], banks)
 
         def finish_e(pair, scaled, banks):
             turn_back(
@@ -153,7 +148,7 @@ def tile_attend_gfm_bi_kernel(tc, vT, W, dz, gy, offs, boffs, soffs, out):
 
         w_codes = keep.tile([P, D], U32, name="w_codes", align_bytes=64)
         w_scales = keep.tile([P, D], U8, name="w_scales", align_bytes=64)
-        dz_codes = keep.tile([P, X], U32, name="dz_codes", align_bytes=64)
+        dz_codes = keep.tile([P, X], U32, name="dz_codes", tag="room_c", align_bytes=64)
         dz_scales = keep.tile([P, X], U8, name="dz_scales", align_bytes=64)
         ds_t = keep.tile([P, X_BLOCKS, D], F32, name="ds_t")
 
@@ -185,12 +180,12 @@ def tile_attend_gfm_bi_kernel(tc, vT, W, dz, gy, offs, boffs, soffs, out):
         e_c = {}
 
         def gather_e(t):
-            e_c[t] = keep.tile([P, C], F32, name="e_c", tag="e_c%d" % (t % 2))
+            e_c[t] = keep.tile([P, C], F32, name="e_c%d" % t)
             gather(e_c[t], e_all, e_at(t), bag_list)
 
         def place(t):
             window = placed[t % 2]
-            nc.vector.tensor_tensor(window[:].indirect(idx_list[:]), e_c[t][:], own_term[t][:], ADD)
+            nc.vector.tensor_tensor(window[:].indirect(idx_list[:]), e_c[t][:], own_term[:, t * C : (t + 1) * C], ADD)
             rows = out[t * P : (t + 1) * P, :]
             if t + 1 < D_TILES:
                 nc.sync.dma_start(rows, window[:])
@@ -206,21 +201,26 @@ def tile_attend_gfm_bi_kernel(tc, vT, W, dz, gy, offs, boffs, soffs, out):
         gather_bags(0)
         gather_bags(1)
         quantise()
-        own_scaled = scale_own(0, (0, 1, 2, 3))
+        neg_gy_c = keep.tile([P, C], F32, name="neg_gy_c", tag="room_a")
+        for h in range(2):
+            bank = bank_tile(h, [P, 4, P])
+            for b in range(4):
+                turn(bank[:, b, :], [neg_gy_c_col[:, 4 * h + b : 4 * h + b + 1].to_broadcast([P, P])])
+            nc.scalar.copy(neg_gy_c[:, h * BANK : (h + 1) * BANK], bank[:].rearrange("p b c -> p (b c)"))
         sums_scaled = scale_sums(0, (4, 5))
         dense_gradient((6, 7, 0, 1))
-        finish_own(0, 0, own_scaled, (2, 3))
-        finish_e(0, sums_scaled, (4, 5))
-        finish_own(0, 1, own_scaled, (0, 1))
+        finish_e(0, sums_scaled, (2, 3))
+        own_term = keep.tile([P, D_TILES * C], F32, name="own_term", tag="room_c", align_bytes=64)
+        make_own(0)
+        make_own(1)
         gather_table(2)
         gather_table(3)
+        make_own(2)
+        make_own(3)
         gather_bags(2)
         gather_bags(3)
-        own_scaled = scale_own(1, (2, 3, 4, 5))
-        sums_scaled = scale_sums(1, (0, 1))
-        finish_own(1, 0, own_scaled, (6, 7))
-        finish_e(1, sums_scaled, (2, 3))
-        finish_own(1, 1, own_scaled, (4, 5))
+        sums_scaled = scale_sums(1, (4, 5))
+        finish_e(1, sums_scaled, (6, 7))
         for pair in range(2):
             gather_e(2 * pair)
             gather_e(2 * pair + 1)

@@ -26,6 +26,8 @@ X_BLOCKS = X // P
 C_BLOCKS = C // P
 WINDOW = 1376
 GY_ROW = P - 1
+SCALAR_COLS = 320
+JOINT_COLS = 3 * T // 4
 
 
 def tile_attend_gfm_bi_kernel(tc, vT, W, dz, gy, offs, boffs, soffs, out):
@@ -52,14 +54,23 @@ def tile_attend_gfm_bi_kernel(tc, vT, W, dz, gy, offs, boffs, soffs, out):
         nc.sync.dma_start(slot_list[:], soffs)
         nc.sync.dma_start(w_raw[:], W.rearrange("(p j) d -> p j d", j=PACK))
         nc.sync.dma_start(dz_raw[:], dz.rearrange("(p j) x -> p j x", j=PACK))
-        nc.sync.dma_start(last_tables[:], vT[2 * P :, :].rearrange("(u p) n -> p u n", p=P))
+        last_rows = vT[2 * P :, :].rearrange("(u p) n -> p u n", p=P)
+        nc.sync.dma_start(last_tables[:, :, :JOINT_COLS], last_rows[:, :, :JOINT_COLS])
+        for u in range(2):
+            nc.sync.dma_start(last_tables[:, u, JOINT_COLS:], last_rows[:, u, JOINT_COLS:])
 
-        picked = keep.tile([P, D_TILES * C], F32, name="picked")
-        e_all = keep.tile([P, D_TILES * X], F32, name="e_all")
+        picked = keep.tile([P, (D_TILES - 1) * C + WINDOW], F32, name="picked")
+        e_all = keep.tile([P, (D_TILES - 1) * X + WINDOW], F32, name="e_all")
         identity = keep.tile([P, P], F32, name="identity")
 
+        placed = [keep.tile([P, T], F32, name="placed%d" % k) for k in range(2)]
+
+        nc.gpsimd.memset(gy_win[:GY_ROW, :], 0.0)
         make_identity(nc, identity[:])
-        nc.vector.memset(gy_win[:GY_ROW, :], 0.0)
+        nc.gpsimd.memset(picked[:, D_TILES * C :], 0.0)
+        nc.gpsimd.memset(e_all[:, D_TILES * X :], 0.0)
+        for window in placed:
+            nc.gpsimd.memset(window[:], 0.0)
 
         def gather(dst, tile, at, entries):
             room = min(tile.shape[1] - at, WINDOW)
@@ -152,16 +163,18 @@ def tile_attend_gfm_bi_kernel(tc, vT, W, dz, gy, offs, boffs, soffs, out):
         dz_scales = keep.tile([P, X], U8, name="dz_scales", align_bytes=64)
         ds_t = keep.tile([P, X_BLOCKS, D], F32, name="ds_t")
 
-        def quantise():
-            for raw, codes, scales, fmt, room in (
-                (w_raw, w_codes, w_scales, E4M3X4, "w_grouped"),
-                (dz_raw, dz_codes, dz_scales, E5M2X4, "room_b"),
-            ):
-                grouped = keep.tile([P, BANK, PACK], BF16, name="grouped", tag=room, align_bytes=64)
-                nc.scalar.copy(
-                    grouped[:].rearrange("p (c i) j -> p c j i", i=4), raw[:].rearrange("p j (c i) -> p c j i", i=4)
+        def quantise(raw, codes, scales, fmt, room):
+            grouped = keep.tile([P, BANK, PACK], BF16, name="grouped", tag=room, align_bytes=64)
+
+            def interleaved(cols):
+                return (
+                    grouped[:, cols, :].rearrange("p (c i) j -> p c j i", i=4),
+                    raw[:, :, cols].rearrange("p j (c i) -> p c j i", i=4),
                 )
-                nc.vector.quantize_mx(out=codes[:].bitcast(fmt), scales=scales[:], in_=grouped[:].rearrange("p w j -> p (w j)"))
+
+            nc.scalar.copy(*interleaved(slice(0, SCALAR_COLS)))
+            nc.gpsimd.tensor_scalar(*interleaved(slice(SCALAR_COLS, BANK)), 1.0, 0.0, MULT, ADD)
+            nc.vector.quantize_mx(out=codes[:].bitcast(fmt), scales=scales[:], in_=grouped[:].rearrange("p w j -> p (w j)"))
 
         def dense_gradient(banks):
             for b in range(X_BLOCKS):
@@ -195,12 +208,10 @@ def tile_attend_gfm_bi_kernel(tc, vT, W, dz, gy, offs, boffs, soffs, out):
 
         gather_table(0)
         gather_table(1)
-        placed = [keep.tile([P, T], F32, name="placed", tag="table%d" % k) for k in range(2)]
-        for window in placed:
-            nc.gpsimd.memset(window[:], 0.0)
         gather_bags(0)
         gather_bags(1)
-        quantise()
+        quantise(w_raw, w_codes, w_scales, E4M3X4, "w_grouped")
+        quantise(dz_raw, dz_codes, dz_scales, E5M2X4, "room_b")
         neg_gy_c = keep.tile([P, C], F32, name="neg_gy_c", tag="room_a")
         for h in range(2):
             bank = bank_tile(h, [P, 4, P])

@@ -27,6 +27,7 @@ C_BLOCKS = C // P
 WINDOW = 1376
 GY_ROW = P - 1
 SCALAR_COLS = 320
+LATE_DS_BYTES = 4 * X_BLOCKS * 2 * P
 JOINT_COLS = 3 * T // 4
 
 
@@ -34,6 +35,7 @@ def tile_attend_gfm_bi_kernel(tc, vT, W, dz, gy, offs, boffs, soffs, out):
     nc = tc.nc
     with ExitStack() as ctx:
         keep = ctx.enter_context(tc.tile_pool(name="keep", bufs=1))
+        shared = ctx.enter_context(tc.tile_pool(name="shared", bufs=1))
         psum = ctx.enter_context(tc.psum_pool(name="psum", bufs=1))
 
         bag_list = keep.tile([P, C // STRIPE], U16, name="bag_list")
@@ -60,17 +62,20 @@ def tile_attend_gfm_bi_kernel(tc, vT, W, dz, gy, offs, boffs, soffs, out):
             nc.sync.dma_start(last_tables[:, u, JOINT_COLS:], last_rows[:, u, JOINT_COLS:])
 
         picked = keep.tile([P, (D_TILES - 1) * C + WINDOW], F32, name="picked")
-        e_all = keep.tile([P, (D_TILES - 1) * X + WINDOW], F32, name="e_all")
+        e_pairs = [
+            shared.tile([P, X + WINDOW], F32, name="e_early", offset=LATE_DS_BYTES - 32),
+            keep.tile([P, X + WINDOW], F32, name="e_late"),
+        ]
         identity = keep.tile([P, P], F32, name="identity")
 
-        placed = [keep.tile([P, T], F32, name="placed%d" % k) for k in range(2)]
+        placed_even = keep.tile([P, T], F32, name="placed_even")
 
         nc.gpsimd.memset(gy_win[:GY_ROW, :], 0.0)
         make_identity(nc, identity[:])
         nc.gpsimd.memset(picked[:, D_TILES * C :], 0.0)
-        nc.gpsimd.memset(e_all[:, D_TILES * X :], 0.0)
-        for window in placed:
-            nc.gpsimd.memset(window[:], 0.0)
+        for e_pair in e_pairs:
+            nc.gpsimd.memset(e_pair[:, 2 * X :], 0.0)
+        nc.gpsimd.memset(placed_even[:], 0.0)
 
         def gather(dst, tile, at, entries):
             room = min(tile.shape[1] - at, WINDOW)
@@ -109,7 +114,7 @@ def tile_attend_gfm_bi_kernel(tc, vT, W, dz, gy, offs, boffs, soffs, out):
             return (D_TILES - 1 - t) * C
 
         def e_at(t):
-            return (D_TILES - 1 - t) * X
+            return (t % 2) * X
 
         def gather_table(t):
             nc.vector.tensor_copy(picked[:, picked_at(t) : picked_at(t) + C], tables[t].indirect(idx_list[:]))
@@ -149,11 +154,11 @@ def tile_attend_gfm_bi_kernel(tc, vT, W, dz, gy, offs, boffs, soffs, out):
                 banks,
             )
 
-        def finish_e(pair, scaled, banks):
+        def finish_e(pair, ds_pair, scaled, banks):
             turn_back(
                 pair,
-                lambda u, b: [ds_t[:, b, block(2 * pair + u)], scaled[:, b, u, :]],
-                lambda t: e_all[:, e_at(t) : e_at(t) + X],
+                lambda u, b: [ds_pair[:, b, block(u)], scaled[:, b, u, :]],
+                lambda t: e_pairs[pair][:, e_at(t) : e_at(t) + X],
                 banks,
             )
 
@@ -161,7 +166,6 @@ def tile_attend_gfm_bi_kernel(tc, vT, W, dz, gy, offs, boffs, soffs, out):
         w_scales = keep.tile([P, D], U8, name="w_scales", align_bytes=64)
         dz_codes = keep.tile([P, X], U32, name="dz_codes", tag="room_c", align_bytes=64)
         dz_scales = keep.tile([P, X], U8, name="dz_scales", align_bytes=64)
-        ds_t = keep.tile([P, X_BLOCKS, D], F32, name="ds_t")
 
         def quantise(raw, codes, scales, fmt, room):
             grouped = keep.tile([P, BANK, PACK], BF16, name="grouped", tag=room, align_bytes=64)
@@ -177,8 +181,8 @@ def tile_attend_gfm_bi_kernel(tc, vT, W, dz, gy, offs, boffs, soffs, out):
             nc.vector.quantize_mx(out=codes[:].bitcast(fmt), scales=scales[:], in_=grouped[:].rearrange("p w j -> p (w j)"))
 
         def dense_gradient(banks):
-            for b in range(X_BLOCKS):
-                acc = bank_tile(banks[b], [P, D])
+            sums = [bank_tile(k, [P, D]) for k in banks]
+            for b, acc in enumerate(sums):
                 nc.tensor.matmul_mx(
                     out=acc[:],
                     lhsT=dz_codes[:, block(b)].bitcast(E5M2X4),
@@ -188,13 +192,18 @@ def tile_attend_gfm_bi_kernel(tc, vT, W, dz, gy, offs, boffs, soffs, out):
                     start=True,
                     stop=True,
                 )
-                nc.scalar.copy(ds_t[:, b, :], acc[:])
+            return sums
+
+        def copy_dense_gradient(pair, sums, ds_pair):
+            for b, acc in enumerate(sums):
+                nc.scalar.copy(ds_pair[:, b, :], acc[:, 2 * pair * P : 2 * (pair + 1) * P])
+            return ds_pair
 
         e_c = {}
 
         def gather_e(t):
             e_c[t] = keep.tile([P, C], F32, name="e_c%d" % t)
-            gather(e_c[t], e_all, e_at(t), bag_list)
+            gather(e_c[t], e_pairs[t // 2], e_at(t), bag_list)
 
         def place(t):
             window = placed[t % 2]
@@ -219,8 +228,9 @@ def tile_attend_gfm_bi_kernel(tc, vT, W, dz, gy, offs, boffs, soffs, out):
                 turn(bank[:, b, :], [neg_gy_c_col[:, 4 * h + b : 4 * h + b + 1].to_broadcast([P, P])])
             nc.scalar.copy(neg_gy_c[:, h * BANK : (h + 1) * BANK], bank[:].rearrange("p b c -> p (b c)"))
         sums_scaled = scale_sums(0, (4, 5))
-        dense_gradient((6, 7, 0, 1))
-        finish_e(0, sums_scaled, (2, 3))
+        ds_sums = dense_gradient((6, 7, 2, 3))
+        ds_early = copy_dense_gradient(0, ds_sums, keep.tile([P, X_BLOCKS, 2 * P], F32, name="ds_early"))
+        finish_e(0, ds_early, sums_scaled, (0, 1))
         own_term = keep.tile([P, D_TILES * C], F32, name="own_term", tag="room_c", align_bytes=64)
         make_own(0)
         make_own(1)
@@ -230,10 +240,17 @@ def tile_attend_gfm_bi_kernel(tc, vT, W, dz, gy, offs, boffs, soffs, out):
         make_own(3)
         gather_bags(2)
         gather_bags(3)
-        sums_scaled = scale_sums(1, (4, 5))
-        finish_e(1, sums_scaled, (6, 7))
-        for pair in range(2):
-            gather_e(2 * pair)
-            gather_e(2 * pair + 1)
-            place(2 * pair)
-            place(2 * pair + 1)
+        gather_e(0)
+        gather_e(1)
+        placed_odd = shared.tile([P, T], F32, name="placed_odd", offset=LATE_DS_BYTES)
+        nc.gpsimd.memset(placed_odd[:], 0.0)
+        placed = [placed_even, placed_odd]
+        ds_late = copy_dense_gradient(1, ds_sums, shared.tile([P, X_BLOCKS, 2 * P], F32, name="ds_late", offset=0))
+        sums_scaled = scale_sums(1, (6, 7))
+        finish_e(1, ds_late, sums_scaled, (2, 3))
+        place(0)
+        place(1)
+        gather_e(2)
+        gather_e(3)
+        place(2)
+        place(3)

@@ -208,12 +208,7 @@ def tile_attend_gfm_bi_kernel(tc, vT, W, dz, gy, offs, boffs, soffs, out):
         def place(t):
             window = placed[t % 2]
             nc.vector.tensor_tensor(window[:].indirect(idx_list[:]), e_c[t][:], own_term[:, t * C : (t + 1) * C], ADD)
-            rows = out[t * P : (t + 1) * P, :]
-            if t + 1 < D_TILES:
-                nc.sync.dma_start(rows, window[:])
-            else:
-                nc.sync.dma_start(rows[:, : T // 2], window[:, : T // 2])
-                nc.scalar.dma_start(rows[:, T // 2 :], window[:, T // 2 :])
+            nc.sync.dma_start(out[t * P : (t + 1) * P, :], window[:])
 
         gather_table(0)
         gather_table(1)

@@ -27,7 +27,10 @@ C_BLOCKS = C // P
 WINDOW = 1376
 GY_ROW = P - 1
 SCALAR_COLS = 320
-LATE_DS_BYTES = 4 * X_BLOCKS * 2 * P
+PIECE = 128
+LEAD = 4
+RING = 7
+RING_AT = C - 4 * PIECE
 JOINT_COLS = 3 * T // 4
 
 
@@ -35,7 +38,6 @@ def tile_attend_gfm_bi_kernel(tc, vT, W, dz, gy, offs, boffs, soffs, out):
     nc = tc.nc
     with ExitStack() as ctx:
         keep = ctx.enter_context(tc.tile_pool(name="keep", bufs=1))
-        shared = ctx.enter_context(tc.tile_pool(name="shared", bufs=1))
         psum = ctx.enter_context(tc.psum_pool(name="psum", bufs=1))
 
         bag_list = keep.tile([P, C // STRIPE], U16, name="bag_list")
@@ -63,19 +65,19 @@ def tile_attend_gfm_bi_kernel(tc, vT, W, dz, gy, offs, boffs, soffs, out):
 
         picked = keep.tile([P, (D_TILES - 1) * C + WINDOW], F32, name="picked")
         e_pairs = [
-            shared.tile([P, X + WINDOW], F32, name="e_early", offset=LATE_DS_BYTES - 32),
+            keep.tile([P, 2 * X], F32, name="e_early"),
             keep.tile([P, X + WINDOW], F32, name="e_late"),
         ]
         identity = keep.tile([P, P], F32, name="identity")
 
-        placed_even = keep.tile([P, T], F32, name="placed_even")
+        placed = [keep.tile([P, T], F32, name="placed%d" % u) for u in range(2)]
 
         nc.gpsimd.memset(gy_win[:GY_ROW, :], 0.0)
         make_identity(nc, identity[:])
         nc.gpsimd.memset(picked[:, D_TILES * C :], 0.0)
-        for e_pair in e_pairs:
-            nc.gpsimd.memset(e_pair[:, 2 * X :], 0.0)
-        nc.gpsimd.memset(placed_even[:], 0.0)
+        nc.gpsimd.memset(e_pairs[1][:, 2 * X :], 0.0)
+        for window in placed:
+            nc.gpsimd.memset(window[:], 0.0)
 
         def gather(dst, tile, at, entries):
             room = min(tile.shape[1] - at, WINDOW)
@@ -164,7 +166,7 @@ def tile_attend_gfm_bi_kernel(tc, vT, W, dz, gy, offs, boffs, soffs, out):
 
         w_codes = keep.tile([P, D], U32, name="w_codes", align_bytes=64)
         w_scales = keep.tile([P, D], U8, name="w_scales", align_bytes=64)
-        dz_codes = keep.tile([P, X], U32, name="dz_codes", tag="room_c", align_bytes=64)
+        dz_codes = keep.tile([P, X], U32, name="dz_codes", align_bytes=64)
         dz_scales = keep.tile([P, X], U8, name="dz_scales", align_bytes=64)
 
         def quantise(raw, codes, scales, fmt, room):
@@ -199,15 +201,30 @@ def tile_attend_gfm_bi_kernel(tc, vT, W, dz, gy, offs, boffs, soffs, out):
                 nc.scalar.copy(ds_pair[:, b, :], acc[:, 2 * pair * P : 2 * (pair + 1) * P])
             return ds_pair
 
-        e_c = {}
+        e_both = keep.tile([P, 2 * C], F32, name="e_both")
+        e_c = [e_both[:, C:], e_both[:, :C]]
 
         def gather_e(t):
-            e_c[t] = keep.tile([P, C], F32, name="e_c%d" % t)
-            gather(e_c[t], e_pairs[t // 2], e_at(t), bag_list)
+            gather(e_c[t % 2], e_pairs[t // 2], e_at(t), bag_list)
+
+        def entries(k):
+            return slice(k * PIECE // STRIPE, (k + 1) * PIECE // STRIPE)
+
+        def ring_slot(j):
+            return e_both[:, RING_AT + j % RING * PIECE : RING_AT + (j % RING + 1) * PIECE]
+
+        def gather_e_piece(j):
+            k, t = divmod(j, 2)
+            nc.vector.tensor_copy(ring_slot(j), e_pairs[0][:, e_at(t) :].indirect(bag_list[:, entries(k)]))
+
+        def place_piece(j):
+            k, t = divmod(j, 2)
+            lo = t * C + k * PIECE
+            nc.vector.tensor_tensor(placed[t][:].indirect(idx_list[:, entries(k)]), ring_slot(j), own_term[:, lo : lo + PIECE], ADD)
 
         def place(t):
             window = placed[t % 2]
-            nc.vector.tensor_tensor(window[:].indirect(idx_list[:]), e_c[t][:], own_term[:, t * C : (t + 1) * C], ADD)
+            nc.vector.tensor_tensor(window[:].indirect(idx_list[:]), e_c[t % 2], own_term[:, t * C : (t + 1) * C], ADD)
             nc.sync.dma_start(out[t * P : (t + 1) * P, :], window[:])
 
         gather_table(0)
@@ -215,7 +232,7 @@ def tile_attend_gfm_bi_kernel(tc, vT, W, dz, gy, offs, boffs, soffs, out):
         gather_bags(0)
         gather_bags(1)
         quantise(w_raw, w_codes, w_scales, E4M3X4, "w_grouped")
-        quantise(dz_raw, dz_codes, dz_scales, E5M2X4, "room_b")
+        quantise(dz_raw, dz_codes, dz_scales, E5M2X4, "room_c")
         neg_gy_c = keep.tile([P, C], F32, name="neg_gy_c", tag="room_a")
         for h in range(2):
             bank = bank_tile(h, [P, 4, P])
@@ -235,16 +252,18 @@ def tile_attend_gfm_bi_kernel(tc, vT, W, dz, gy, offs, boffs, soffs, out):
         make_own(3)
         gather_bags(2)
         gather_bags(3)
-        gather_e(0)
-        gather_e(1)
-        placed_odd = shared.tile([P, T], F32, name="placed_odd", offset=LATE_DS_BYTES)
-        nc.gpsimd.memset(placed_odd[:], 0.0)
-        placed = [placed_even, placed_odd]
-        ds_late = copy_dense_gradient(1, ds_sums, shared.tile([P, X_BLOCKS, 2 * P], F32, name="ds_late", offset=0))
+        ds_late = copy_dense_gradient(1, ds_sums, keep.tile([P, X_BLOCKS, 2 * P], F32, name="ds_late"))
         sums_scaled = scale_sums(1, (6, 7))
         finish_e(1, ds_late, sums_scaled, (2, 3))
-        place(0)
-        place(1)
+        steps = 2 * C // PIECE
+        for j in range(LEAD):
+            gather_e_piece(j)
+        for j in range(steps):
+            place_piece(j)
+            if j + LEAD < steps:
+                gather_e_piece(j + LEAD)
+        for t in range(2):
+            nc.sync.dma_start(out[t * P : (t + 1) * P, :], placed[t][:])
         gather_e(2)
         gather_e(3)
         place(2)

@@ -28,9 +28,11 @@ WINDOW = 1376
 GY_ROW = P - 1
 SCALAR_COLS = 320
 PIECE = 128
-LEAD = 4
-RING = 7
-RING_AT = C - 4 * PIECE
+HALF = PIECE // 2
+PIECES = C // PIECE
+RING = 3
+EARLY_DS = X_BLOCKS * 2 * P
+LATE_ORDER = ((2, 0), (2, 1), (2, 2), (2, 6), (3, 0), (2, 3), (3, 1), (2, 4), (3, 2), (2, 5), (3, 3), (2, 7), (3, 4), (3, 5), (3, 6), (3, 7))
 JOINT_COLS = 3 * T // 4
 
 
@@ -38,6 +40,7 @@ def tile_attend_gfm_bi_kernel(tc, vT, W, dz, gy, offs, boffs, soffs, out):
     nc = tc.nc
     with ExitStack() as ctx:
         keep = ctx.enter_context(tc.tile_pool(name="keep", bufs=1))
+        shared = ctx.enter_context(tc.tile_pool(name="shared", bufs=1))
         psum = ctx.enter_context(tc.psum_pool(name="psum", bufs=1))
 
         bag_list = keep.tile([P, C // STRIPE], U16, name="bag_list")
@@ -45,10 +48,10 @@ def tile_attend_gfm_bi_kernel(tc, vT, W, dz, gy, offs, boffs, soffs, out):
         slot_list = keep.tile([P, C // STRIPE], U16, name="slot_list")
         gy_win = keep.tile([P, X], F32, name="gy_win")
         first_tables = [keep.tile([P, T], F32, name="table", tag="table%d" % t) for t in range(2)]
-        last_tables = keep.tile([P, 2, T], F32, name="last_tables")
+        last_tables = shared.tile([P, 2, T], F32, name="last_tables", offset=0)
         tables = [first_tables[0][:], first_tables[1][:], last_tables[:, 0, :], last_tables[:, 1, :]]
         w_raw = keep.tile([P, PACK, D], F32, name="w_raw")
-        dz_raw = keep.tile([P, PACK, X], F32, name="dz_raw", tag="room_a")
+        dz_raw = keep.tile([P, PACK, X], F32, name="dz_raw", tag="room_a", align_bytes=64)
 
         nc.scalar.dma_start(gy_win[GY_ROW:, :], gy[0:1, :])
         nc.sync.dma_start(bag_list[:], boffs)
@@ -64,10 +67,7 @@ def tile_attend_gfm_bi_kernel(tc, vT, W, dz, gy, offs, boffs, soffs, out):
             nc.sync.dma_start(last_tables[:, u, JOINT_COLS:], last_rows[:, u, JOINT_COLS:])
 
         picked = keep.tile([P, (D_TILES - 1) * C + WINDOW], F32, name="picked")
-        e_pairs = [
-            keep.tile([P, 2 * X], F32, name="e_early"),
-            keep.tile([P, X + WINDOW], F32, name="e_late"),
-        ]
+        e_all = keep.tile([P, D_TILES * X], F32, name="e_all")
         identity = keep.tile([P, P], F32, name="identity")
 
         placed = [keep.tile([P, T], F32, name="placed%d" % u) for u in range(2)]
@@ -75,7 +75,6 @@ def tile_attend_gfm_bi_kernel(tc, vT, W, dz, gy, offs, boffs, soffs, out):
         nc.gpsimd.memset(gy_win[:GY_ROW, :], 0.0)
         make_identity(nc, identity[:])
         nc.gpsimd.memset(picked[:, D_TILES * C :], 0.0)
-        nc.gpsimd.memset(e_pairs[1][:, 2 * X :], 0.0)
         for window in placed:
             nc.gpsimd.memset(window[:], 0.0)
 
@@ -112,64 +111,90 @@ def tile_attend_gfm_bi_kernel(tc, vT, W, dz, gy, offs, boffs, soffs, out):
                 turn(bank[:, b, :], [gy_c[:, block(4 * h + b)]])
             nc.scalar.activation(neg_gy_c_col[:, 4 * h : 4 * h + 4], bank[:, :, GY_ROW], COPY, scale=-1.0)
 
-        def picked_at(t):
-            return (D_TILES - 1 - t) * C
+        neg_gy_c = keep.tile([P, C], F32, name="neg_gy_c")
+        for h in range(2):
+            bank = bank_tile(h, [P, 4, P])
+            for b in range(4):
+                turn(bank[:, b, :], [neg_gy_c_col[:, 4 * h + b : 4 * h + b + 1].to_broadcast([P, P])])
+            nc.scalar.copy(neg_gy_c[:, h * BANK : (h + 1) * BANK], bank[:].rearrange("p b c -> p (b c)"))
 
-        def e_at(t):
-            return (t % 2) * X
+        late = keep.tile([P, PIECE + 2 * C], F32, name="late")
+        ring = keep.tile([P, RING * PIECE], F32, name="ring")
+        by_sample = [keep.tile([P, C], F32, name="by_sample%d" % t)[:] for t in range(2)]
+
+        def picked_at(t):
+            return (2, 3, 1, 0)[t] * C
+
+        def entries(lo, hi):
+            return slice(lo // STRIPE, hi // STRIPE)
 
         def gather_table(t):
             nc.vector.tensor_copy(picked[:, picked_at(t) : picked_at(t) + C], tables[t].indirect(idx_list[:]))
 
-        by_sample = [keep.tile([P, C], F32, name="by_sample%d" % t) for t in range(D_TILES)]
-
-        def make_own(t):
-            nc.gpsimd.tensor_tensor(own_term[:, t * C : (t + 1) * C], picked[:, picked_at(t) : picked_at(t) + C], neg_gy_c[:], MULT)
+        def make_early_own():
+            nc.gpsimd.tensor_tensor(
+                early[:, EARLY_DS : EARLY_DS + 2 * C].rearrange("p (k u c) -> p u k c", u=2, c=HALF),
+                picked[:, picked_at(0) : picked_at(0) + 2 * C].rearrange("p (u k c) -> p u k c", u=2, c=HALF),
+                neg_gy_c[:].rearrange("p (u k c) -> p u k c", u=1, c=HALF).to_broadcast([P, 2, C // HALF, HALF]),
+                MULT,
+            )
 
         def gather_bags(t):
             gather(by_sample[t], picked, picked_at(t), slot_list)
 
-        def turn_and_scale(pair, blocks, source, factors, room, banks):
-            scaled = keep.tile([P, blocks, 2, P], F32, name="scaled", tag=room, align_bytes=64)
-            turned = [bank_tile(k, [P, 2, 2, P]) for k in banks]
-            for u in range(2):
-                for b in range(blocks):
-                    turn(turned[b // 2][:, b % 2, u, :], source(2 * pair + u, b))
-            for b in range(blocks):
-                nc.scalar.activation(scaled[:, b, :, :], turned[b // 2][:, b % 2, :, :], COPY, scale=factors[:, b : b + 1])
+        def gather_bags_piece(i):
+            u, k = divmod(i, PIECES)
+            at = picked_at(2 + u)
+            nc.vector.tensor_copy(by_sample[2 + u][:, block(k)], picked[:, at : at + C].indirect(slot_list[:, entries(k * PIECE, (k + 1) * PIECE)]))
+
+        def gather_e(dst, t, lo, hi, tiles=1):
+            nc.vector.tensor_copy(dst, e_all[:, t * X : (t + tiles) * X].indirect(bag_list[:, entries(lo, hi)]))
+
+        def place(t, lo, hi, e_part, own_part):
+            nc.vector.tensor_tensor(placed[t][:].indirect(idx_list[:, entries(lo, hi)]), e_part, own_part, ADD)
+
+        def store(t):
+            nc.sync.dma_start(out[t * P : (t + 1) * P, :], placed[t][:])
+
+        def scale_sums(tiles, room, banks):
+            n = len(tiles)
+            scaled = keep.tile([P, X_BLOCKS, n, P], F32, name="scaled", tag=room, align_bytes=64)
+            per_bank = X_BLOCKS // n
+            turned = [bank_tile(k, [P, per_bank, n, P]) for k in banks]
+            for u, t in enumerate(tiles):
+                pairs = by_sample[t].rearrange("p (x j) -> p j x", j=2)
+                for b in range(X_BLOCKS):
+                    turn(turned[b // per_bank][:, b % per_bank, u, :], [pairs[:, j, block(b)] for j in range(2)])
+            for b in range(X_BLOCKS):
+                nc.scalar.activation(scaled[:, b, :, :], turned[b // per_bank][:, b % per_bank, :, :], COPY, scale=gy_col[:, b : b + 1])
             return scaled
 
-        def turn_back(pair, parts, result, banks):
-            for u in range(2):
-                back = bank_tile(banks[u], [P, 4, P])
-                for b in range(4):
-                    turn(back[:, b, :], parts(u, b))
-                nc.scalar.copy(result(2 * pair + u), back[:].rearrange("p b c -> p (b c)"))
+        def finish_e(tiles, ds_pair, scaled, banks):
+            for u, t in enumerate(tiles):
+                back = bank_tile(banks[u], [P, X_BLOCKS, P])
+                for b in range(X_BLOCKS):
+                    turn(back[:, b, :], [ds_pair[:, b, block(t % 2)], scaled[:, b, u, :]])
+                nc.scalar.copy(e_all[:, t * X : (t + 1) * X], back[:].rearrange("p b c -> p (b c)"))
 
-        def scale_sums(pair, banks):
-            return turn_and_scale(
-                pair,
-                X_BLOCKS,
-                lambda t, b: [by_sample[t][:].rearrange("p (x j) -> p j x", j=2)[:, j, block(b)] for j in range(2)],
-                gy_col,
-                "room_b",
-                banks,
-            )
-
-        def finish_e(pair, ds_pair, scaled, banks):
-            turn_back(
-                pair,
-                lambda u, b: [ds_pair[:, b, block(u)], scaled[:, b, u, :]],
-                lambda t: e_pairs[pair][:, e_at(t) : e_at(t) + X],
-                banks,
-            )
+        def make_late_own(g, banks):
+            group = LATE_ORDER[4 * g : 4 * g + 4]
+            turned = bank_tile(banks[0], [P, 4, P])
+            scaled = keep.tile([P, 4, P], F32, name="scaled_own", tag="scaled_own%d" % (g % 2))
+            for n, (t, k) in enumerate(group):
+                turn(turned[:, n, :], [picked[:, picked_at(t) + k * P : picked_at(t) + (k + 1) * P]])
+            for n, (t, k) in enumerate(group):
+                nc.scalar.activation(scaled[:, n, :], turned[:, n, :], COPY, scale=neg_gy_c_col[:, k : k + 1])
+            back = bank_tile(banks[1], [P, 4, P])
+            for n in range(4):
+                turn(back[:, n, :], [scaled[:, n, :]])
+            nc.scalar.copy(late[:, PIECE + g * BANK : PIECE + (g + 1) * BANK], back[:].rearrange("p b c -> p (b c)"))
 
         w_codes = keep.tile([P, D], U32, name="w_codes", align_bytes=64)
         w_scales = keep.tile([P, D], U8, name="w_scales", align_bytes=64)
         dz_codes = keep.tile([P, X], U32, name="dz_codes", align_bytes=64)
         dz_scales = keep.tile([P, X], U8, name="dz_scales", align_bytes=64)
 
-        def quantise(raw, codes, scales, fmt, room):
+        def quantise(raw, codes, scales, fmt, room, scalar_cols):
             grouped = keep.tile([P, BANK, PACK], BF16, name="grouped", tag=room, align_bytes=64)
 
             def interleaved(cols):
@@ -178,8 +203,9 @@ def tile_attend_gfm_bi_kernel(tc, vT, W, dz, gy, offs, boffs, soffs, out):
                     raw[:, :, cols].rearrange("p j (c i) -> p c j i", i=4),
                 )
 
-            nc.scalar.copy(*interleaved(slice(0, SCALAR_COLS)))
-            nc.gpsimd.tensor_scalar(*interleaved(slice(SCALAR_COLS, BANK)), 1.0, 0.0, MULT, ADD)
+            nc.scalar.copy(*interleaved(slice(0, scalar_cols)))
+            if scalar_cols < BANK:
+                nc.gpsimd.tensor_scalar(*interleaved(slice(scalar_cols, BANK)), 1.0, 0.0, MULT, ADD)
             nc.vector.quantize_mx(out=codes[:].bitcast(fmt), scales=scales[:], in_=grouped[:].rearrange("p w j -> p (w j)"))
 
         def dense_gradient(banks):
@@ -201,70 +227,82 @@ def tile_attend_gfm_bi_kernel(tc, vT, W, dz, gy, offs, boffs, soffs, out):
                 nc.scalar.copy(ds_pair[:, b, :], acc[:, 2 * pair * P : 2 * (pair + 1) * P])
             return ds_pair
 
-        e_both = keep.tile([P, 2 * C], F32, name="e_both")
-        e_c = [e_both[:, C:], e_both[:, :C]]
-
-        def gather_e(t):
-            gather(e_c[t % 2], e_pairs[t // 2], e_at(t), bag_list)
-
-        def entries(k):
-            return slice(k * PIECE // STRIPE, (k + 1) * PIECE // STRIPE)
-
-        def ring_slot(j):
-            return e_both[:, RING_AT + j % RING * PIECE : RING_AT + (j % RING + 1) * PIECE]
-
-        def gather_e_piece(j):
-            k, t = divmod(j, 2)
-            nc.vector.tensor_copy(ring_slot(j), e_pairs[0][:, e_at(t) :].indirect(bag_list[:, entries(k)]))
-
-        def place_piece(j):
-            k, t = divmod(j, 2)
-            lo = t * C + k * PIECE
-            nc.vector.tensor_tensor(placed[t][:].indirect(idx_list[:, entries(k)]), ring_slot(j), own_term[:, lo : lo + PIECE], ADD)
-
-        def place(t):
-            window = placed[t % 2]
-            nc.vector.tensor_tensor(window[:].indirect(idx_list[:]), e_c[t % 2], own_term[:, t * C : (t + 1) * C], ADD)
-            nc.sync.dma_start(out[t * P : (t + 1) * P, :], window[:])
-
         gather_table(0)
         gather_table(1)
         gather_bags(0)
         gather_bags(1)
-        quantise(w_raw, w_codes, w_scales, E4M3X4, "w_grouped")
-        quantise(dz_raw, dz_codes, dz_scales, E5M2X4, "room_c")
-        neg_gy_c = keep.tile([P, C], F32, name="neg_gy_c", tag="room_a")
-        for h in range(2):
-            bank = bank_tile(h, [P, 4, P])
-            for b in range(4):
-                turn(bank[:, b, :], [neg_gy_c_col[:, 4 * h + b : 4 * h + b + 1].to_broadcast([P, P])])
-            nc.scalar.copy(neg_gy_c[:, h * BANK : (h + 1) * BANK], bank[:].rearrange("p b c -> p (b c)"))
-        sums_scaled = scale_sums(0, (4, 5))
+        quantise(w_raw, w_codes, w_scales, E4M3X4, "w_grouped", SCALAR_COLS)
+        quantise(dz_raw, dz_codes, dz_scales, E5M2X4, "room_b", SCALAR_COLS)
+        early = keep.tile([P, EARLY_DS + 2 * C + PIECE], F32, name="early", tag="room_b", align_bytes=64)
+        by_sample += [early[:, EARLY_DS - PIECE + u * C : EARLY_DS - PIECE + (u + 1) * C] for u in range(2)]
+        make_early_own()
+        sums_scaled = scale_sums((0, 1), "room_a", (0, 1))
         ds_sums = dense_gradient((6, 7, 2, 3))
-        ds_early = copy_dense_gradient(0, ds_sums, keep.tile([P, X_BLOCKS, 2 * P], F32, name="ds_early"))
-        finish_e(0, ds_early, sums_scaled, (0, 1))
-        own_term = keep.tile([P, D_TILES * C], F32, name="own_term", tag="room_c", align_bytes=64)
-        make_own(0)
-        make_own(1)
+        ds_early = copy_dense_gradient(0, ds_sums, early[:, :EARLY_DS].rearrange("p (b c) -> p b c", b=X_BLOCKS))
+        finish_e((0, 1), ds_early, sums_scaled, (4, 5))
         gather_table(2)
         gather_table(3)
-        make_own(2)
-        make_own(3)
-        gather_bags(2)
-        gather_bags(3)
-        ds_late = copy_dense_gradient(1, ds_sums, keep.tile([P, X_BLOCKS, 2 * P], F32, name="ds_late"))
-        sums_scaled = scale_sums(1, (6, 7))
-        finish_e(1, ds_late, sums_scaled, (2, 3))
-        steps = 2 * C // PIECE
-        for j in range(LEAD):
-            gather_e_piece(j)
-        for j in range(steps):
-            place_piece(j)
-            if j + LEAD < steps:
-                gather_e_piece(j + LEAD)
-        for t in range(2):
-            nc.sync.dma_start(out[t * P : (t + 1) * P, :], placed[t][:])
-        gather_e(2)
-        gather_e(3)
-        place(2)
-        place(3)
+        for u in range(2):
+            placed.append(shared.tile([P, T], F32, name="placed%d" % (2 + u), offset=4 * T * u))
+            nc.gpsimd.memset(placed[2 + u][:], 0.0)
+        ds_late = copy_dense_gradient(1, ds_sums, keep.tile([P, X_BLOCKS, 2 * P], F32, name="ds_late", tag="room_a", align_bytes=64))
+        for g in range(4):
+            make_late_own(g, (5 - g % 2, g % 2))
+
+        def ring_slot(i):
+            return ring[:, block(i % RING)]
+
+        def gather_ring(i):
+            k, t = divmod(i, 2)
+            if k < PIECES:
+                gather_e(ring_slot(i), t, k * PIECE, (k + 1) * PIECE, 2 if i in (0, 2) else 1)
+            else:
+                gather_e(ring_slot(i), 2, t * PIECE, (t + 1) * PIECE)
+
+        def place_early(t, h):
+            j = 2 * h + t
+            e_part = ring_slot(h // 2 * 2 + t)[:, h % 2 * HALF : (h % 2 + 1) * HALF]
+            place(t, h * HALF, (h + 1) * HALF, e_part, early[:, EARLY_DS + j * HALF : EARLY_DS + (j + 1) * HALF])
+
+        gather_ring(0)
+        gather_ring(1)
+        for k in range(PIECES):
+            place_early(0, 2 * k)
+            gather_ring(2 * k + 2)
+            place_early(1, 2 * k)
+            gather_bags_piece(2 * k)
+            place_early(0, 2 * k + 1)
+            gather_bags_piece(2 * k + 1)
+            place_early(1, 2 * k + 1)
+            gather_ring(2 * k + 3)
+            if k == PIECES // 2 - 1:
+                finish_e((2,), ds_late, scale_sums((2,), "scaled2", (6,)), (7,))
+        finish_e((3,), ds_late, scale_sums((3,), "scaled3", (7,)), (6,))
+        store(0)
+        store(1)
+
+        def late_at(q, n=1):
+            return late[:, (q + 1) * PIECE : (q + 1 + n) * PIECE]
+
+        def place_late(q, e_part, n=1):
+            t, k = LATE_ORDER[q]
+            place(t, k * PIECE, (k + n) * PIECE, e_part, late_at(q, n))
+
+        early_end = early[:, EARLY_DS + 2 * C - PIECE :]
+        place_late(0, ring_slot(16))
+        gather_e(early_end, 2, 2 * PIECE, 4 * PIECE)
+        place_late(1, ring_slot(17))
+        gather_e(late_at(-1, 2), 2, 4 * PIECE, 6 * PIECE)
+        place_late(2, early_end[:, :PIECE])
+        gather_e(late_at(1), 2, 6 * PIECE, 7 * PIECE, 2)
+        gather_e(ring_slot(17), 3, 0, PIECE)
+        place_late(3, late_at(1))
+        gather_e(late_at(2), 2, 7 * PIECE, C)
+        sources = [ring_slot(17), early_end[:, PIECE:], late_at(3), late_at(-1), late_at(4), late_at(0), late_at(5), late_at(2)]
+        for q in range(4, 12):
+            place_late(q, sources[q - 4])
+            if q < 11:
+                gather_e(late_at(q - 1), 3, (q - 3) * PIECE, (q - 2) * PIECE)
+        store(2)
+        place_late(12, late_at(6, 4), 4)
+        store(3)

@@ -26,11 +26,11 @@ X_BLOCKS = X // P
 C_BLOCKS = C // P
 WINDOW = 1376
 GY_ROW = P - 1
-SCALAR_COLS = 320
+SCALAR_COLS = 384
 PIECE = 128
 HALF = PIECE // 2
 PIECES = C // PIECE
-RING = 3
+FIRST_BAGS = 512
 EARLY_DS = X_BLOCKS * 2 * P
 LATE_ORDER = ((2, 0), (2, 1), (2, 2), (2, 6), (3, 0), (2, 3), (3, 1), (2, 4), (3, 2), (2, 5), (3, 3), (2, 7), (3, 4), (3, 5), (3, 6), (3, 7))
 JOINT_COLS = 3 * T // 4
@@ -50,7 +50,7 @@ def tile_attend_gfm_bi_kernel(tc, vT, W, dz, gy, offs, boffs, soffs, out):
         first_tables = [keep.tile([P, T], F32, name="table", tag="table%d" % t) for t in range(2)]
         last_tables = shared.tile([P, 2, T], F32, name="last_tables", offset=0)
         tables = [first_tables[0][:], first_tables[1][:], last_tables[:, 0, :], last_tables[:, 1, :]]
-        w_raw = keep.tile([P, PACK, D], F32, name="w_raw")
+        w_raw = keep.tile([P, PACK, D], F32, name="w_raw", tag="room_w", align_bytes=64)
         dz_raw = keep.tile([P, PACK, X], F32, name="dz_raw", tag="room_a", align_bytes=64)
 
         nc.scalar.dma_start(gy_win[GY_ROW:, :], gy[0:1, :])
@@ -119,8 +119,8 @@ def tile_attend_gfm_bi_kernel(tc, vT, W, dz, gy, offs, boffs, soffs, out):
             nc.scalar.copy(neg_gy_c[:, h * BANK : (h + 1) * BANK], bank[:].rearrange("p b c -> p (b c)"))
 
         late = keep.tile([P, PIECE + 2 * C], F32, name="late")
-        ring = keep.tile([P, RING * PIECE], F32, name="ring")
-        by_sample = [keep.tile([P, C], F32, name="by_sample%d" % t)[:] for t in range(2)]
+        stairs = [keep.tile([P, PIECES * HALF + PIECE], F32, name="stairs%d" % t) for t in range(2)]
+        by_sample = [keep.tile([P, C], F32, name="by_sample0")[:], keep.tile([P, FIRST_BAGS], F32, name="by_sample1")[:]]
 
         def picked_at(t):
             return (2, 3, 1, 0)[t] * C
@@ -131,16 +131,21 @@ def tile_attend_gfm_bi_kernel(tc, vT, W, dz, gy, offs, boffs, soffs, out):
         def gather_table(t):
             nc.vector.tensor_copy(picked[:, picked_at(t) : picked_at(t) + C], tables[t].indirect(idx_list[:]))
 
+        def early_own_at(t, h):
+            return EARLY_DS + (2 * (h // 2 + 1) + t) * PIECE + h % 2 * HALF
+
         def make_early_own():
+            lo = early_own_at(0, 0)
             nc.gpsimd.tensor_tensor(
-                early[:, EARLY_DS : EARLY_DS + 2 * C].rearrange("p (k u c) -> p u k c", u=2, c=HALF),
-                picked[:, picked_at(0) : picked_at(0) + 2 * C].rearrange("p (u k c) -> p u k c", u=2, c=HALF),
-                neg_gy_c[:].rearrange("p (u k c) -> p u k c", u=1, c=HALF).to_broadcast([P, 2, C // HALF, HALF]),
+                early[:, lo : lo + 2 * C].rearrange("p (k u c) -> p u k c", u=2, c=PIECE),
+                picked[:, picked_at(0) : picked_at(0) + 2 * C].rearrange("p (u k c) -> p u k c", u=2, c=PIECE),
+                neg_gy_c[:].rearrange("p (u k c) -> p u k c", u=1, c=PIECE).to_broadcast([P, 2, PIECES, PIECE]),
                 MULT,
             )
 
-        def gather_bags(t):
-            gather(by_sample[t], picked, picked_at(t), slot_list)
+        def gather_bags(dst, t, lo, hi):
+            at = picked_at(t)
+            nc.vector.tensor_copy(dst, picked[:, at : at + WINDOW].indirect(slot_list[:, entries(lo, hi)]))
 
         def gather_bags_piece(i):
             u, k = divmod(i, PIECES)
@@ -156,25 +161,34 @@ def tile_attend_gfm_bi_kernel(tc, vT, W, dz, gy, offs, boffs, soffs, out):
         def store(t):
             nc.sync.dma_start(out[t * P : (t + 1) * P, :], placed[t][:])
 
-        def scale_sums(tiles, room, banks):
-            n = len(tiles)
-            scaled = keep.tile([P, X_BLOCKS, n, P], F32, name="scaled", tag=room, align_bytes=64)
-            per_bank = X_BLOCKS // n
-            turned = [bank_tile(k, [P, per_bank, n, P]) for k in banks]
-            for u, t in enumerate(tiles):
-                pairs = by_sample[t].rearrange("p (x j) -> p j x", j=2)
-                for b in range(X_BLOCKS):
-                    turn(turned[b // per_bank][:, b % per_bank, u, :], [pairs[:, j, block(b)] for j in range(2)])
+        def scale_sums(sources, room, banks):
+            scaled = keep.tile([P, X_BLOCKS, P], F32, name="scaled", tag=room, align_bytes=64)
+            turned = {k: bank_tile(k, [P, X_BLOCKS, P]) for k in sorted(set(banks))}
             for b in range(X_BLOCKS):
-                nc.scalar.activation(scaled[:, b, :, :], turned[b // per_bank][:, b % per_bank, :, :], COPY, scale=gy_col[:, b : b + 1])
-            return scaled
+                pairs = sources[b].rearrange("p (x j) -> p j x", j=2)
+                turn(turned[banks[b]][:, b, :], [pairs[:, j, :] for j in range(2)])
+            for b in range(X_BLOCKS):
+                nc.scalar.activation(scaled[:, b, :], turned[banks[b]][:, b, :], COPY, scale=gy_col[:, b : b + 1])
+            return [scaled[:, b, :] for b in range(X_BLOCKS)]
 
-        def finish_e(tiles, ds_pair, scaled, banks):
-            for u, t in enumerate(tiles):
-                back = bank_tile(banks[u], [P, X_BLOCKS, P])
-                for b in range(X_BLOCKS):
-                    turn(back[:, b, :], [ds_pair[:, b, block(t % 2)], scaled[:, b, u, :]])
-                nc.scalar.copy(e_all[:, t * X : (t + 1) * X], back[:].rearrange("p b c -> p (b c)"))
+        def turn_back(back, parts, opens):
+            for b, part in enumerate(parts):
+                nc.tensor.matmul(back[:, b, :], part, identity[:], start=(opens and b == 0), stop=(not opens and b == X_BLOCKS - 1), is_transpose=True)
+
+        def copy_e(t, back):
+            nc.scalar.copy(e_all[:, t * X : (t + 1) * X], back[:].rearrange("p b c -> p (b c)"))
+
+        def blocks_of(run):
+            return [run[:, 2 * b * P : 2 * (b + 1) * P] for b in range(run.shape[1] // (2 * P))]
+
+        def ds_blocks(ds_pair, t):
+            return [ds_pair[:, b, block(t % 2)] for b in range(X_BLOCKS)]
+
+        def make_late_e(t, ds_pair, room, banks):
+            back = bank_tile(banks[-1], [P, X_BLOCKS, P])
+            turn_back(back, ds_blocks(ds_pair, t), True)
+            turn_back(back, scale_sums(blocks_of(by_sample[t]), room, banks[:-1]), False)
+            copy_e(t, back)
 
         def make_late_own(g, banks):
             group = LATE_ORDER[4 * g : 4 * g + 4]
@@ -229,55 +243,61 @@ def tile_attend_gfm_bi_kernel(tc, vT, W, dz, gy, offs, boffs, soffs, out):
 
         gather_table(0)
         gather_table(1)
-        gather_bags(0)
-        gather_bags(1)
+        gather_bags(by_sample[0], 0, 0, C)
+        gather_bags(by_sample[1], 1, 0, FIRST_BAGS)
         quantise(w_raw, w_codes, w_scales, E4M3X4, "w_grouped", SCALAR_COLS)
         quantise(dz_raw, dz_codes, dz_scales, E5M2X4, "room_b", SCALAR_COLS)
-        early = keep.tile([P, EARLY_DS + 2 * C + PIECE], F32, name="early", tag="room_b", align_bytes=64)
-        by_sample += [early[:, EARLY_DS - PIECE + u * C : EARLY_DS - PIECE + (u + 1) * C] for u in range(2)]
+        early = keep.tile([P, EARLY_DS + 2 * C + 2 * PIECE], F32, name="early", tag="room_b", align_bytes=64)
+        by_sample += [early[:, EARLY_DS + u * C : EARLY_DS + (u + 1) * C] for u in range(2)]
         make_early_own()
-        sums_scaled = scale_sums((0, 1), "room_a", (0, 1))
+        last_bags = keep.tile([P, C - FIRST_BAGS], F32, name="last_bags", tag="room_a", align_bytes=64)
+        gather_bags(last_bags[:], 1, FIRST_BAGS, C)
+        backs = [bank_tile(4 + t, [P, X_BLOCKS, P]) for t in range(2)]
+        turn_back(backs[0], scale_sums(blocks_of(by_sample[0]), "room_w", (0, 0, 0, 0)), True)
         ds_sums = dense_gradient((6, 7, 2, 3))
         ds_early = copy_dense_gradient(0, ds_sums, early[:, :EARLY_DS].rearrange("p (b c) -> p b c", b=X_BLOCKS))
-        finish_e((0, 1), ds_early, sums_scaled, (4, 5))
+        scaled = scale_sums(blocks_of(by_sample[1]) + blocks_of(last_bags[:]), "scaled1", (1, 1, 0, 0))
+        turn_back(backs[0], ds_blocks(ds_early, 0), False)
+        copy_e(0, backs[0])
+        turn_back(backs[1], ds_blocks(ds_early, 1), True)
+        turn_back(backs[1], scaled, False)
+        copy_e(1, backs[1])
         gather_table(2)
         gather_table(3)
         for u in range(2):
             placed.append(shared.tile([P, T], F32, name="placed%d" % (2 + u), offset=4 * T * u))
             nc.gpsimd.memset(placed[2 + u][:], 0.0)
-        ds_late = copy_dense_gradient(1, ds_sums, keep.tile([P, X_BLOCKS, 2 * P], F32, name="ds_late", tag="room_a", align_bytes=64))
+        ds_late = copy_dense_gradient(1, ds_sums, keep.tile([P, X_BLOCKS, 2 * P], F32, name="ds_late", tag="scaled1", align_bytes=64))
         for g in range(4):
             make_late_own(g, (5 - g % 2, g % 2))
 
         def ring_slot(i):
-            return ring[:, block(i % RING)]
+            k, t = divmod(i, 2)
+            return stairs[t][:, (PIECES - k) * HALF : (PIECES - k) * HALF + PIECE]
 
         def gather_ring(i):
             k, t = divmod(i, 2)
             if k < PIECES:
-                gather_e(ring_slot(i), t, k * PIECE, (k + 1) * PIECE, 2 if i in (0, 2) else 1)
+                gather_e(ring_slot(i), t, k * PIECE, (k + 1) * PIECE, 2 if i == 0 else 1)
             else:
                 gather_e(ring_slot(i), 2, t * PIECE, (t + 1) * PIECE)
 
         def place_early(t, h):
-            j = 2 * h + t
             e_part = ring_slot(h // 2 * 2 + t)[:, h % 2 * HALF : (h % 2 + 1) * HALF]
-            place(t, h * HALF, (h + 1) * HALF, e_part, early[:, EARLY_DS + j * HALF : EARLY_DS + (j + 1) * HALF])
+            place(t, h * HALF, (h + 1) * HALF, e_part, early[:, early_own_at(t, h) : early_own_at(t, h) + HALF])
 
         gather_ring(0)
         gather_ring(1)
         for k in range(PIECES):
-            place_early(0, 2 * k)
-            gather_ring(2 * k + 2)
-            place_early(1, 2 * k)
-            gather_bags_piece(2 * k)
-            place_early(0, 2 * k + 1)
-            gather_bags_piece(2 * k + 1)
-            place_early(1, 2 * k + 1)
-            gather_ring(2 * k + 3)
+            for t in range(2):
+                place_early(t, 2 * k)
+                gather_bags_piece(2 * k + t)
+            for t in range(2):
+                place_early(t, 2 * k + 1)
+                gather_ring(2 * k + 2 + t)
             if k == PIECES // 2 - 1:
-                finish_e((2,), ds_late, scale_sums((2,), "scaled2", (6,)), (7,))
-        finish_e((3,), ds_late, scale_sums((3,), "scaled3", (7,)), (6,))
+                make_late_e(2, ds_late, "scaled2", (6, 6, 6, 6, 7))
+        make_late_e(3, ds_late, "scaled3", (6, 6, 6, 7, 2))
         store(0)
         store(1)
 
@@ -288,7 +308,7 @@ def tile_attend_gfm_bi_kernel(tc, vT, W, dz, gy, offs, boffs, soffs, out):
             t, k = LATE_ORDER[q]
             place(t, k * PIECE, (k + n) * PIECE, e_part, late_at(q, n))
 
-        early_end = early[:, EARLY_DS + 2 * C - PIECE :]
+        early_end = early[:, EARLY_DS + 2 * C :]
         place_late(0, ring_slot(16))
         gather_e(early_end, 2, 2 * PIECE, 4 * PIECE)
         place_late(1, ring_slot(17))
@@ -296,9 +316,9 @@ def tile_attend_gfm_bi_kernel(tc, vT, W, dz, gy, offs, boffs, soffs, out):
         place_late(2, early_end[:, :PIECE])
         gather_e(late_at(1), 2, 6 * PIECE, 7 * PIECE, 2)
         gather_e(ring_slot(17), 3, 0, PIECE)
+        gather_e(early[:, :PIECE], 2, 7 * PIECE, C, 2)
         place_late(3, late_at(1))
-        gather_e(late_at(2), 2, 7 * PIECE, C)
-        sources = [ring_slot(17), early_end[:, PIECE:], late_at(3), late_at(-1), late_at(4), late_at(0), late_at(5), late_at(2)]
+        sources = [ring_slot(17), early_end[:, PIECE:], late_at(3), late_at(-1), late_at(4), late_at(0), late_at(5), early[:, :PIECE]]
         for q in range(4, 12):
             place_late(q, sources[q - 4])
             if q < 11:

@@ -32,7 +32,9 @@ HALF = PIECE // 2
 PIECES = C // PIECE
 FIRST_BAGS = 512
 EARLY_DS = X_BLOCKS * 2 * P
-LATE_ORDER = ((2, 0), (2, 1), (2, 2), (2, 6), (3, 0), (2, 3), (3, 1), (2, 4), (3, 2), (2, 5), (3, 3), (2, 7), (3, 4), (3, 5), (3, 6), (3, 7))
+ALONE = 192
+ROUNDS = (C - 2 * ALONE) // HALF
+WOVEN = (5, 3, 4, 6, 7)
 JOINT_COLS = 3 * T // 4
 
 
@@ -118,8 +120,8 @@ def tile_attend_gfm_bi_kernel(tc, vT, W, dz, gy, offs, boffs, soffs, out):
                 turn(bank[:, b, :], [neg_gy_c_col[:, 4 * h + b : 4 * h + b + 1].to_broadcast([P, P])])
             nc.scalar.copy(neg_gy_c[:, h * BANK : (h + 1) * BANK], bank[:].rearrange("p b c -> p (b c)"))
 
-        late = keep.tile([P, PIECE + 2 * C], F32, name="late")
-        stairs = [keep.tile([P, PIECES * HALF + PIECE], F32, name="stairs%d" % t) for t in range(2)]
+        late = keep.tile([P, 2 * C], F32, name="late")
+        stairs = [keep.tile([P, (PIECES + 1) * HALF + PIECE], F32, name="stairs%d" % t) for t in range(2)]
         by_sample = [keep.tile([P, C], F32, name="by_sample0")[:], keep.tile([P, FIRST_BAGS], F32, name="by_sample1")[:]]
 
         def picked_at(t):
@@ -190,18 +192,21 @@ def tile_attend_gfm_bi_kernel(tc, vT, W, dz, gy, offs, boffs, soffs, out):
             turn_back(back, scale_sums(blocks_of(by_sample[t]), room, banks[:-1]), False)
             copy_e(t, back)
 
-        def make_late_own(g, banks):
-            group = LATE_ORDER[4 * g : 4 * g + 4]
-            turned = bank_tile(banks[0], [P, 4, P])
+        def make_late_own(g, group, at, woven):
+            turned = bank_tile(5 - g % 2, [P, 4, P])
             scaled = keep.tile([P, 4, P], F32, name="scaled_own", tag="scaled_own%d" % (g % 2))
             for n, (t, k) in enumerate(group):
                 turn(turned[:, n, :], [picked[:, picked_at(t) + k * P : picked_at(t) + (k + 1) * P]])
             for n, (t, k) in enumerate(group):
                 nc.scalar.activation(scaled[:, n, :], turned[:, n, :], COPY, scale=neg_gy_c_col[:, k : k + 1])
-            back = bank_tile(banks[1], [P, 4, P])
-            for n in range(4):
-                turn(back[:, n, :], [scaled[:, n, :]])
-            nc.scalar.copy(late[:, PIECE + g * BANK : PIECE + (g + 1) * BANK], back[:].rearrange("p b c -> p (b c)"))
+            back = bank_tile(g % 2, [P, 4 * P])
+            for n in range(len(group)):
+                turn(back[:, block(n)], [scaled[:, n, :]])
+            dst, src = late[:, at : at + len(group) * P], back[:, : len(group) * P]
+            if woven:
+                dst = dst.rearrange("p (m h u c) -> p m h u c", h=2, u=2, c=HALF)
+                src = src.rearrange("p (m u h c) -> p m h u c", h=2, u=2, c=HALF)
+            nc.scalar.copy(dst, src)
 
         w_codes = keep.tile([P, D], U32, name="w_codes", align_bytes=64)
         w_scales = keep.tile([P, D], U8, name="w_scales", align_bytes=64)
@@ -268,19 +273,25 @@ def tile_attend_gfm_bi_kernel(tc, vT, W, dz, gy, offs, boffs, soffs, out):
             placed.append(shared.tile([P, T], F32, name="placed%d" % (2 + u), offset=4 * T * u))
             nc.gpsimd.memset(placed[2 + u][:], 0.0)
         ds_late = copy_dense_gradient(1, ds_sums, keep.tile([P, X_BLOCKS, 2 * P], F32, name="ds_late", tag="scaled1", align_bytes=64))
-        for g in range(4):
-            make_late_own(g, (5 - g % 2, g % 2))
+        lead = 2 * ALONE // P
+        make_late_own(0, [(2, k) for k in range(lead)], 0, False)
+        for g, m in enumerate(range(0, len(WOVEN), 2)):
+            group = [pair for n in range(m, min(m + 2, len(WOVEN))) for pair in ((3, n), (2, WOVEN[n]))]
+            make_late_own(1 + g, group, 2 * ALONE + 2 * m * P, True)
+        make_late_own(4, [(3, k) for k in range(len(WOVEN), PIECES)], 2 * C - 2 * ALONE, False)
 
         def ring_slot(i):
             k, t = divmod(i, 2)
-            return stairs[t][:, (PIECES - k) * HALF : (PIECES - k) * HALF + PIECE]
+            if k == PIECES:
+                return stairs[t][:, :ALONE]
+            return stairs[t][:, (PIECES + 1 - k) * HALF : (PIECES + 1 - k) * HALF + PIECE]
 
         def gather_ring(i):
             k, t = divmod(i, 2)
             if k < PIECES:
                 gather_e(ring_slot(i), t, k * PIECE, (k + 1) * PIECE, 2 if i == 0 else 1)
             else:
-                gather_e(ring_slot(i), 2, t * PIECE, (t + 1) * PIECE)
+                gather_e(ring_slot(i), 2, t * ALONE, (t + 1) * ALONE)
 
         def place_early(t, h):
             e_part = ring_slot(h // 2 * 2 + t)[:, h % 2 * HALF : (h % 2 + 1) * HALF]
@@ -301,28 +312,35 @@ def tile_attend_gfm_bi_kernel(tc, vT, W, dz, gy, offs, boffs, soffs, out):
         store(0)
         store(1)
 
-        def late_at(q, n=1):
-            return late[:, (q + 1) * PIECE : (q + 1 + n) * PIECE]
-
-        def place_late(q, e_part, n=1):
-            t, k = LATE_ORDER[q]
-            place(t, k * PIECE, (k + n) * PIECE, e_part, late_at(q, n))
-
         early_end = early[:, EARLY_DS + 2 * C :]
-        place_late(0, ring_slot(16))
-        gather_e(early_end, 2, 2 * PIECE, 4 * PIECE)
-        place_late(1, ring_slot(17))
-        gather_e(late_at(-1, 2), 2, 4 * PIECE, 6 * PIECE)
-        place_late(2, early_end[:, :PIECE])
-        gather_e(late_at(1), 2, 6 * PIECE, 7 * PIECE, 2)
-        gather_e(ring_slot(17), 3, 0, PIECE)
-        gather_e(early[:, :PIECE], 2, 7 * PIECE, C, 2)
-        place_late(3, late_at(1))
-        sources = [ring_slot(17), early_end[:, PIECE:], late_at(3), late_at(-1), late_at(4), late_at(0), late_at(5), early[:, :PIECE]]
-        for q in range(4, 12):
-            place_late(q, sources[q - 4])
-            if q < 11:
-                gather_e(late_at(q - 1), 3, (q - 3) * PIECE, (q - 2) * PIECE)
+        held_lo = WOVEN[0] * P
+        place(2, 0, ALONE, ring_slot(16), late[:, :ALONE])
+        gather_e(early_end, 2, 2 * ALONE, held_lo)
+        place(2, ALONE, 2 * ALONE, ring_slot(17), late[:, ALONE : 2 * ALONE])
+        gather_e(late[:, :PIECE], 3, 0, PIECE)
+        gather_e(ring_slot(16)[:, :PIECE], 2, held_lo, held_lo + PIECE, 2)
+
+        def cell(s):
+            return late[:, 2 * ALONE + s * HALF : 2 * ALONE + (s + 1) * HALF]
+
+        where = {}
+        for h in range(2):
+            where[3, h * HALF] = late[:, h * HALF : (h + 1) * HALF]
+            where[2, held_lo + h * HALF] = ring_slot(16)[:, h * HALF : (h + 1) * HALF]
+        for lo in range(2 * ALONE, held_lo, HALF):
+            where[2, lo] = early_end[:, lo - 2 * ALONE : lo - 2 * ALONE + HALF]
+        todo = {2: list(range(held_lo + PIECE, C, HALF)), 3: list(range(PIECE, C, HALF))}
+        for s in range(2 * ROUNDS):
+            r, t = s // 2, 3 - s % 2
+            lo = r * HALF if t == 3 else WOVEN[r // 2] * P + r % 2 * HALF
+            place(t, lo, lo + HALF, where[t, lo], cell(s))
+            u = 2 if t == 3 and s > 0 and todo[2] else 3
+            if todo[u]:
+                lo = todo[u].pop(0)
+                where[u, lo] = cell(s - 2)
+                gather_e(cell(s - 2), u, lo, lo + HALF)
         store(2)
-        place_late(12, late_at(6, 4), 4)
+        tail = ROUNDS * HALF
+        first = 2 * ROUNDS - 4 - (C - tail) // HALF
+        place(3, tail, C, late[:, 2 * ALONE + first * HALF : 2 * ALONE + first * HALF + C - tail], late[:, 2 * C - 2 * ALONE :])
         store(3)

@@ -26,7 +26,7 @@ X_BLOCKS = X // P
 C_BLOCKS = C // P
 WINDOW = 1376
 GY_ROW = P - 1
-SCALAR_COLS = 384
+SCALAR_COLS = 352
 PIECE = 128
 HALF = PIECE // 2
 PIECES = C // PIECE
@@ -125,7 +125,7 @@ def tile_attend_gfm_bi_kernel(tc, vT, W, dz, gy, offs, boffs, soffs, out):
         by_sample = [keep.tile([P, C], F32, name="by_sample0")[:], keep.tile([P, FIRST_BAGS], F32, name="by_sample1")[:]]
 
         def picked_at(t):
-            return (2, 3, 1, 0)[t] * C
+            return (D_TILES - 1 - t) * C
 
         def entries(lo, hi):
             return slice(lo // STRIPE, hi // STRIPE)
@@ -134,13 +134,13 @@ def tile_attend_gfm_bi_kernel(tc, vT, W, dz, gy, offs, boffs, soffs, out):
             nc.vector.tensor_copy(picked[:, picked_at(t) : picked_at(t) + C], tables[t].indirect(idx_list[:]))
 
         def early_own_at(t, h):
-            return EARLY_DS + (2 * (h // 2 + 1) + t) * PIECE + h % 2 * HALF
+            return EARLY_DS + (2 * (h // 2 + 1) + 1 - t) * PIECE + h % 2 * HALF
 
         def make_early_own():
-            lo = early_own_at(0, 0)
+            lo = early_own_at(1, 0)
             nc.gpsimd.tensor_tensor(
                 early[:, lo : lo + 2 * C].rearrange("p (k u c) -> p u k c", u=2, c=PIECE),
-                picked[:, picked_at(0) : picked_at(0) + 2 * C].rearrange("p (u k c) -> p u k c", u=2, c=PIECE),
+                picked[:, picked_at(1) : picked_at(1) + 2 * C].rearrange("p (u k c) -> p u k c", u=2, c=PIECE),
                 neg_gy_c[:].rearrange("p (u k c) -> p u k c", u=1, c=PIECE).to_broadcast([P, 2, PIECES, PIECE]),
                 MULT,
             )
@@ -175,10 +175,11 @@ def tile_attend_gfm_bi_kernel(tc, vT, W, dz, gy, offs, boffs, soffs, out):
 
         def turn_back(back, parts, opens):
             for b, part in enumerate(parts):
-                nc.tensor.matmul(back[:, b, :], part, identity[:], start=(opens and b == 0), stop=(not opens and b == X_BLOCKS - 1), is_transpose=True)
+                nc.tensor.matmul(back[:, b, :], part, identity[:], start=(opens and b == 0), stop=(not opens and b == len(parts) - 1), is_transpose=True)
 
-        def copy_e(t, back):
-            nc.scalar.copy(e_all[:, t * X : (t + 1) * X], back[:].rearrange("p b c -> p (b c)"))
+        def copy_e(t, back, first=0):
+            lo = t * X + first * P
+            nc.scalar.copy(e_all[:, lo : lo + back.shape[1] * P], back[:].rearrange("p b c -> p (b c)"))
 
         def blocks_of(run):
             return [run[:, 2 * b * P : 2 * (b + 1) * P] for b in range(run.shape[1] // (2 * P))]
@@ -186,11 +187,16 @@ def tile_attend_gfm_bi_kernel(tc, vT, W, dz, gy, offs, boffs, soffs, out):
         def ds_blocks(ds_pair, t):
             return [ds_pair[:, b, block(t % 2)] for b in range(X_BLOCKS)]
 
-        def make_late_e(t, ds_pair, room, banks):
-            back = bank_tile(banks[-1], [P, X_BLOCKS, P])
-            turn_back(back, ds_blocks(ds_pair, t), True)
-            turn_back(back, scale_sums(blocks_of(by_sample[t]), room, banks[:-1]), False)
-            copy_e(t, back)
+        def make_late_e(t, bags, ds_pair, room, banks):
+            last = X_BLOCKS - 1
+            parts = ((0, last), (last, X_BLOCKS))
+            backs = [bank_tile(k, [P, hi - lo, P]) for k, (lo, hi) in zip(banks[2:], parts)]
+            for back, (lo, hi) in zip(backs, parts):
+                turn_back(back, ds_blocks(ds_pair, t)[lo:hi], True)
+            scaled = scale_sums(bags, room, [banks[0]] * last + [banks[1]])
+            for back, (lo, hi) in zip(backs, parts):
+                turn_back(back, scaled[lo:hi], False)
+                copy_e(t, back, lo)
 
         def make_late_own(g, group, at, woven):
             turned = bank_tile(5 - g % 2, [P, 4, P])
@@ -291,34 +297,34 @@ def tile_attend_gfm_bi_kernel(tc, vT, W, dz, gy, offs, boffs, soffs, out):
             if k < PIECES:
                 gather_e(ring_slot(i), t, k * PIECE, (k + 1) * PIECE, 2 if i == 0 else 1)
             else:
-                gather_e(ring_slot(i), 2, t * ALONE, (t + 1) * ALONE)
+                gather_e(ring_slot(i), 2, (1 - t) * ALONE, (2 - t) * ALONE)
 
         def place_early(t, h):
             e_part = ring_slot(h // 2 * 2 + t)[:, h % 2 * HALF : (h % 2 + 1) * HALF]
             place(t, h * HALF, (h + 1) * HALF, e_part, early[:, early_own_at(t, h) : early_own_at(t, h) + HALF])
 
-        gather_ring(0)
         gather_ring(1)
+        gather_ring(0)
         for k in range(PIECES):
-            for t in range(2):
+            for t in (1, 0):
                 place_early(t, 2 * k)
-                gather_bags_piece(2 * k + t)
-            for t in range(2):
+                gather_bags_piece(2 * k + 1 - t)
+            for t in (1, 0):
                 place_early(t, 2 * k + 1)
                 gather_ring(2 * k + 2 + t)
             if k == PIECES // 2 - 1:
-                make_late_e(2, ds_late, "scaled2", (6, 6, 6, 6, 7))
-        make_late_e(3, ds_late, "scaled3", (6, 6, 6, 7, 2))
-        store(0)
+                make_late_e(2, blocks_of(by_sample[2]), ds_late, "scaled2", (6, 3, 7, 2))
+        make_late_e(3, blocks_of(by_sample[3]), ds_late, "scaled3", (6, 7, 2, 3))
         store(1)
+        store(0)
 
         early_end = early[:, EARLY_DS + 2 * C :]
         held_lo = WOVEN[0] * P
-        place(2, 0, ALONE, ring_slot(16), late[:, :ALONE])
+        place(2, 0, ALONE, ring_slot(17), late[:, :ALONE])
         gather_e(early_end, 2, 2 * ALONE, held_lo)
-        place(2, ALONE, 2 * ALONE, ring_slot(17), late[:, ALONE : 2 * ALONE])
+        place(2, ALONE, 2 * ALONE, ring_slot(16), late[:, ALONE : 2 * ALONE])
         gather_e(late[:, :PIECE], 3, 0, PIECE)
-        gather_e(ring_slot(16)[:, :PIECE], 2, held_lo, held_lo + PIECE, 2)
+        gather_e(ring_slot(17)[:, :PIECE], 2, held_lo, held_lo + PIECE, 2)
 
         def cell(s):
             return late[:, 2 * ALONE + s * HALF : 2 * ALONE + (s + 1) * HALF]
@@ -326,7 +332,7 @@ def tile_attend_gfm_bi_kernel(tc, vT, W, dz, gy, offs, boffs, soffs, out):
         where = {}
         for h in range(2):
             where[3, h * HALF] = late[:, h * HALF : (h + 1) * HALF]
-            where[2, held_lo + h * HALF] = ring_slot(16)[:, h * HALF : (h + 1) * HALF]
+            where[2, held_lo + h * HALF] = ring_slot(17)[:, h * HALF : (h + 1) * HALF]
         for lo in range(2 * ALONE, held_lo, HALF):
             where[2, lo] = early_end[:, lo - 2 * ALONE : lo - 2 * ALONE + HALF]
         todo = {2: list(range(held_lo + PIECE, C, HALF)), 3: list(range(PIECE, C, HALF))}

@@ -198,8 +198,8 @@ def tile_attend_gfm_bi_kernel(tc, vT, W, dz, gy, offs, boffs, soffs, out):
                 turn_back(back, scaled[lo:hi], False)
                 copy_e(t, back, lo)
 
-        def make_late_own(g, group, at, woven):
-            turned = bank_tile(5 - g % 2, [P, 4, P])
+        def make_late_own(g, group, at, woven, turn_bank):
+            turned = bank_tile(turn_bank, [P, 4, P])
             scaled = keep.tile([P, 4, P], F32, name="scaled_own", tag="scaled_own%d" % (g % 2))
             for n, (t, k) in enumerate(group):
                 turn(turned[:, n, :], [picked[:, picked_at(t) + k * P : picked_at(t) + (k + 1) * P]])
@@ -254,7 +254,8 @@ def tile_attend_gfm_bi_kernel(tc, vT, W, dz, gy, offs, boffs, soffs, out):
 
         gather_table(0)
         gather_table(1)
-        gather_bags(by_sample[0], 0, 0, C)
+        for lo in range(0, C, FIRST_BAGS):
+            gather_bags(by_sample[0][:, lo : lo + FIRST_BAGS], 0, lo, lo + FIRST_BAGS)
         gather_bags(by_sample[1], 1, 0, FIRST_BAGS)
         quantise(w_raw, w_codes, w_scales, E4M3X4, "w_grouped", SCALAR_COLS)
         quantise(dz_raw, dz_codes, dz_scales, E5M2X4, "room_b", SCALAR_COLS)
@@ -280,11 +281,11 @@ def tile_attend_gfm_bi_kernel(tc, vT, W, dz, gy, offs, boffs, soffs, out):
             nc.gpsimd.memset(placed[2 + u][:], 0.0)
         ds_late = copy_dense_gradient(1, ds_sums, keep.tile([P, X_BLOCKS, 2 * P], F32, name="ds_late", tag="scaled1", align_bytes=64))
         lead = 2 * ALONE // P
-        make_late_own(0, [(2, k) for k in range(lead)], 0, False)
-        for g, m in enumerate(range(0, len(WOVEN), 2)):
+        make_late_own(0, [(2, k) for k in range(lead)], 0, False, 5)
+
+        def make_woven_own(m, turn_bank):
             group = [pair for n in range(m, min(m + 2, len(WOVEN))) for pair in ((3, n), (2, WOVEN[n]))]
-            make_late_own(1 + g, group, 2 * ALONE + 2 * m * P, True)
-        make_late_own(4, [(3, k) for k in range(len(WOVEN), PIECES)], 2 * C - 2 * ALONE, False)
+            make_late_own(1 + m // 2, group, 2 * ALONE + 2 * m * P, True, turn_bank)
 
         def ring_slot(i):
             k, t = divmod(i, 2)
@@ -314,7 +315,11 @@ def tile_attend_gfm_bi_kernel(tc, vT, W, dz, gy, offs, boffs, soffs, out):
                 gather_ring(2 * k + 2 + t)
             if k == PIECES // 2 - 1:
                 make_late_e(2, blocks_of(by_sample[2]), ds_late, "scaled2", (6, 3, 7, 2))
+                make_woven_own(0, 4)
+                make_woven_own(2, 5)
         make_late_e(3, blocks_of(by_sample[3]), ds_late, "scaled3", (6, 7, 2, 3))
+        make_woven_own(4, 3)
+        make_late_own(4, [(3, k) for k in range(len(WOVEN), PIECES)], 2 * C - 2 * ALONE, False, 3)
         store(1)
         store(0)
 

@@ -328,19 +328,18 @@ def tile_attend_gfm_bi_kernel(tc, vT, W, dz, gy, offs, boffs, soffs, out):
         place(2, 0, ALONE, ring_slot(17), late[:, :ALONE])
         gather_e(early_end, 2, 2 * ALONE, held_lo)
         place(2, ALONE, 2 * ALONE, ring_slot(16), late[:, ALONE : 2 * ALONE])
-        gather_e(late[:, :PIECE], 3, 0, PIECE)
+        gather_e(late[:, :HALF], 3, 0, HALF)
         gather_e(ring_slot(17)[:, :PIECE], 2, held_lo, held_lo + PIECE, 2)
 
         def cell(s):
             return late[:, 2 * ALONE + s * HALF : 2 * ALONE + (s + 1) * HALF]
 
-        where = {}
+        where = {(3, 0): late[:, :HALF]}
         for h in range(2):
-            where[3, h * HALF] = late[:, h * HALF : (h + 1) * HALF]
             where[2, held_lo + h * HALF] = ring_slot(17)[:, h * HALF : (h + 1) * HALF]
         for lo in range(2 * ALONE, held_lo, HALF):
             where[2, lo] = early_end[:, lo - 2 * ALONE : lo - 2 * ALONE + HALF]
-        todo = {2: list(range(held_lo + PIECE, C, HALF)), 3: list(range(PIECE, C, HALF))}
+        todo = {2: list(range(held_lo + PIECE, C, HALF)), 3: list(range(HALF, C, HALF))}
         for s in range(2 * ROUNDS):
             r, t = s // 2, 3 - s % 2
             lo = r * HALF if t == 3 else WOVEN[r // 2] * P + r % 2 * HALF
@@ -348,10 +347,10 @@ def tile_attend_gfm_bi_kernel(tc, vT, W, dz, gy, offs, boffs, soffs, out):
             u = 2 if t == 3 and s > 0 and todo[2] else 3
             if todo[u]:
                 lo = todo[u].pop(0)
-                where[u, lo] = cell(s - 2)
-                gather_e(cell(s - 2), u, lo, lo + HALF)
+                where[u, lo] = where[3, 0] if s == 1 else cell(s - 2)
+                gather_e(where[u, lo], u, lo, lo + HALF)
         store(2)
         tail = ROUNDS * HALF
-        first = 2 * ROUNDS - 4 - (C - tail) // HALF
+        first = 2 * ROUNDS - 3 - (C - tail) // HALF
         place(3, tail, C, late[:, 2 * ALONE + first * HALF : 2 * ALONE + first * HALF + C - tail], late[:, 2 * C - 2 * ALONE :])
         store(3)

@@ -1,7 +1,6 @@
 from contextlib import ExitStack
 
 import concourse.mybir as mybir
-from concourse.masks import make_identity
 
 D, M, X, C, T = 512, 512, 512, 1024, 2048
 FLOPS = 2 * M * D * X
@@ -19,338 +18,205 @@ MULT = mybir.AluOpType.mult
 
 P = 128
 PACK = 4
-BANK = 512
 STRIPE = 16
 D_TILES = D // P
-X_BLOCKS = X // P
-C_BLOCKS = C // P
-WINDOW = 1376
-GY_ROW = P - 1
-SCALAR_COLS = 352
-PIECE = 128
-HALF = PIECE // 2
-PIECES = C // PIECE
-FIRST_BAGS = 512
-EARLY_DS = X_BLOCKS * 2 * P
-ALONE = 192
-ROUNDS = (C - 2 * ALONE) // HALF
-WOVEN = (5, 3, 4, 6, 7)
-JOINT_COLS = 3 * T // 4
+GY_PIECE = 256
+GY_ON_VECTOR = 512
+DZ_SCALAR_COLS = 176
+E_PIECE = 256
+SCALAR_PIECES = ((0, 352), (352, 704), (704, 1024))
 
 
 def tile_attend_gfm_bi_kernel(tc, vT, W, dz, gy, offs, boffs, soffs, out):
     nc = tc.nc
     with ExitStack() as ctx:
         keep = ctx.enter_context(tc.tile_pool(name="keep", bufs=1))
-        shared = ctx.enter_context(tc.tile_pool(name="shared", bufs=1))
         psum = ctx.enter_context(tc.psum_pool(name="psum", bufs=1))
 
         bag_list = keep.tile([P, C // STRIPE], U16, name="bag_list")
         idx_list = keep.tile([P, C // STRIPE], U16, name="idx_list")
         slot_list = keep.tile([P, C // STRIPE], U16, name="slot_list")
         gy_win = keep.tile([P, X], F32, name="gy_win")
-        first_tables = [keep.tile([P, T], F32, name="table", tag="table%d" % t) for t in range(2)]
-        last_tables = shared.tile([P, 2, T], F32, name="last_tables", offset=0)
-        tables = [first_tables[0][:], first_tables[1][:], last_tables[:, 0, :], last_tables[:, 1, :]]
-        w_raw = keep.tile([P, PACK, D], F32, name="w_raw", tag="room_w", align_bytes=64)
-        dz_raw = keep.tile([P, PACK, X], F32, name="dz_raw", tag="room_a", align_bytes=64)
+        tables = [keep.tile([P, T], F32, name="table%d" % t) for t in range(D_TILES)]
+        w_raw = [keep.tile([P, PACK, D // 2], F32, name="w_raw%d" % h) for h in range(2)]
+        dz_raw = keep.tile([P, PACK, X], F32, name="dz_raw")
+        w_rows = W.rearrange("(p j) d -> p j d", j=PACK)
 
-        nc.scalar.dma_start(gy_win[GY_ROW:, :], gy[0:1, :])
         nc.sync.dma_start(bag_list[:], boffs)
+        nc.sync.dma_start(gy_win[:], gy)
         nc.sync.dma_start(idx_list[:], offs)
-        nc.sync.dma_start(tables[0], vT[0:P, :])
-        nc.sync.dma_start(tables[1], vT[P : 2 * P, :])
+        nc.sync.dma_start(tables[0][:], vT[0:P, :])
         nc.sync.dma_start(slot_list[:], soffs)
-        nc.sync.dma_start(w_raw[:], W.rearrange("(p j) d -> p j d", j=PACK))
         nc.sync.dma_start(dz_raw[:], dz.rearrange("(p j) x -> p j x", j=PACK))
-        last_rows = vT[2 * P :, :].rearrange("(u p) n -> p u n", p=P)
-        nc.sync.dma_start(last_tables[:, :, :JOINT_COLS], last_rows[:, :, :JOINT_COLS])
-        for u in range(2):
-            nc.sync.dma_start(last_tables[:, u, JOINT_COLS:], last_rows[:, u, JOINT_COLS:])
+        nc.sync.dma_start(w_raw[0][:], w_rows[:, :, : D // 2])
+        nc.sync.dma_start(tables[1][:], vT[P : 2 * P, :])
+        nc.sync.dma_start(w_raw[1][:], w_rows[:, :, D // 2 :])
+        nc.sync.dma_start(tables[2][:], vT[2 * P : 3 * P, :])
+        nc.sync.dma_start(tables[3][:], vT[3 * P :, :])
 
-        picked = keep.tile([P, (D_TILES - 1) * C + WINDOW], F32, name="picked")
-        e_all = keep.tile([P, D_TILES * X], F32, name="e_all")
-        identity = keep.tile([P, P], F32, name="identity")
+        placed = [keep.tile([P, T], F32, name="placed%d" % t) for t in range(D_TILES)]
+        minus_one = keep.tile([P, GY_PIECE], F32, name="minus_one")
+        nc.vector.memset(minus_one[:], -1.0)
+        nc.vector.memset(placed[0][:], 0.0)
+        for t in (1, 3, 2):
+            nc.gpsimd.memset(placed[t][:], 0.0)
 
-        placed = [keep.tile([P, T], F32, name="placed%d" % u) for u in range(2)]
-
-        nc.gpsimd.memset(gy_win[:GY_ROW, :], 0.0)
-        make_identity(nc, identity[:])
-        nc.gpsimd.memset(picked[:, D_TILES * C :], 0.0)
-        for window in placed:
-            nc.gpsimd.memset(window[:], 0.0)
-
-        def gather(dst, tile, at, entries):
-            room = min(tile.shape[1] - at, WINDOW)
-            piece = min(C, (3 * room // 4) // (2 * STRIPE) * (2 * STRIPE))
-            pieces = -(-C // piece)
-            piece = -(-C // (pieces * 2 * STRIPE)) * 2 * STRIPE
-            for lo in range(0, C, piece):
-                hi = min(C, lo + piece)
-                nc.vector.tensor_copy(dst[:, lo:hi], tile[:, at : at + room].indirect(entries[:, lo // STRIPE : hi // STRIPE]))
-
-        def turn(dst, parts):
-            for n, part in enumerate(parts):
-                nc.tensor.matmul(dst, part, identity[:], start=(n == 0), stop=(n == len(parts) - 1), is_transpose=True)
-
-        def block(b):
-            return slice(b * P, (b + 1) * P)
-
-        def bank_tile(k, shape):
-            return psum.tile(shape, F32, name="bank", tag="bank%d" % k)
-
-        gy_c = keep.tile([P, C], F32, name="gy_c")
-        gather(gy_c, gy_win, 0, bag_list)
-        gy_col = keep.tile([P, X_BLOCKS], F32, name="gy_col")
-        neg_gy_c_col = keep.tile([P, C_BLOCKS], F32, name="neg_gy_c_col")
-        bank = bank_tile(4, [P, X_BLOCKS, P])
-        for b in range(X_BLOCKS):
-            turn(bank[:, b, :], [gy_win[:, block(b)]])
-        nc.scalar.copy(gy_col[:], bank[:, :, GY_ROW])
-        for h in range(2):
-            bank = bank_tile(5 + h, [P, 4, P])
-            for b in range(4):
-                turn(bank[:, b, :], [gy_c[:, block(4 * h + b)]])
-            nc.scalar.activation(neg_gy_c_col[:, 4 * h : 4 * h + 4], bank[:, :, GY_ROW], COPY, scale=-1.0)
-
+        picked = [keep.tile([P, C], F32, name="picked%d" % t) for t in range(D_TILES)]
+        by_sample = [keep.tile([P, C], F32, name="by_sample%d" % t) for t in range(D_TILES)]
+        sums = {t: keep.tile([P, X], F32, name="sums%d" % t) for t in (0, 1)}
+        scaled = [keep.tile([P, X], F32, name="scaled%d" % t) for t in range(D_TILES)]
+        e = [keep.tile([P, X], F32, name="e%d" % t, align_bytes=64) for t in range(D_TILES)]
+        dv = [keep.tile([P, C], F32, name="dv%d" % t) for t in range(1)]
         neg_gy_c = keep.tile([P, C], F32, name="neg_gy_c")
-        for h in range(2):
-            bank = bank_tile(h, [P, 4, P])
-            for b in range(4):
-                turn(bank[:, b, :], [neg_gy_c_col[:, 4 * h + b : 4 * h + b + 1].to_broadcast([P, P])])
-            nc.scalar.copy(neg_gy_c[:, h * BANK : (h + 1) * BANK], bank[:].rearrange("p b c -> p (b c)"))
 
-        late = keep.tile([P, 2 * C], F32, name="late")
-        stairs = [keep.tile([P, (PIECES + 1) * HALF + PIECE], F32, name="stairs%d" % t) for t in range(2)]
-        by_sample = [keep.tile([P, C], F32, name="by_sample0")[:], keep.tile([P, FIRST_BAGS], F32, name="by_sample1")[:]]
+        def entries(listed, lo, hi):
+            return listed[:, lo // STRIPE : hi // STRIPE]
 
-        def picked_at(t):
-            return (D_TILES - 1 - t) * C
+        def gather(engine, dst, window, listed, lo, hi):
+            src = window[:].indirect(entries(listed, lo, hi))
+            if engine == "vector":
+                nc.vector.tensor_copy(dst[:, lo:hi], src)
+            else:
+                nc.scalar.activation(dst[:, lo:hi], src, COPY)
 
-        def entries(lo, hi):
-            return slice(lo // STRIPE, hi // STRIPE)
+        def gather_table(engine, t, lo=0, hi=C):
+            gather(engine, picked[t], tables[t], idx_list, lo, hi)
 
-        def gather_table(t):
-            nc.vector.tensor_copy(picked[:, picked_at(t) : picked_at(t) + C], tables[t].indirect(idx_list[:]))
+        def gather_bags(engine, t, lo, hi):
+            gather(engine, by_sample[t], picked[t], slot_list, lo, hi)
 
-        def early_own_at(t, h):
-            return EARLY_DS + (2 * (h // 2 + 1) + 1 - t) * PIECE + h % 2 * HALF
+        def add_pairs(engine, t):
+            pairs = by_sample[t][:].rearrange("p (x j) -> p j x", j=2)
+            engine.tensor_tensor(sums[t][:], pairs[:, 0, :], pairs[:, 1, :], ADD)
 
-        def make_early_own():
-            lo = early_own_at(1, 0)
-            nc.gpsimd.tensor_tensor(
-                early[:, lo : lo + 2 * C].rearrange("p (k u c) -> p u k c", u=2, c=PIECE),
-                picked[:, picked_at(1) : picked_at(1) + 2 * C].rearrange("p (u k c) -> p u k c", u=2, c=PIECE),
-                neg_gy_c[:].rearrange("p (u k c) -> p u k c", u=1, c=PIECE).to_broadcast([P, 2, PIECES, PIECE]),
-                MULT,
+        def scale_sums(engine, t):
+            engine.tensor_tensor(scaled[t][:], sums[t][:], gy_win[:], MULT)
+
+        def make_own(dst, t, lo, hi):
+            nc.gpsimd.tensor_tensor(dst, picked[t][:, lo:hi], neg_gy_c[:, lo:hi], MULT)
+
+        def interleaved(grouped, raw, cols):
+            return (
+                grouped[:, cols, :].rearrange("p (c i) j -> p c j i", i=4),
+                raw[:, :, cols].rearrange("p j (c i) -> p c j i", i=4),
             )
 
-        def gather_bags(dst, t, lo, hi):
-            at = picked_at(t)
-            nc.vector.tensor_copy(dst, picked[:, at : at + WINDOW].indirect(slot_list[:, entries(lo, hi)]))
+        def quantise(grouped, name, fmt):
+            width = grouped.shape[1]
+            codes = keep.tile([P, width], U32, name=name + "_codes", align_bytes=64)
+            scales = keep.tile([P, width], U8, name=name + "_scales", align_bytes=64)
+            nc.vector.quantize_mx(out=codes[:].bitcast(fmt), scales=scales[:], in_=grouped[:].rearrange("p w j -> p (w j)"))
+            return codes, scales
 
-        def gather_bags_piece(i):
-            u, k = divmod(i, PIECES)
-            at = picked_at(2 + u)
-            nc.vector.tensor_copy(by_sample[2 + u][:, block(k)], picked[:, at : at + C].indirect(slot_list[:, entries(k * PIECE, (k + 1) * PIECE)]))
+        def dense_gradient(t, w_planes, dz_planes):
+            acc = psum.tile([P, X], F32, name="ds%d" % t)
+            cols = slice(t % 2 * P, (t % 2 + 1) * P)
+            nc.tensor.matmul_mx(
+                out=acc[:],
+                lhsT=w_planes[0][:, cols].bitcast(E4M3X4),
+                lhsT_scale=w_planes[1][:, cols],
+                rhs=dz_planes[0][:].bitcast(E5M2X4),
+                rhs_scale=dz_planes[1][:],
+                start=True,
+                stop=True,
+            )
+            return acc
 
-        def gather_e(dst, t, lo, hi, tiles=1):
-            nc.vector.tensor_copy(dst, e_all[:, t * X : (t + tiles) * X].indirect(bag_list[:, entries(lo, hi)]))
+        def make_e(t, ds):
+            nc.vector.tensor_tensor(e[t][:], ds[:], scaled[t][:], ADD)
 
-        def place(t, lo, hi, e_part, own_part):
-            nc.vector.tensor_tensor(placed[t][:].indirect(idx_list[:, entries(lo, hi)]), e_part, own_part, ADD)
+        def add_own(dst, t, lo, hi, own_part):
+            nc.vector.tensor_tensor(dst, e[t][:].indirect(entries(bag_list, lo, hi)), own_part, ADD)
+
+        def make_dv(dst, t, first, last):
+            for lo, hi in SCALAR_PIECES:
+                if first <= lo < last:
+                    add_own(dst[:, lo - first : hi - first], t, lo, hi, own[t][:, lo:hi])
+
+        def place_on_scalar(t, src, first, pieces):
+            for lo, hi in pieces:
+                nc.scalar.activation(placed[t][:].indirect(entries(idx_list, lo, hi)), src[:, lo - first : hi - first], COPY)
 
         def store(t):
             nc.sync.dma_start(out[t * P : (t + 1) * P, :], placed[t][:])
 
-        def scale_sums(sources, room, banks):
-            scaled = keep.tile([P, X_BLOCKS, P], F32, name="scaled", tag=room, align_bytes=64)
-            turned = {k: bank_tile(k, [P, X_BLOCKS, P]) for k in sorted(set(banks))}
-            for b in range(X_BLOCKS):
-                pairs = sources[b].rearrange("p (x j) -> p j x", j=2)
-                turn(turned[banks[b]][:, b, :], [pairs[:, j, :] for j in range(2)])
-            for b in range(X_BLOCKS):
-                nc.scalar.activation(scaled[:, b, :], turned[banks[b]][:, b, :], COPY, scale=gy_col[:, b : b + 1])
-            return [scaled[:, b, :] for b in range(X_BLOCKS)]
-
-        def turn_back(back, parts, opens):
-            for b, part in enumerate(parts):
-                nc.tensor.matmul(back[:, b, :], part, identity[:], start=(opens and b == 0), stop=(not opens and b == len(parts) - 1), is_transpose=True)
-
-        def copy_e(t, back, first=0):
-            lo = t * X + first * P
-            nc.scalar.copy(e_all[:, lo : lo + back.shape[1] * P], back[:].rearrange("p b c -> p (b c)"))
-
-        def blocks_of(run):
-            return [run[:, 2 * b * P : 2 * (b + 1) * P] for b in range(run.shape[1] // (2 * P))]
-
-        def ds_blocks(ds_pair, t):
-            return [ds_pair[:, b, block(t % 2)] for b in range(X_BLOCKS)]
-
-        def make_late_e(t, bags, ds_pair, room, banks):
-            last = X_BLOCKS - 1
-            parts = ((0, last), (last, X_BLOCKS))
-            backs = [bank_tile(k, [P, hi - lo, P]) for k, (lo, hi) in zip(banks[2:], parts)]
-            for back, (lo, hi) in zip(backs, parts):
-                turn_back(back, ds_blocks(ds_pair, t)[lo:hi], True)
-            scaled = scale_sums(bags, room, [banks[0]] * last + [banks[1]])
-            for back, (lo, hi) in zip(backs, parts):
-                turn_back(back, scaled[lo:hi], False)
-                copy_e(t, back, lo)
-
-        def make_late_own(g, group, at, woven, turn_bank):
-            turned = bank_tile(turn_bank, [P, 4, P])
-            scaled = keep.tile([P, 4, P], F32, name="scaled_own", tag="scaled_own%d" % (g % 2))
-            for n, (t, k) in enumerate(group):
-                turn(turned[:, n, :], [picked[:, picked_at(t) + k * P : picked_at(t) + (k + 1) * P]])
-            for n, (t, k) in enumerate(group):
-                nc.scalar.activation(scaled[:, n, :], turned[:, n, :], COPY, scale=neg_gy_c_col[:, k : k + 1])
-            back = bank_tile(g % 2, [P, 4 * P])
-            for n in range(len(group)):
-                turn(back[:, block(n)], [scaled[:, n, :]])
-            dst, src = late[:, at : at + len(group) * P], back[:, : len(group) * P]
-            if woven:
-                dst = dst.rearrange("p (m h u c) -> p m h u c", h=2, u=2, c=HALF)
-                src = src.rearrange("p (m u h c) -> p m h u c", h=2, u=2, c=HALF)
-            nc.scalar.copy(dst, src)
-
-        w_codes = keep.tile([P, D], U32, name="w_codes", align_bytes=64)
-        w_scales = keep.tile([P, D], U8, name="w_scales", align_bytes=64)
-        dz_codes = keep.tile([P, X], U32, name="dz_codes", align_bytes=64)
-        dz_scales = keep.tile([P, X], U8, name="dz_scales", align_bytes=64)
-
-        def quantise(raw, codes, scales, fmt, room, scalar_cols):
-            grouped = keep.tile([P, BANK, PACK], BF16, name="grouped", tag=room, align_bytes=64)
-
-            def interleaved(cols):
-                return (
-                    grouped[:, cols, :].rearrange("p (c i) j -> p c j i", i=4),
-                    raw[:, :, cols].rearrange("p j (c i) -> p c j i", i=4),
-                )
-
-            nc.scalar.copy(*interleaved(slice(0, scalar_cols)))
-            if scalar_cols < BANK:
-                nc.gpsimd.tensor_scalar(*interleaved(slice(scalar_cols, BANK)), 1.0, 0.0, MULT, ADD)
-            nc.vector.quantize_mx(out=codes[:].bitcast(fmt), scales=scales[:], in_=grouped[:].rearrange("p w j -> p (w j)"))
-
-        def dense_gradient(banks):
-            sums = [bank_tile(k, [P, D]) for k in banks]
-            for b, acc in enumerate(sums):
-                nc.tensor.matmul_mx(
-                    out=acc[:],
-                    lhsT=dz_codes[:, block(b)].bitcast(E5M2X4),
-                    lhsT_scale=dz_scales[:, block(b)],
-                    rhs=w_codes[:].bitcast(E4M3X4),
-                    rhs_scale=w_scales[:],
-                    start=True,
-                    stop=True,
-                )
-            return sums
-
-        def copy_dense_gradient(pair, sums, ds_pair):
-            for b, acc in enumerate(sums):
-                nc.scalar.copy(ds_pair[:, b, :], acc[:, 2 * pair * P : 2 * (pair + 1) * P])
-            return ds_pair
-
-        gather_table(0)
-        gather_table(1)
-        for lo in range(0, C, FIRST_BAGS):
-            gather_bags(by_sample[0][:, lo : lo + FIRST_BAGS], 0, lo, lo + FIRST_BAGS)
-        gather_bags(by_sample[1], 1, 0, FIRST_BAGS)
-        quantise(w_raw, w_codes, w_scales, E4M3X4, "w_grouped", SCALAR_COLS)
-        quantise(dz_raw, dz_codes, dz_scales, E5M2X4, "room_b", SCALAR_COLS)
-        early = keep.tile([P, EARLY_DS + 2 * C + 2 * PIECE], F32, name="early", tag="room_b", align_bytes=64)
-        by_sample += [early[:, EARLY_DS + u * C : EARLY_DS + (u + 1) * C] for u in range(2)]
-        make_early_own()
-        last_bags = keep.tile([P, C - FIRST_BAGS], F32, name="last_bags", tag="room_a", align_bytes=64)
-        gather_bags(last_bags[:], 1, FIRST_BAGS, C)
-        backs = [bank_tile(4 + t, [P, X_BLOCKS, P]) for t in range(2)]
-        turn_back(backs[0], scale_sums(blocks_of(by_sample[0]), "room_w", (0, 0, 0, 0)), True)
-        ds_sums = dense_gradient((6, 7, 2, 3))
-        ds_early = copy_dense_gradient(0, ds_sums, early[:, :EARLY_DS].rearrange("p (b c) -> p b c", b=X_BLOCKS))
-        scaled = scale_sums(blocks_of(by_sample[1]) + blocks_of(last_bags[:]), "scaled1", (1, 1, 0, 0))
-        turn_back(backs[0], ds_blocks(ds_early, 0), False)
-        copy_e(0, backs[0])
-        turn_back(backs[1], ds_blocks(ds_early, 1), True)
-        turn_back(backs[1], scaled, False)
-        copy_e(1, backs[1])
-        gather_table(2)
-        gather_table(3)
-        for u in range(2):
-            placed.append(shared.tile([P, T], F32, name="placed%d" % (2 + u), offset=4 * T * u))
-            nc.gpsimd.memset(placed[2 + u][:], 0.0)
-        ds_late = copy_dense_gradient(1, ds_sums, keep.tile([P, X_BLOCKS, 2 * P], F32, name="ds_late", tag="scaled1", align_bytes=64))
-        lead = 2 * ALONE // P
-        make_late_own(0, [(2, k) for k in range(lead)], 0, False, 5)
-
-        def make_woven_own(m, turn_bank):
-            group = [pair for n in range(m, min(m + 2, len(WOVEN))) for pair in ((3, n), (2, WOVEN[n]))]
-            make_late_own(1 + m // 2, group, 2 * ALONE + 2 * m * P, True, turn_bank)
-
-        def ring_slot(i):
-            k, t = divmod(i, 2)
-            if k == PIECES:
-                return stairs[t][:, :ALONE]
-            return stairs[t][:, (PIECES + 1 - k) * HALF : (PIECES + 1 - k) * HALF + PIECE]
-
-        def gather_ring(i):
-            k, t = divmod(i, 2)
-            if k < PIECES:
-                gather_e(ring_slot(i), t, k * PIECE, (k + 1) * PIECE, 2 if i == 0 else 1)
+        half = C // 2
+        gy_twice = keep.tile([P, X // 2, 2], F32, name="gy_twice")
+        nc.scalar.copy(gy_twice[:], gy_win[:, : X // 2].unsqueeze(2).to_broadcast([P, X // 2, 2]))
+        for lo in range(0, C, GY_PIECE):
+            dst, src = neg_gy_c[:, lo : lo + GY_PIECE], gy_win[:].indirect(entries(bag_list, lo, lo + GY_PIECE))
+            if lo < GY_ON_VECTOR:
+                nc.vector.tensor_tensor(dst, src, minus_one[:], MULT)
             else:
-                gather_e(ring_slot(i), 2, (1 - t) * ALONE, (2 - t) * ALONE)
+                nc.scalar.activation(dst, src, COPY, scale=-1.0)
 
-        def place_early(t, h):
-            e_part = ring_slot(h // 2 * 2 + t)[:, h % 2 * HALF : (h % 2 + 1) * HALF]
-            place(t, h * HALF, (h + 1) * HALF, e_part, early[:, early_own_at(t, h) : early_own_at(t, h) + HALF])
+        gather_table("vector", 0, 0, half)
+        gather_table("scalar", 0, half, C)
+        nc.vector.tensor_tensor(by_sample[0][:, :half], picked[0][:].indirect(entries(slot_list, 0, half)), gy_twice[:].rearrange("p x j -> p (x j)"), MULT)
+        gather_bags("scalar", 0, half, C)
+        own0_low = keep.tile([P, half], F32, name="own0_low")
+        make_own(own0_low[:], 0, 0, half)
 
-        gather_ring(1)
-        gather_ring(0)
-        for k in range(PIECES):
-            for t in (1, 0):
-                place_early(t, 2 * k)
-                gather_bags_piece(2 * k + 1 - t)
-            for t in (1, 0):
-                place_early(t, 2 * k + 1)
-                gather_ring(2 * k + 2 + t)
-            if k == PIECES // 2 - 1:
-                make_late_e(2, blocks_of(by_sample[2]), ds_late, "scaled2", (6, 3, 7, 2))
-                make_woven_own(0, 4)
-                make_woven_own(2, 5)
-        make_late_e(3, blocks_of(by_sample[3]), ds_late, "scaled3", (6, 7, 2, 3))
-        make_woven_own(4, 3)
-        make_late_own(4, [(3, k) for k in range(len(WOVEN), PIECES)], 2 * C - 2 * ALONE, False, 3)
-        store(1)
+        dz_grouped = keep.tile([P, X, PACK], BF16, name="dz_grouped", align_bytes=64)
+        nc.vector.tensor_copy(*interleaved(dz_grouped, dz_raw, slice(DZ_SCALAR_COLS, X)))
+        nc.scalar.copy(*interleaved(dz_grouped, dz_raw, slice(0, DZ_SCALAR_COLS)))
+        w_grouped = keep.tile([P, D // 2, PACK], BF16, name="w_grouped", tag="w_room", align_bytes=64)
+        nc.scalar.copy(*interleaved(w_grouped, w_raw[0], slice(0, D // 2)))
+        pairs = by_sample[0][:].rearrange("p (x j) -> p j x", j=2)
+        nc.vector.tensor_tensor(sums[0][:, X // 2 :], pairs[:, 0, X // 2 :], pairs[:, 1, X // 2 :], ADD)
+        dz_planes = quantise(dz_grouped, "dz", E5M2X4)
+        nc.vector.tensor_tensor(scaled[0][:, : X // 2], pairs[:, 0, : X // 2], pairs[:, 1, : X // 2], ADD)
+        nc.vector.tensor_tensor(scaled[0][:, X // 2 :], sums[0][:, X // 2 :], gy_win[:, X // 2 :], MULT)
+        w_planes = quantise(w_grouped, "w_low", E4M3X4)
+        ds = [dense_gradient(t, w_planes, dz_planes) for t in range(2)]
+        own0_high = keep.tile([P, half], F32, name="own0_high", tag="w_room", align_bytes=64)
+        make_own(own0_high[:], 0, half, C)
+        make_e(0, ds[0])
+        for lo in range(0, C, E_PIECE):
+            own_half = own0_low if lo < half else own0_high
+            add_own(dv[0][:, lo : lo + E_PIECE], 0, lo, lo + E_PIECE, own_half[:, lo % half : lo % half + E_PIECE])
+        nc.vector.tensor_copy(placed[0][:].indirect(idx_list[:, 0 : C // STRIPE]), dv[0][:])
         store(0)
 
-        early_end = early[:, EARLY_DS + 2 * C :]
-        held_lo = WOVEN[0] * P
-        place(2, 0, ALONE, ring_slot(17), late[:, :ALONE])
-        gather_e(early_end, 2, 2 * ALONE, held_lo)
-        place(2, ALONE, 2 * ALONE, ring_slot(16), late[:, ALONE : 2 * ALONE])
-        gather_e(late[:, :HALF], 3, 0, HALF)
-        gather_e(ring_slot(17)[:, :PIECE], 2, held_lo, held_lo + PIECE, 2)
+        own = [None] + [keep.tile([P, C], F32, name="own%d" % t) for t in range(1, D_TILES)]
+        for t in range(1, D_TILES):
+            gather_table("scalar", t)
+            for lo in (0, half):
+                gather_bags("scalar", t, lo, lo + half)
+            make_own(own[t][:], t, 0, C)
+            if t == 1:
+                add_pairs(nc.gpsimd, t)
+                scale_sums(nc.gpsimd, t)
 
-        def cell(s):
-            return late[:, 2 * ALONE + s * HALF : 2 * ALONE + (s + 1) * HALF]
-
-        where = {(3, 0): late[:, :HALF]}
-        for h in range(2):
-            where[2, held_lo + h * HALF] = ring_slot(17)[:, h * HALF : (h + 1) * HALF]
-        for lo in range(2 * ALONE, held_lo, HALF):
-            where[2, lo] = early_end[:, lo - 2 * ALONE : lo - 2 * ALONE + HALF]
-        todo = {2: list(range(held_lo + PIECE, C, HALF)), 3: list(range(HALF, C, HALF))}
-        for s in range(2 * ROUNDS):
-            r, t = s // 2, 3 - s % 2
-            lo = r * HALF if t == 3 else WOVEN[r // 2] * P + r % 2 * HALF
-            place(t, lo, lo + HALF, where[t, lo], cell(s))
-            u = 2 if t == 3 and s > 0 and todo[2] else 3
-            if todo[u]:
-                lo = todo[u].pop(0)
-                where[u, lo] = where[3, 0] if s == 1 else cell(s - 2)
-                gather_e(where[u, lo], u, lo, lo + HALF)
-        store(2)
-        tail = ROUNDS * HALF
-        first = 2 * ROUNDS - 3 - (C - tail) // HALF
-        place(3, tail, C, late[:, 2 * ALONE + first * HALF : 2 * ALONE + first * HALF + C - tail], late[:, 2 * C - 2 * ALONE :])
+        w_grouped = keep.tile([P, D // 2, PACK], BF16, name="w_grouped_high", tag="e0", align_bytes=64)
+        nc.vector.tensor_copy(*interleaved(w_grouped, w_raw[1], slice(0, D // 2)))
+        make_e(1, ds[1])
+        w_planes = quantise(w_grouped, "w_high", E4M3X4)
+        ds += [None, dense_gradient(3, w_planes, dz_planes)]
+        ds[2] = dense_gradient(2, w_planes, dz_planes)
+        held = SCALAR_PIECES[-1][0]
+        dv1 = keep.tile([P, held], F32, name="dv1", tag="table3")
+        make_dv(dv1, 1, 0, held)
+        place_on_scalar(1, dv1, 0, SCALAR_PIECES[:-1])
+        sums[3] = keep.tile([P, X], F32, name="sums3", tag="scaled1")
+        add_pairs(nc.vector, 3)
+        scale_sums(nc.vector, 3)
+        sums[2] = keep.tile([P, X], F32, name="sums2", tag="by_sample3")
+        add_pairs(nc.vector, 2)
+        make_e(3, ds[3])
+        scale_sums(nc.vector, 2)
+        e_by_slot = keep.tile([P, C], F32, name="e_by_slot")
+        for lo in range(0, C, E_PIECE):
+            gather("scalar", e_by_slot, e[3], bag_list, lo, lo + E_PIECE)
+        late = keep.tile([P, 2 * C - held], F32, name="late", tag="scaled3")
+        dv1_last, dv2 = late[:, C:], late[:, :C]
+        make_dv(dv1_last, 1, held, C)
+        place_on_scalar(1, dv1_last, held, SCALAR_PIECES[-1:])
+        store(1)
+        make_e(2, ds[2])
+        make_dv(dv2, 2, 0, C)
+        for lo in (0, half):
+            nc.vector.tensor_tensor(placed[3][:].indirect(entries(idx_list, lo, lo + half)), e_by_slot[:, lo : lo + half], own[3][:, lo : lo + half], ADD)
         store(3)
+        place_on_scalar(2, dv2, 0, SCALAR_PIECES)
+        store(2)

@@ -63,7 +63,7 @@ def tile_attend_gfm_bi_kernel(tc, vT, W, dz, gy, offs, boffs, soffs, out):
 
         picked = [keep.tile([P, C], F32, name="picked%d" % t) for t in range(D_TILES)]
         by_sample = [keep.tile([P, C], F32, name="by_sample%d" % t) for t in range(D_TILES)]
-        sums = {t: keep.tile([P, X], F32, name="sums%d" % t) for t in (0, 1)}
+        sums = {t: keep.tile([P, X], F32, name="sums%d" % t)[:] for t in (0, 1)}
         scaled = [keep.tile([P, X], F32, name="scaled%d" % t) for t in range(D_TILES)]
         e = [keep.tile([P, X], F32, name="e%d" % t, align_bytes=64) for t in range(D_TILES)]
         dv = [keep.tile([P, C], F32, name="dv%d" % t) for t in range(1)]
@@ -87,10 +87,10 @@ def tile_attend_gfm_bi_kernel(tc, vT, W, dz, gy, offs, boffs, soffs, out):
 
         def add_pairs(engine, t):
             pairs = by_sample[t][:].rearrange("p (x j) -> p j x", j=2)
-            engine.tensor_tensor(sums[t][:], pairs[:, 0, :], pairs[:, 1, :], ADD)
+            engine.tensor_tensor(sums[t], pairs[:, 0, :], pairs[:, 1, :], ADD)
 
         def scale_sums(engine, t):
-            engine.tensor_tensor(scaled[t][:], sums[t][:], gy_win[:], MULT)
+            engine.tensor_tensor(scaled[t][:], sums[t], gy_win[:], MULT)
 
         def make_own(dst, t, lo, hi):
             nc.gpsimd.tensor_tensor(dst, picked[t][:, lo:hi], neg_gy_c[:, lo:hi], MULT)
@@ -175,8 +175,6 @@ def tile_attend_gfm_bi_kernel(tc, vT, W, dz, gy, offs, boffs, soffs, out):
         for lo in range(0, C, E_PIECE):
             own_half = own0_low if lo < half else own0_high
             add_own(dv[0][:, lo : lo + E_PIECE], 0, lo, lo + E_PIECE, own_half[:, lo % half : lo % half + E_PIECE])
-        nc.vector.tensor_copy(placed[0][:].indirect(idx_list[:, 0 : C // STRIPE]), dv[0][:])
-        store(0)
 
         own = [None] + [keep.tile([P, C], F32, name="own%d" % t) for t in range(1, D_TILES)]
         for t in range(1, D_TILES):
@@ -188,35 +186,21 @@ def tile_attend_gfm_bi_kernel(tc, vT, W, dz, gy, offs, boffs, soffs, out):
                 add_pairs(nc.gpsimd, t)
                 scale_sums(nc.gpsimd, t)
 
+        place_on_scalar(0, dv[0], 0, SCALAR_PIECES)
+        store(0)
         w_grouped = keep.tile([P, D // 2, PACK], BF16, name="w_grouped_high", tag="e0", align_bytes=64)
         nc.vector.tensor_copy(*interleaved(w_grouped, w_raw[1], slice(0, D // 2)))
         make_e(1, ds[1])
         w_planes = quantise(w_grouped, "w_high", E4M3X4)
         ds += [None, dense_gradient(3, w_planes, dz_planes)]
         ds[2] = dense_gradient(2, w_planes, dz_planes)
-        held = SCALAR_PIECES[-1][0]
-        dv1 = keep.tile([P, held], F32, name="dv1", tag="table3")
-        make_dv(dv1, 1, 0, held)
-        place_on_scalar(1, dv1, 0, SCALAR_PIECES[:-1])
-        sums[3] = keep.tile([P, X], F32, name="sums3", tag="scaled1")
-        add_pairs(nc.vector, 3)
-        scale_sums(nc.vector, 3)
-        sums[2] = keep.tile([P, X], F32, name="sums2", tag="by_sample3")
-        add_pairs(nc.vector, 2)
-        make_e(3, ds[3])
-        scale_sums(nc.vector, 2)
-        e_by_slot = keep.tile([P, C], F32, name="e_by_slot")
-        for lo in range(0, C, E_PIECE):
-            gather("scalar", e_by_slot, e[3], bag_list, lo, lo + E_PIECE)
-        late = keep.tile([P, 2 * C - held], F32, name="late", tag="scaled3")
-        dv1_last, dv2 = late[:, C:], late[:, :C]
-        make_dv(dv1_last, 1, held, C)
-        place_on_scalar(1, dv1_last, held, SCALAR_PIECES[-1:])
-        store(1)
-        make_e(2, ds[2])
-        make_dv(dv2, 2, 0, C)
-        for lo in (0, half):
-            nc.vector.tensor_tensor(placed[3][:].indirect(entries(idx_list, lo, lo + half)), e_by_slot[:, lo : lo + half], own[3][:, lo : lo + half], ADD)
-        store(3)
-        place_on_scalar(2, dv2, 0, SCALAR_PIECES)
-        store(2)
+        for t in range(1, D_TILES):
+            if t > 1:
+                sums[t] = keep.tile([P, X], F32, name="sums%d" % t)[:]
+                add_pairs(nc.vector, t)
+                scale_sums(nc.vector, t)
+                make_e(t, ds[t])
+            values = keep.tile([P, C], F32, name="dv%d" % t)
+            make_dv(values, t, 0, C)
+            place_on_scalar(t, values, 0, SCALAR_PIECES)
+            store(t)

@@ -21,9 +21,10 @@ PACK = 4
 STRIPE = 16
 D_TILES = D // P
 GY_PIECE = 256
-GY_ON_VECTOR = 512
-DZ_SCALAR_COLS = 176
 E_PIECE = 256
+GY_ON_VECTOR = 768
+FIRST_ON_VECTOR = 576
+DZ_SCALAR_COLS = 224
 SCALAR_PIECES = ((0, 352), (352, 704), (704, 1024))
 
 
@@ -31,6 +32,7 @@ def tile_attend_gfm_bi_kernel(tc, vT, W, dz, gy, offs, boffs, soffs, out):
     nc = tc.nc
     with ExitStack() as ctx:
         keep = ctx.enter_context(tc.tile_pool(name="keep", bufs=1))
+        shared = ctx.enter_context(tc.tile_pool(name="shared", bufs=1))
         psum = ctx.enter_context(tc.psum_pool(name="psum", bufs=1))
 
         bag_list = keep.tile([P, C // STRIPE], U16, name="bag_list")
@@ -54,19 +56,18 @@ def tile_attend_gfm_bi_kernel(tc, vT, W, dz, gy, offs, boffs, soffs, out):
         nc.sync.dma_start(tables[2][:], vT[2 * P : 3 * P, :])
         nc.sync.dma_start(tables[3][:], vT[3 * P :, :])
 
-        placed = [keep.tile([P, T], F32, name="placed%d" % t) for t in range(D_TILES)]
         minus_one = keep.tile([P, GY_PIECE], F32, name="minus_one")
         nc.vector.memset(minus_one[:], -1.0)
-        nc.vector.memset(placed[0][:], 0.0)
-        for t in (1, 3, 2):
-            nc.gpsimd.memset(placed[t][:], 0.0)
+        placed = [keep.tile([P, T], F32, name="placed%d" % t) for t in range(2)]
+        for window in placed:
+            nc.gpsimd.memset(window[:], 0.0)
 
         picked = [keep.tile([P, C], F32, name="picked%d" % t) for t in range(D_TILES)]
         by_sample = [keep.tile([P, C], F32, name="by_sample%d" % t) for t in range(D_TILES)]
-        sums = {t: keep.tile([P, X], F32, name="sums%d" % t)[:] for t in (0, 1)}
-        scaled = [keep.tile([P, X], F32, name="scaled%d" % t) for t in range(D_TILES)]
+        own = {t: keep.tile([P, C], F32, name="own%d" % t)[:] for t in range(1, D_TILES)}
+        scaled = {t: keep.tile([P, X], F32, name="scaled%d" % t)[:] for t in range(1, D_TILES)}
         e = [keep.tile([P, X], F32, name="e%d" % t, align_bytes=64) for t in range(D_TILES)]
-        dv = [keep.tile([P, C], F32, name="dv%d" % t) for t in range(1)]
+        dv = [keep.tile([P, C], F32, name="dv%d" % t) for t in range(2)]
         neg_gy_c = keep.tile([P, C], F32, name="neg_gy_c")
 
         def entries(listed, lo, hi):
@@ -84,16 +85,6 @@ def tile_attend_gfm_bi_kernel(tc, vT, W, dz, gy, offs, boffs, soffs, out):
 
         def gather_bags(engine, t, lo, hi):
             gather(engine, by_sample[t], picked[t], slot_list, lo, hi)
-
-        def add_pairs(engine, t):
-            pairs = by_sample[t][:].rearrange("p (x j) -> p j x", j=2)
-            engine.tensor_tensor(sums[t], pairs[:, 0, :], pairs[:, 1, :], ADD)
-
-        def scale_sums(engine, t):
-            engine.tensor_tensor(scaled[t][:], sums[t], gy_win[:], MULT)
-
-        def make_own(dst, t, lo, hi):
-            nc.gpsimd.tensor_tensor(dst, picked[t][:, lo:hi], neg_gy_c[:, lo:hi], MULT)
 
         def interleaved(grouped, raw, cols):
             return (
@@ -123,26 +114,15 @@ def tile_attend_gfm_bi_kernel(tc, vT, W, dz, gy, offs, boffs, soffs, out):
             return acc
 
         def make_e(t, ds):
-            nc.vector.tensor_tensor(e[t][:], ds[:], scaled[t][:], ADD)
-
-        def add_own(dst, t, lo, hi, own_part):
-            nc.vector.tensor_tensor(dst, e[t][:].indirect(entries(bag_list, lo, hi)), own_part, ADD)
-
-        def make_dv(dst, t, first, last):
-            for lo, hi in SCALAR_PIECES:
-                if first <= lo < last:
-                    add_own(dst[:, lo - first : hi - first], t, lo, hi, own[t][:, lo:hi])
-
-        def place_on_scalar(t, src, first, pieces):
-            for lo, hi in pieces:
-                nc.scalar.activation(placed[t][:].indirect(entries(idx_list, lo, hi)), src[:, lo - first : hi - first], COPY)
+            nc.vector.tensor_tensor(e[t][:], ds[:], scaled[t], ADD)
 
         def store(t):
             nc.sync.dma_start(out[t * P : (t + 1) * P, :], placed[t][:])
 
         half = C // 2
-        gy_twice = keep.tile([P, X // 2, 2], F32, name="gy_twice")
-        nc.scalar.copy(gy_twice[:], gy_win[:, : X // 2].unsqueeze(2).to_broadcast([P, X // 2, 2]))
+        gy_twice = keep.tile([P, X, 2], F32, name="gy_twice")
+        gy_by_entry = gy_twice[:].rearrange("p x j -> p (x j)")
+        nc.scalar.copy(gy_twice[:], gy_win[:].unsqueeze(2).to_broadcast([P, X, 2]))
         for lo in range(0, C, GY_PIECE):
             dst, src = neg_gy_c[:, lo : lo + GY_PIECE], gy_win[:].indirect(entries(bag_list, lo, lo + GY_PIECE))
             if lo < GY_ON_VECTOR:
@@ -150,57 +130,73 @@ def tile_attend_gfm_bi_kernel(tc, vT, W, dz, gy, offs, boffs, soffs, out):
             else:
                 nc.scalar.activation(dst, src, COPY, scale=-1.0)
 
-        gather_table("vector", 0, 0, half)
-        gather_table("scalar", 0, half, C)
-        nc.vector.tensor_tensor(by_sample[0][:, :half], picked[0][:].indirect(entries(slot_list, 0, half)), gy_twice[:].rearrange("p x j -> p (x j)"), MULT)
-        gather_bags("scalar", 0, half, C)
-        own0_low = keep.tile([P, half], F32, name="own0_low")
-        make_own(own0_low[:], 0, 0, half)
+        def gather_scaled_bags(t, lo, hi):
+            nc.vector.tensor_tensor(by_sample[t][:, lo:hi], picked[t][:].indirect(entries(slot_list, lo, hi)), gy_by_entry[:, lo:hi], MULT)
+
+        def add_pairs(dst, t, lo, hi):
+            pairs = by_sample[t][:].rearrange("p (x j) -> p j x", j=2)
+            nc.vector.tensor_tensor(dst, pairs[:, 0, lo:hi], pairs[:, 1, lo:hi], ADD)
+
+        def make_own(t):
+            nc.vector.tensor_tensor(own[t], picked[t][:], neg_gy_c[:], MULT)
+
+        def make_sample_terms(t):
+            for lo in (0, half):
+                gather_scaled_bags(t, lo, lo + half)
+            make_own(t)
+            add_pairs(scaled[t], t, 0, X)
+            make_e(t, ds[t])
+
+        def finish(t, pieces=SCALAR_PIECES, stored=True):
+            for lo, hi in pieces:
+                nc.vector.tensor_tensor(dv[t][:, lo:hi], e[t][:].indirect(entries(bag_list, lo, hi)), own[t][:, lo:hi], ADD)
+                nc.scalar.activation(placed[t][:].indirect(entries(idx_list, lo, hi)), dv[t][:, lo:hi], COPY)
+            if stored and pieces[-1][1] == C:
+                store(t)
+
+        gather_table("vector", 0, 0, FIRST_ON_VECTOR)
+        gather_table("scalar", 0, FIRST_ON_VECTOR, C)
+        gather_scaled_bags(0, 0, FIRST_ON_VECTOR)
+        gather_bags("scalar", 0, FIRST_ON_VECTOR, C)
+        cut = FIRST_ON_VECTOR // 2
 
         dz_grouped = keep.tile([P, X, PACK], BF16, name="dz_grouped", align_bytes=64)
         nc.vector.tensor_copy(*interleaved(dz_grouped, dz_raw, slice(DZ_SCALAR_COLS, X)))
         nc.scalar.copy(*interleaved(dz_grouped, dz_raw, slice(0, DZ_SCALAR_COLS)))
-        w_grouped = keep.tile([P, D // 2, PACK], BF16, name="w_grouped", tag="w_room", align_bytes=64)
+        w_grouped = shared.tile([P, D // 2, PACK], BF16, name="w_grouped", offset=4 * T - 1024, align_bytes=64)
         nc.scalar.copy(*interleaved(w_grouped, w_raw[0], slice(0, D // 2)))
-        pairs = by_sample[0][:].rearrange("p (x j) -> p j x", j=2)
-        nc.vector.tensor_tensor(sums[0][:, X // 2 :], pairs[:, 0, X // 2 :], pairs[:, 1, X // 2 :], ADD)
         dz_planes = quantise(dz_grouped, "dz", E5M2X4)
-        nc.vector.tensor_tensor(scaled[0][:, : X // 2], pairs[:, 0, : X // 2], pairs[:, 1, : X // 2], ADD)
-        nc.vector.tensor_tensor(scaled[0][:, X // 2 :], sums[0][:, X // 2 :], gy_win[:, X // 2 :], MULT)
         w_planes = quantise(w_grouped, "w_low", E4M3X4)
         ds = [dense_gradient(t, w_planes, dz_planes) for t in range(2)]
-        own0_high = keep.tile([P, half], F32, name="own0_high", tag="w_room", align_bytes=64)
-        make_own(own0_high[:], 0, half, C)
+        first = keep.tile([P, C + 2 * X - cut], F32, name="first", tag="dz_grouped", align_bytes=64)
+        own[0], scaled[0], sums = first[:, :C], first[:, C : C + X], first[:, C + X :]
+        add_pairs(sums, 0, cut, X)
+        add_pairs(scaled[0][:, :cut], 0, 0, cut)
+        nc.vector.tensor_tensor(scaled[0][:, cut:], sums, gy_win[:, cut:], MULT)
+        for u in range(2):
+            placed.append(shared.tile([P, T], F32, name="placed%d" % (2 + u), offset=4 * T * u))
+            nc.gpsimd.memset(placed[2 + u][:], 0.0)
+        make_own(0)
+        gather_table("scalar", 1)
         make_e(0, ds[0])
-        for lo in range(0, C, E_PIECE):
-            own_half = own0_low if lo < half else own0_high
-            add_own(dv[0][:, lo : lo + E_PIECE], 0, lo, lo + E_PIECE, own_half[:, lo % half : lo % half + E_PIECE])
-
-        own = [None] + [keep.tile([P, C], F32, name="own%d" % t) for t in range(1, D_TILES)]
-        for t in range(1, D_TILES):
-            gather_table("scalar", t)
-            for lo in (0, half):
-                gather_bags("scalar", t, lo, lo + half)
-            make_own(own[t][:], t, 0, C)
-            if t == 1:
-                add_pairs(nc.gpsimd, t)
-                scale_sums(nc.gpsimd, t)
-
-        place_on_scalar(0, dv[0], 0, SCALAR_PIECES)
-        store(0)
+        finish(0)
+        gather_table("scalar", 2)
+        make_sample_terms(1)
+        gather_table("scalar", 3)
         w_grouped = keep.tile([P, D // 2, PACK], BF16, name="w_grouped_high", tag="e0", align_bytes=64)
         nc.vector.tensor_copy(*interleaved(w_grouped, w_raw[1], slice(0, D // 2)))
-        make_e(1, ds[1])
+        finish(1, SCALAR_PIECES[:1])
         w_planes = quantise(w_grouped, "w_high", E4M3X4)
-        ds += [None, dense_gradient(3, w_planes, dz_planes)]
-        ds[2] = dense_gradient(2, w_planes, dz_planes)
-        for t in range(1, D_TILES):
-            if t > 1:
-                sums[t] = keep.tile([P, X], F32, name="sums%d" % t)[:]
-                add_pairs(nc.vector, t)
-                scale_sums(nc.vector, t)
-                make_e(t, ds[t])
-            values = keep.tile([P, C], F32, name="dv%d" % t)
-            make_dv(values, t, 0, C)
-            place_on_scalar(t, values, 0, SCALAR_PIECES)
-            store(t)
+        ds += [dense_gradient(u, w_planes, dz_planes) for u in (2, 3)]
+        finish(1, SCALAR_PIECES[1:])
+        make_sample_terms(2)
+        make_sample_terms(3)
+        e_by_slot = keep.tile([P, C], F32, name="e_by_slot")
+        for lo in range(0, C, E_PIECE):
+            gather("scalar", e_by_slot, e[3], bag_list, lo, lo + E_PIECE)
+        dv.append(keep.tile([P, C], F32, name="dv2", tag="scaled3"))
+        finish(2, stored=False)
+        for lo in (0, half):
+            nc.vector.tensor_tensor(placed[3][:].indirect(entries(idx_list, lo, lo + half)), e_by_slot[:, lo : lo + half], own[3][:, lo : lo + half], ADD)
+        store(3)
+        store(2)

@@ -22,9 +22,9 @@ STRIPE = 16
 D_TILES = D // P
 GY_PIECE = 256
 E_PIECE = 256
+TABLE2_AT = 2048
 GY_ON_VECTOR = 768
 FIRST_ON_VECTOR = 576
-DZ_SCALAR_COLS = 224
 SCALAR_PIECES = ((0, 352), (352, 704), (704, 1024))
 
 
@@ -32,14 +32,15 @@ def tile_attend_gfm_bi_kernel(tc, vT, W, dz, gy, offs, boffs, soffs, out):
     nc = tc.nc
     with ExitStack() as ctx:
         keep = ctx.enter_context(tc.tile_pool(name="keep", bufs=1))
-        shared = ctx.enter_context(tc.tile_pool(name="shared", bufs=1))
+        chain = ctx.enter_context(tc.tile_pool(name="chain", bufs=1))
         psum = ctx.enter_context(tc.psum_pool(name="psum", bufs=1))
 
         bag_list = keep.tile([P, C // STRIPE], U16, name="bag_list")
         idx_list = keep.tile([P, C // STRIPE], U16, name="idx_list")
         slot_list = keep.tile([P, C // STRIPE], U16, name="slot_list")
         gy_win = keep.tile([P, X], F32, name="gy_win")
-        tables = [keep.tile([P, T], F32, name="table%d" % t) for t in range(D_TILES)]
+        tables = {t: keep.tile([P, T], F32, name="table%d" % t, align_bytes=64) for t in (0, 1, 3)}
+        tables[2] = chain.tile([P, T], F32, name="table2", offset=4 * TABLE2_AT)
         w_raw = [keep.tile([P, PACK, D // 2], F32, name="w_raw%d" % h) for h in range(2)]
         dz_raw = keep.tile([P, PACK, X], F32, name="dz_raw")
         w_rows = W.rearrange("(p j) d -> p j d", j=PACK)
@@ -58,16 +59,14 @@ def tile_attend_gfm_bi_kernel(tc, vT, W, dz, gy, offs, boffs, soffs, out):
 
         minus_one = keep.tile([P, GY_PIECE], F32, name="minus_one")
         nc.vector.memset(minus_one[:], -1.0)
-        placed = [keep.tile([P, T], F32, name="placed%d" % t) for t in range(2)]
+        placed = [keep.tile([P, T], F32, name="placed%d" % t) for t in range(3)]
         for window in placed:
             nc.gpsimd.memset(window[:], 0.0)
 
-        picked = [keep.tile([P, C], F32, name="picked%d" % t) for t in range(D_TILES)]
-        by_sample = [keep.tile([P, C], F32, name="by_sample%d" % t) for t in range(D_TILES)]
-        own = {t: keep.tile([P, C], F32, name="own%d" % t)[:] for t in range(1, D_TILES)}
-        scaled = {t: keep.tile([P, X], F32, name="scaled%d" % t)[:] for t in range(1, D_TILES)}
+        picked = {t: keep.tile([P, C], F32, name="picked%d" % t) for t in (0, 1, 2)}
+        by_sample = {t: keep.tile([P, C], F32, name="by_sample%d" % t) for t in (0, 2, 3)}
+        scaled = {t: keep.tile([P, X], F32, name="scaled%d" % t)[:] for t in range(D_TILES)}
         e = [keep.tile([P, X], F32, name="e%d" % t, align_bytes=64) for t in range(D_TILES)]
-        dv = [keep.tile([P, C], F32, name="dv%d" % t) for t in range(2)]
         neg_gy_c = keep.tile([P, C], F32, name="neg_gy_c")
 
         def entries(listed, lo, hi):
@@ -92,9 +91,12 @@ def tile_attend_gfm_bi_kernel(tc, vT, W, dz, gy, offs, boffs, soffs, out):
                 raw[:, :, cols].rearrange("p j (c i) -> p c j i", i=4),
             )
 
-        def quantise(grouped, name, fmt):
+        def quantise(grouped, name, fmt, at=None):
             width = grouped.shape[1]
-            codes = keep.tile([P, width], U32, name=name + "_codes", align_bytes=64)
+            if at is None:
+                codes = keep.tile([P, width], U32, name=name + "_codes", align_bytes=64)
+            else:
+                codes = chain.tile([P, width], U32, name=name + "_codes", offset=at, align_bytes=64)
             scales = keep.tile([P, width], U8, name=name + "_scales", align_bytes=64)
             nc.vector.quantize_mx(out=codes[:].bitcast(fmt), scales=scales[:], in_=grouped[:].rearrange("p w j -> p (w j)"))
             return codes, scales
@@ -120,9 +122,9 @@ def tile_attend_gfm_bi_kernel(tc, vT, W, dz, gy, offs, boffs, soffs, out):
             nc.sync.dma_start(out[t * P : (t + 1) * P, :], placed[t][:])
 
         half = C // 2
-        gy_twice = keep.tile([P, X, 2], F32, name="gy_twice")
-        gy_by_entry = gy_twice[:].rearrange("p x j -> p (x j)")
-        nc.scalar.copy(gy_twice[:], gy_win[:].unsqueeze(2).to_broadcast([P, X, 2]))
+        gy_twice = [keep.tile([P, X // 2, 2], F32, name="gy_twice%d" % h) for h in range(2)]
+        for h in range(2):
+            nc.scalar.copy(gy_twice[h][:], gy_win[:, h * X // 2 : (h + 1) * X // 2].unsqueeze(2).to_broadcast([P, X // 2, 2]))
         for lo in range(0, C, GY_PIECE):
             dst, src = neg_gy_c[:, lo : lo + GY_PIECE], gy_win[:].indirect(entries(bag_list, lo, lo + GY_PIECE))
             if lo < GY_ON_VECTOR:
@@ -130,73 +132,107 @@ def tile_attend_gfm_bi_kernel(tc, vT, W, dz, gy, offs, boffs, soffs, out):
             else:
                 nc.scalar.activation(dst, src, COPY, scale=-1.0)
 
-        def gather_scaled_bags(t, lo, hi):
-            nc.vector.tensor_tensor(by_sample[t][:, lo:hi], picked[t][:].indirect(entries(slot_list, lo, hi)), gy_by_entry[:, lo:hi], MULT)
+        def gather_scaled_bags(t, h):
+            lo, hi = h * half, (h + 1) * half
+            nc.vector.tensor_tensor(by_sample[t][:, lo:hi], picked[t][:].indirect(entries(slot_list, lo, hi)), gy_twice[h][:].rearrange("p x j -> p (x j)"), MULT)
 
         def add_pairs(dst, t, lo, hi):
             pairs = by_sample[t][:].rearrange("p (x j) -> p j x", j=2)
             nc.vector.tensor_tensor(dst, pairs[:, 0, lo:hi], pairs[:, 1, lo:hi], ADD)
 
-        def make_own(t):
-            nc.vector.tensor_tensor(own[t], picked[t][:], neg_gy_c[:], MULT)
+        def make_own(dst, t, lo, hi):
+            nc.gpsimd.tensor_tensor(dst, picked[t][:, lo:hi], neg_gy_c[:, lo:hi], MULT)
 
-        def make_sample_terms(t):
-            for lo in (0, half):
-                gather_scaled_bags(t, lo, lo + half)
-            make_own(t)
-            add_pairs(scaled[t], t, 0, X)
-            make_e(t, ds[t])
-
-        def finish(t, pieces=SCALAR_PIECES, stored=True):
+        def finish(t, pieces, values, own):
+            first = pieces[0][0]
             for lo, hi in pieces:
-                nc.vector.tensor_tensor(dv[t][:, lo:hi], e[t][:].indirect(entries(bag_list, lo, hi)), own[t][:, lo:hi], ADD)
-                nc.scalar.activation(placed[t][:].indirect(entries(idx_list, lo, hi)), dv[t][:, lo:hi], COPY)
-            if stored and pieces[-1][1] == C:
-                store(t)
+                part = slice(lo - first, hi - first)
+                nc.vector.tensor_tensor(values[:, part], e[t][:].indirect(entries(bag_list, lo, hi)), own[:, part], ADD)
+                nc.scalar.activation(placed[t][:].indirect(entries(idx_list, lo, hi)), values[:, part], COPY)
 
         gather_table("vector", 0, 0, FIRST_ON_VECTOR)
         gather_table("scalar", 0, FIRST_ON_VECTOR, C)
-        gather_scaled_bags(0, 0, FIRST_ON_VECTOR)
-        gather_bags("scalar", 0, FIRST_ON_VECTOR, C)
-        cut = FIRST_ON_VECTOR // 2
+        word = 4
+        lead = SCALAR_PIECES[0][1]
+        own0 = chain.tile([P, C], F32, name="own0", offset=0)
+        nc.vector.tensor_tensor(own0[:], picked[0][:], neg_gy_c[:], MULT)
+        for lo in (0, half):
+            gather_bags("scalar", 0, lo, lo + half)
 
         dz_grouped = keep.tile([P, X, PACK], BF16, name="dz_grouped", align_bytes=64)
-        nc.vector.tensor_copy(*interleaved(dz_grouped, dz_raw, slice(DZ_SCALAR_COLS, X)))
-        nc.scalar.copy(*interleaved(dz_grouped, dz_raw, slice(0, DZ_SCALAR_COLS)))
-        w_grouped = shared.tile([P, D // 2, PACK], BF16, name="w_grouped", offset=4 * T - 1024, align_bytes=64)
+        nc.vector.tensor_copy(*interleaved(dz_grouped, dz_raw, slice(0, X)))
+        w_grouped = keep.tile([P, D // 2, PACK], BF16, name="w_grouped", align_bytes=64)
         nc.scalar.copy(*interleaved(w_grouped, w_raw[0], slice(0, D // 2)))
         dz_planes = quantise(dz_grouped, "dz", E5M2X4)
+        sums0 = keep.tile([P, X], F32, name="sums0", tag="dz_raw")
+        add_pairs(sums0[:], 0, 0, X)
         w_planes = quantise(w_grouped, "w_low", E4M3X4)
         ds = [dense_gradient(t, w_planes, dz_planes) for t in range(2)]
-        first = keep.tile([P, C + 2 * X - cut], F32, name="first", tag="dz_grouped", align_bytes=64)
-        own[0], scaled[0], sums = first[:, :C], first[:, C : C + X], first[:, C + X :]
-        add_pairs(sums, 0, cut, X)
-        add_pairs(scaled[0][:, :cut], 0, 0, cut)
-        nc.vector.tensor_tensor(scaled[0][:, cut:], sums, gy_win[:, cut:], MULT)
-        for u in range(2):
-            placed.append(shared.tile([P, T], F32, name="placed%d" % (2 + u), offset=4 * T * u))
-            nc.gpsimd.memset(placed[2 + u][:], 0.0)
-        make_own(0)
+        nc.vector.tensor_tensor(scaled[0], sums0[:], gy_win[:], MULT)
         gather_table("scalar", 1)
         make_e(0, ds[0])
-        finish(0)
-        gather_table("scalar", 2)
-        make_sample_terms(1)
-        gather_table("scalar", 3)
-        w_grouped = keep.tile([P, D // 2, PACK], BF16, name="w_grouped_high", tag="e0", align_bytes=64)
-        nc.vector.tensor_copy(*interleaved(w_grouped, w_raw[1], slice(0, D // 2)))
-        finish(1, SCALAR_PIECES[:1])
-        w_planes = quantise(w_grouped, "w_high", E4M3X4)
-        ds += [dense_gradient(u, w_planes, dz_planes) for u in (2, 3)]
-        finish(1, SCALAR_PIECES[1:])
-        make_sample_terms(2)
-        make_sample_terms(3)
-        e_by_slot = keep.tile([P, C], F32, name="e_by_slot")
-        for lo in range(0, C, E_PIECE):
-            gather("scalar", e_by_slot, e[3], bag_list, lo, lo + E_PIECE)
-        dv.append(keep.tile([P, C], F32, name="dv2", tag="scaled3"))
-        finish(2, stored=False)
+        first, second, third = ([piece] for piece in SCALAR_PIECES)
+        dv0_first = keep.tile([P, lead], F32, name="dv0_first")
+        finish(0, first, dv0_first, own0[:, :lead])
+        w_grouped = keep.tile([P, D // 2, PACK], BF16, name="w_grouped_high", align_bytes=64)
+        nc.scalar.copy(*interleaved(w_grouped, w_raw[1], slice(0, D // 2)))
+        by_sample[1] = keep.tile([P, C], F32, name="by_sample1", tag="scaled0")
+        for h in range(2):
+            gather_scaled_bags(1, h)
+        dv0_second = keep.tile([P, lead], F32, name="dv0_second", tag="gy_twice0")
+        finish(0, second, dv0_second, own0[:, lead:])
+        add_pairs(scaled[1], 1, 0, X)
+        dv0_third = keep.tile([P, C - 2 * lead], F32, name="dv0_third", tag="gy_twice1")
+        finish(0, third, dv0_third, own0[:, 2 * lead :])
+        store(0)
+        own1_first = chain.tile([P, lead], F32, name="own1_first", offset=word * (C - lead))
+        own1_rest = chain.tile([P, C - lead], F32, name="own1_rest", offset=0)
+        make_own(own1_first[:], 1, 0, lead)
+        make_own(own1_rest[:], 1, lead, C)
+        placed.append(keep.tile([P, T], F32, name="placed3", tag="picked1"))
+        nc.gpsimd.memset(placed[3][:], 0.0)
+        make_e(1, ds[1])
+        gather_table("vector", 2)
         for lo in (0, half):
-            nc.vector.tensor_tensor(placed[3][:].indirect(entries(idx_list, lo, lo + half)), e_by_slot[:, lo : lo + half], own[3][:, lo : lo + half], ADD)
-        store(3)
+            gather_bags("scalar", 2, lo, lo + half)
+        w_planes = quantise(w_grouped, "w_high", E4M3X4, word * (TABLE2_AT + C))
+        ds += [dense_gradient(u, w_planes, dz_planes) for u in (2, 3)]
+        dv1_first = keep.tile([P, lead], F32, name="dv1_first")
+        finish(1, first, dv1_first, own1_first)
+        own2 = chain.tile([P, C], F32, name="own2", offset=word * (C - lead))
+        make_own(own2[:], 2, 0, C)
+        picked[3] = chain.tile([P, C], F32, name="picked3", offset=word * TABLE2_AT)
+        gather_table("vector", 3)
+        for lo in (0, half):
+            gather_bags("scalar", 3, lo, lo + half)
+        behind_table = keep.tile([P, X + C - lead], F32, name="behind_table", tag="table3", align_bytes=64)
+        finish(1, second, behind_table[:, X:], own1_rest)
+        halves = [slice(0, X // 2), slice(X // 2, X)]
+        for part in halves:
+            add_pairs(behind_table[:, part], 2, part.start, part.stop)
+        for part in halves:
+            nc.vector.tensor_tensor(scaled[2][:, part], behind_table[:, part], gy_win[:, part], MULT)
+        for part in halves:
+            nc.vector.tensor_tensor(e[2][:, part], ds[2][:, part], scaled[2][:, part], ADD)
+        finish(1, third, behind_table[:, X + lead :], own1_rest[:, lead:])
+        store(1)
+        dv2 = keep.tile([P, C], F32, name="dv2")
+        sums3 = keep.tile([P, X], F32, name="sums3", tag="scaled2")
+        steps = (
+            lambda: add_pairs(sums3[:], 3, 0, X),
+            lambda: nc.vector.tensor_tensor(scaled[3], sums3[:], gy_win[:], MULT),
+            lambda: make_e(3, ds[3]),
+        )
+        for (lo, hi), step in zip(SCALAR_PIECES, steps):
+            finish(2, [(lo, hi)], dv2[:, lo:], own2[:, lo:])
+            step()
+        own3 = chain.tile([P, C], F32, name="own3", offset=word * (C - lead))
+        make_own(own3[:], 3, 0, C)
+        e_by_slot = keep.tile([P, C], F32, name="e_by_slot")
+        for lo in range(0, C - E_PIECE, E_PIECE):
+            gather("vector", e_by_slot, e[3], bag_list, lo, lo + E_PIECE)
         store(2)
+        nc.vector.tensor_tensor(placed[3][:].indirect(entries(idx_list, 0, half)), e_by_slot[:, :half], own3[:, :half], ADD)
+        gather("vector", e_by_slot, e[3], bag_list, C - E_PIECE, C)
+        nc.vector.tensor_tensor(placed[3][:].indirect(entries(idx_list, half, C)), e_by_slot[:, half:], own3[:, half:], ADD)
+        store(3)

@@ -189,8 +189,6 @@ def tile_attend_gfm_bi_kernel(tc, vT, W, dz, gy, offs, boffs, soffs, out):
         own1_rest = chain.tile([P, C - lead], F32, name="own1_rest", offset=0)
         make_own(own1_first[:], 1, 0, lead)
         make_own(own1_rest[:], 1, lead, C)
-        placed.append(keep.tile([P, T], F32, name="placed3", tag="picked1"))
-        nc.gpsimd.memset(placed[3][:], 0.0)
         make_e(1, ds[1])
         gather_table("vector", 2)
         for lo in (0, half):
@@ -201,6 +199,8 @@ def tile_attend_gfm_bi_kernel(tc, vT, W, dz, gy, offs, boffs, soffs, out):
         finish(1, first, dv1_first, own1_first)
         own2 = chain.tile([P, C], F32, name="own2", offset=word * (C - lead))
         make_own(own2[:], 2, 0, C)
+        placed.append(keep.tile([P, T], F32, name="placed3", tag="picked2"))
+        nc.gpsimd.memset(placed[3][:], 0.0)
         picked[3] = chain.tile([P, C], F32, name="picked3", offset=word * TABLE2_AT)
         gather_table("vector", 3)
         for lo in (0, half):

@@ -19,30 +19,37 @@ MULT = mybir.AluOpType.mult
 P = 128
 PACK = 4
 STRIPE = 16
+WORD = 4
 D_TILES = D // P
-GY_PIECE = 256
-E_PIECE = 256
-TABLE2_AT = 2048
+HALF = C // 2
+PIECE = C // 4
 GY_ON_VECTOR = 768
-FIRST_ON_VECTOR = 576
-SCALAR_PIECES = ((0, 352), (352, 704), (704, 1024))
 
 
 def tile_attend_gfm_bi_kernel(tc, vT, W, dz, gy, offs, boffs, soffs, out):
     nc = tc.nc
     with ExitStack() as ctx:
         keep = ctx.enter_context(tc.tile_pool(name="keep", bufs=1))
-        chain = ctx.enter_context(tc.tile_pool(name="chain", bufs=1))
+        reuse = ctx.enter_context(tc.tile_pool(name="reuse", bufs=1))
         psum = ctx.enter_context(tc.psum_pool(name="psum", bufs=1))
+
+        def fresh(name, *shape):
+            return keep.tile([P, *shape], F32, name=name)
+
+        def placed_at(name, at, *shape):
+            return reuse.tile([P, *shape], F32, name=name, offset=WORD * at)
+
+        table_at = {t: (t - 1) * T for t in (1, 2, 3)}
+        dz_at = 3 * T
+        w_at = 4 * T + X
 
         bag_list = keep.tile([P, C // STRIPE], U16, name="bag_list")
         idx_list = keep.tile([P, C // STRIPE], U16, name="idx_list")
         slot_list = keep.tile([P, C // STRIPE], U16, name="slot_list")
-        gy_win = keep.tile([P, X], F32, name="gy_win")
-        tables = {t: keep.tile([P, T], F32, name="table%d" % t, align_bytes=64) for t in (0, 1, 3)}
-        tables[2] = chain.tile([P, T], F32, name="table2", offset=4 * TABLE2_AT)
-        w_raw = [keep.tile([P, PACK, D // 2], F32, name="w_raw%d" % h) for h in range(2)]
-        dz_raw = keep.tile([P, PACK, X], F32, name="dz_raw")
+        gy_win = fresh("gy_win", X)
+        tables = [fresh("table0", T)] + [placed_at("table%d" % t, table_at[t], T) for t in (1, 2, 3)]
+        dz_raw = placed_at("dz_raw", dz_at, PACK, X)
+        w_raw = [placed_at("w_raw0", w_at, PACK, D // 2), fresh("w_raw1", PACK, D // 2)]
         w_rows = W.rearrange("(p j) d -> p j d", j=PACK)
 
         nc.sync.dma_start(bag_list[:], boffs)
@@ -50,24 +57,22 @@ def tile_attend_gfm_bi_kernel(tc, vT, W, dz, gy, offs, boffs, soffs, out):
         nc.sync.dma_start(idx_list[:], offs)
         nc.sync.dma_start(tables[0][:], vT[0:P, :])
         nc.sync.dma_start(slot_list[:], soffs)
+        nc.sync.dma_start(tables[1][:], vT[P : 2 * P, :])
         nc.sync.dma_start(dz_raw[:], dz.rearrange("(p j) x -> p j x", j=PACK))
         nc.sync.dma_start(w_raw[0][:], w_rows[:, :, : D // 2])
-        nc.sync.dma_start(tables[1][:], vT[P : 2 * P, :])
-        nc.sync.dma_start(w_raw[1][:], w_rows[:, :, D // 2 :])
         nc.sync.dma_start(tables[2][:], vT[2 * P : 3 * P, :])
         nc.sync.dma_start(tables[3][:], vT[3 * P :, :])
+        nc.sync.dma_start(w_raw[1][:], w_rows[:, :, D // 2 :])
 
-        minus_one = keep.tile([P, GY_PIECE], F32, name="minus_one")
+        minus_one = fresh("minus_one", GY_ON_VECTOR // 2)
         nc.vector.memset(minus_one[:], -1.0)
-        placed = [keep.tile([P, T], F32, name="placed%d" % t) for t in range(3)]
-        for window in placed:
+        windows = [fresh("window%d" % t, T) for t in range(3)]
+        for window in windows:
             nc.gpsimd.memset(window[:], 0.0)
+        windows.append(windows[0])
 
-        picked = {t: keep.tile([P, C], F32, name="picked%d" % t) for t in (0, 1, 2)}
-        by_sample = {t: keep.tile([P, C], F32, name="by_sample%d" % t) for t in (0, 2, 3)}
-        scaled = {t: keep.tile([P, X], F32, name="scaled%d" % t)[:] for t in range(D_TILES)}
-        e = [keep.tile([P, X], F32, name="e%d" % t, align_bytes=64) for t in range(D_TILES)]
-        neg_gy_c = keep.tile([P, C], F32, name="neg_gy_c")
+        picked = [fresh("picked%d" % t, C) for t in range(D_TILES)]
+        neg_gy_c = fresh("neg_gy_c", C)
 
         def entries(listed, lo, hi):
             return listed[:, lo // STRIPE : hi // STRIPE]
@@ -75,28 +80,25 @@ def tile_attend_gfm_bi_kernel(tc, vT, W, dz, gy, offs, boffs, soffs, out):
         def gather(engine, dst, window, listed, lo, hi):
             src = window[:].indirect(entries(listed, lo, hi))
             if engine == "vector":
-                nc.vector.tensor_copy(dst[:, lo:hi], src)
+                nc.vector.tensor_copy(dst, src)
             else:
-                nc.scalar.activation(dst[:, lo:hi], src, COPY)
+                nc.scalar.activation(dst, src, COPY)
 
         def gather_table(engine, t, lo=0, hi=C):
-            gather(engine, picked[t], tables[t], idx_list, lo, hi)
+            gather(engine, picked[t][:, lo:hi], tables[t], idx_list, lo, hi)
 
-        def gather_bags(engine, t, lo, hi):
-            gather(engine, by_sample[t], picked[t], slot_list, lo, hi)
+        def gather_bags(engine, t, dst, lo, hi):
+            gather(engine, dst[:, lo:hi], picked[t], slot_list, lo, hi)
 
-        def interleaved(grouped, raw, cols):
+        def interleaved(grouped, raw):
             return (
-                grouped[:, cols, :].rearrange("p (c i) j -> p c j i", i=4),
-                raw[:, :, cols].rearrange("p j (c i) -> p c j i", i=4),
+                grouped[:].rearrange("p (c i) j -> p c j i", i=4),
+                raw[:].rearrange("p j (c i) -> p c j i", i=4),
             )
 
-        def quantise(grouped, name, fmt, at=None):
+        def quantise(grouped, name, fmt):
             width = grouped.shape[1]
-            if at is None:
-                codes = keep.tile([P, width], U32, name=name + "_codes", align_bytes=64)
-            else:
-                codes = chain.tile([P, width], U32, name=name + "_codes", offset=at, align_bytes=64)
+            codes = keep.tile([P, width], U32, name=name + "_codes", align_bytes=64)
             scales = keep.tile([P, width], U8, name=name + "_scales", align_bytes=64)
             nc.vector.quantize_mx(out=codes[:].bitcast(fmt), scales=scales[:], in_=grouped[:].rearrange("p w j -> p (w j)"))
             return codes, scales
@@ -115,124 +117,135 @@ def tile_attend_gfm_bi_kernel(tc, vT, W, dz, gy, offs, boffs, soffs, out):
             )
             return acc
 
-        def make_e(t, ds):
-            nc.vector.tensor_tensor(e[t][:], ds[:], scaled[t], ADD)
+        def add_pairs(dst, by_sample):
+            pairs = by_sample.rearrange("p (x j) -> p j x", j=2)
+            nc.vector.tensor_tensor(dst[:], pairs[:, 0, :], pairs[:, 1, :], ADD)
 
-        def store(t):
-            nc.sync.dma_start(out[t * P : (t + 1) * P, :], placed[t][:])
+        def scale_by_gy(dst, sums):
+            nc.vector.tensor_tensor(dst[:], sums[:], gy_win[:], MULT)
 
-        half = C // 2
-        gy_twice = [keep.tile([P, X // 2, 2], F32, name="gy_twice%d" % h) for h in range(2)]
-        for h in range(2):
-            nc.scalar.copy(gy_twice[h][:], gy_win[:, h * X // 2 : (h + 1) * X // 2].unsqueeze(2).to_broadcast([P, X // 2, 2]))
-        for lo in range(0, C, GY_PIECE):
-            dst, src = neg_gy_c[:, lo : lo + GY_PIECE], gy_win[:].indirect(entries(bag_list, lo, lo + GY_PIECE))
-            if lo < GY_ON_VECTOR:
-                nc.vector.tensor_tensor(dst, src, minus_one[:], MULT)
-            else:
-                nc.scalar.activation(dst, src, COPY, scale=-1.0)
+        def make_e(dst, ds, scaled):
+            nc.vector.tensor_tensor(dst[:], ds[:], scaled[:], ADD)
 
-        def gather_scaled_bags(t, h):
-            lo, hi = h * half, (h + 1) * half
-            nc.vector.tensor_tensor(by_sample[t][:, lo:hi], picked[t][:].indirect(entries(slot_list, lo, hi)), gy_twice[h][:].rearrange("p x j -> p (x j)"), MULT)
+        def finish(t, k, e, values, own):
+            lo, hi = k * PIECE, (k + 1) * PIECE
+            nc.vector.tensor_tensor(values, e[:].indirect(entries(bag_list, lo, hi)), own, ADD)
+            nc.scalar.activation(windows[t][:].indirect(entries(idx_list, lo, hi)), values, COPY)
 
-        def add_pairs(dst, t, lo, hi):
-            pairs = by_sample[t][:].rearrange("p (x j) -> p j x", j=2)
-            nc.vector.tensor_tensor(dst, pairs[:, 0, lo:hi], pairs[:, 1, lo:hi], ADD)
+        def piece(tile, k, first=0):
+            return tile[:, first + k * PIECE : first + (k + 1) * PIECE]
 
-        def make_own(dst, t, lo, hi):
-            nc.gpsimd.tensor_tensor(dst, picked[t][:, lo:hi], neg_gy_c[:, lo:hi], MULT)
+        def rows(t):
+            return out[t * P : (t + 1) * P, :]
 
-        def finish(t, pieces, values, own):
-            first = pieces[0][0]
-            for lo, hi in pieces:
-                part = slice(lo - first, hi - first)
-                nc.vector.tensor_tensor(values[:, part], e[t][:].indirect(entries(bag_list, lo, hi)), own[:, part], ADD)
-                nc.scalar.activation(placed[t][:].indirect(entries(idx_list, lo, hi)), values[:, part], COPY)
+        gy_twice = fresh("gy_twice", X, 2)
+        nc.scalar.copy(gy_twice[:], gy_win[:].unsqueeze(2).to_broadcast([P, X, 2]))
+        for lo in (0, GY_ON_VECTOR // 2):
+            hi = lo + GY_ON_VECTOR // 2
+            nc.vector.tensor_tensor(neg_gy_c[:, lo:hi], gy_win[:].indirect(entries(bag_list, lo, hi)), minus_one[:], MULT)
+        nc.scalar.activation(neg_gy_c[:, GY_ON_VECTOR:], gy_win[:].indirect(entries(bag_list, GY_ON_VECTOR, C)), COPY, scale=-1.0)
 
-        gather_table("vector", 0, 0, FIRST_ON_VECTOR)
-        gather_table("scalar", 0, FIRST_ON_VECTOR, C)
-        word = 4
-        lead = SCALAR_PIECES[0][1]
-        own0 = chain.tile([P, C], F32, name="own0", offset=0)
-        nc.vector.tensor_tensor(own0[:], picked[0][:], neg_gy_c[:], MULT)
-        for lo in (0, half):
-            gather_bags("scalar", 0, lo, lo + half)
+        own0_at, own0_step, own2_at, own3_at = 640, 1408, 1024, 1920
+        relay = fresh("relay", own0_at + 2 * own0_step)
+        own0_rows = relay[:, own0_at:].rearrange("p (r w) -> p r w", r=2)[:, :, :HALF]
+        own0 = [piece(relay, k % 2, own0_at + k // 2 * own0_step) for k in range(4)]
 
+        shares = (("vector", 0, HALF), ("scalar", HALF, C))
+        by_sample0 = fresh("by_sample0", C)
+        for engine, lo, hi in shares:
+            gather_table(engine, 0, lo, hi)
+        nc.gpsimd.tensor_tensor(own0_rows, picked[0][:].rearrange("p (r w) -> p r w", r=2), neg_gy_c[:].rearrange("p (r w) -> p r w", r=2), MULT)
+        for engine, lo, hi in shares:
+            gather_bags(engine, 0, by_sample0, lo, hi)
+        for engine, lo, hi in shares:
+            gather_table(engine, 1, lo, hi)
+        by_sample1 = fresh("by_sample1", C)
+        for lo in (0, HALF):
+            gather_bags("scalar", 1, by_sample1, lo, lo + HALF)
+
+        sums0 = placed_at("sums0", table_at[1], X)
+        add_pairs(sums0, by_sample0[:])
+        scaled0 = fresh("scaled0", X)
+        scale_by_gy(scaled0, sums0)
         dz_grouped = keep.tile([P, X, PACK], BF16, name="dz_grouped", align_bytes=64)
-        nc.vector.tensor_copy(*interleaved(dz_grouped, dz_raw, slice(0, X)))
-        w_grouped = keep.tile([P, D // 2, PACK], BF16, name="w_grouped", align_bytes=64)
-        nc.scalar.copy(*interleaved(w_grouped, w_raw[0], slice(0, D // 2)))
+        nc.vector.tensor_copy(*interleaved(dz_grouped, dz_raw))
         dz_planes = quantise(dz_grouped, "dz", E5M2X4)
-        sums0 = keep.tile([P, X], F32, name="sums0", tag="dz_raw")
-        add_pairs(sums0[:], 0, 0, X)
-        w_planes = quantise(w_grouped, "w_low", E4M3X4)
+        sums1 = placed_at("sums1", dz_at, X)
+        add_pairs(sums1, by_sample1[:])
+        w_low = keep.tile([P, D // 2, PACK], BF16, name="w_low", align_bytes=64)
+        nc.scalar.copy(*interleaved(w_low, w_raw[0]))
+        w_planes = quantise(w_low, "w_low", E4M3X4)
         ds = [dense_gradient(t, w_planes, dz_planes) for t in range(2)]
-        nc.vector.tensor_tensor(scaled[0], sums0[:], gy_win[:], MULT)
-        gather_table("scalar", 1)
-        make_e(0, ds[0])
-        first, second, third = ([piece] for piece in SCALAR_PIECES)
-        dv0_first = keep.tile([P, lead], F32, name="dv0_first")
-        finish(0, first, dv0_first, own0[:, :lead])
-        w_grouped = keep.tile([P, D // 2, PACK], BF16, name="w_grouped_high", align_bytes=64)
-        nc.scalar.copy(*interleaved(w_grouped, w_raw[1], slice(0, D // 2)))
-        by_sample[1] = keep.tile([P, C], F32, name="by_sample1", tag="scaled0")
-        for h in range(2):
-            gather_scaled_bags(1, h)
-        dv0_second = keep.tile([P, lead], F32, name="dv0_second", tag="gy_twice0")
-        finish(0, second, dv0_second, own0[:, lead:])
-        add_pairs(scaled[1], 1, 0, X)
-        dv0_third = keep.tile([P, C - 2 * lead], F32, name="dv0_third", tag="gy_twice1")
-        finish(0, third, dv0_third, own0[:, 2 * lead :])
-        store(0)
-        own1_first = chain.tile([P, lead], F32, name="own1_first", offset=word * (C - lead))
-        own1_rest = chain.tile([P, C - lead], F32, name="own1_rest", offset=0)
-        make_own(own1_first[:], 1, 0, lead)
-        make_own(own1_rest[:], 1, lead, C)
-        make_e(1, ds[1])
-        gather_table("vector", 2)
-        for lo in (0, half):
-            gather_bags("scalar", 2, lo, lo + half)
-        w_planes = quantise(w_grouped, "w_high", E4M3X4, word * (TABLE2_AT + C))
-        ds += [dense_gradient(u, w_planes, dz_planes) for u in (2, 3)]
-        dv1_first = keep.tile([P, lead], F32, name="dv1_first")
-        finish(1, first, dv1_first, own1_first)
-        own2 = chain.tile([P, C], F32, name="own2", offset=word * (C - lead))
-        make_own(own2[:], 2, 0, C)
-        placed.append(keep.tile([P, T], F32, name="placed3", tag="picked2"))
-        nc.gpsimd.memset(placed[3][:], 0.0)
-        picked[3] = chain.tile([P, C], F32, name="picked3", offset=word * TABLE2_AT)
+        scaled1 = placed_at("scaled1", w_at - X // 2, X)
+        scale_by_gy(scaled1, sums1)
+        own1 = placed_at("own1", w_at + C - PIECE, C)
+        nc.vector.tensor_tensor(own1[:, :HALF], picked[1][:, :HALF], neg_gy_c[:, :HALF], MULT)
+        e0 = fresh("e0", X)
+        make_e(e0, ds[0], scaled0)
+        nc.vector.tensor_tensor(own1[:, HALF:], picked[1][:, HALF:], neg_gy_c[:, HALF:], MULT)
+
+        gather_table("scalar", 2)
+        for k in range(2):
+            gather_bags("scalar", 2, relay, k * PIECE, (k + 1) * PIECE)
+        dv0_first = placed_at("dv0_first", table_at[2], HALF)
+        for k in range(2):
+            finish(0, k, e0, piece(dv0_first, k), own0[k])
+            gather_bags("scalar", 2, relay, (k + 2) * PIECE, (k + 3) * PIECE)
+        own2 = relay[:, own2_at : own2_at + C]
+        nc.gpsimd.tensor_tensor(own2, picked[2][:], neg_gy_c[:], MULT)
         gather_table("vector", 3)
-        for lo in (0, half):
-            gather_bags("scalar", 3, lo, lo + half)
-        behind_table = keep.tile([P, X + C - lead], F32, name="behind_table", tag="table3", align_bytes=64)
-        finish(1, second, behind_table[:, X:], own1_rest)
-        halves = [slice(0, X // 2), slice(X // 2, X)]
-        for part in halves:
-            add_pairs(behind_table[:, part], 2, part.start, part.stop)
-        for part in halves:
-            nc.vector.tensor_tensor(scaled[2][:, part], behind_table[:, part], gy_win[:, part], MULT)
-        for part in halves:
-            nc.vector.tensor_tensor(e[2][:, part], ds[2][:, part], scaled[2][:, part], ADD)
-        finish(1, third, behind_table[:, X + lead :], own1_rest[:, lead:])
-        store(1)
-        dv2 = keep.tile([P, C], F32, name="dv2")
-        sums3 = keep.tile([P, X], F32, name="sums3", tag="scaled2")
-        steps = (
-            lambda: add_pairs(sums3[:], 3, 0, X),
-            lambda: nc.vector.tensor_tensor(scaled[3], sums3[:], gy_win[:], MULT),
-            lambda: make_e(3, ds[3]),
-        )
-        for (lo, hi), step in zip(SCALAR_PIECES, steps):
-            finish(2, [(lo, hi)], dv2[:, lo:], own2[:, lo:])
-            step()
-        own3 = chain.tile([P, C], F32, name="own3", offset=word * (C - lead))
-        make_own(own3[:], 3, 0, C)
-        e_by_slot = keep.tile([P, C], F32, name="e_by_slot")
-        for lo in range(0, C - E_PIECE, E_PIECE):
-            gather("vector", e_by_slot, e[3], bag_list, lo, lo + E_PIECE)
-        store(2)
-        nc.vector.tensor_tensor(placed[3][:].indirect(entries(idx_list, 0, half)), e_by_slot[:, :half], own3[:, :half], ADD)
-        gather("vector", e_by_slot, e[3], bag_list, C - E_PIECE, C)
-        nc.vector.tensor_tensor(placed[3][:].indirect(entries(idx_list, half, C)), e_by_slot[:, half:], own3[:, half:], ADD)
-        store(3)
+        e1 = placed_at("e1", table_at[3], X)
+        make_e(e1, ds[1], scaled1)
+        dv0_last = placed_at("dv0_last", table_at[3] + X, HALF)
+        dv1 = fresh("dv1", C)
+        dv2 = fresh("dv2", C)
+
+        def finish1(k):
+            finish(1, k, e1, piece(dv1, k), piece(own1, k))
+
+        finish(0, 2, e0, piece(dv0_last, 0), own0[2])
+        w_high = keep.tile([P, D // 2, PACK], BF16, name="w_high", align_bytes=64)
+        nc.vector.tensor_copy(*interleaved(w_high, w_raw[1]))
+        finish1(0)
+        w_planes = quantise(w_high, "w_high", E4M3X4)
+        ds += [dense_gradient(t, w_planes, dz_planes) for t in (2, 3)]
+        sums2 = placed_at("sums2", table_at[3] + X + HALF, X)
+        add_pairs(sums2, relay[:, :C])
+        finish(0, 3, e0, piece(dv0_last, 1), own0[3])
+        nc.sync.dma_start(rows(0), windows[0][:])
+        scaled2 = fresh("scaled2", X)
+        scale_by_gy(scaled2, sums2)
+        finish1(1)
+        e2 = fresh("e2", X)
+        make_e(e2, ds[2], scaled2)
+
+        def finish2(k):
+            finish(2, k, e2, piece(dv2, k), piece(relay, k, own2_at))
+
+        by_sample3 = fresh("by_sample3", C)
+        gy_by_pair = gy_twice[:].rearrange("p x j -> p (x j)")
+
+        def gather_scaled_bags(lo, hi):
+            nc.vector.tensor_tensor(by_sample3[:, lo:hi], picked[3][:].indirect(entries(slot_list, lo, hi)), gy_by_pair[:, lo:hi], MULT)
+
+        gather_scaled_bags(0, HALF)
+        finish2(0)
+        gather_scaled_bags(HALF, C)
+        finish1(2)
+        scaled3 = fresh("scaled3", X)
+        add_pairs(scaled3, by_sample3[:])
+        finish2(1)
+        finish1(3)
+        nc.sync.dma_start(rows(1), windows[1][:])
+        finish2(2)
+        e3 = placed_at("e3", table_at[3], X)
+        make_e(e3, ds[3], scaled3)
+        finish2(3)
+        nc.scalar.dma_start(rows(2), windows[2][:])
+        own3 = relay[:, own3_at : own3_at + C]
+        nc.gpsimd.tensor_tensor(own3, picked[3][:], neg_gy_c[:], MULT)
+        e3_by_slot = fresh("e3_by_slot", C)
+        for lo, hi in ((0, 352), (352, 704), (704, C)):
+            gather("vector", e3_by_slot[:, lo:hi], e3, bag_list, lo, hi)
+        nc.vector.tensor_tensor(windows[3][:].indirect(idx_list[:]), e3_by_slot[:], own3, ADD)
+        nc.sync.dma_start(rows(3), windows[3][:])

@@ -23,7 +23,8 @@ WORD = 4
 D_TILES = D // P
 HALF = C // 2
 PIECE = C // 4
-GY_ON_VECTOR = 768
+THIRD = 320
+GY_ON_VECTOR = 640
 
 
 def tile_attend_gfm_bi_kernel(tc, vT, W, dz, gy, offs, boffs, soffs, out):
@@ -52,8 +53,8 @@ def tile_attend_gfm_bi_kernel(tc, vT, W, dz, gy, offs, boffs, soffs, out):
         w_raw = [placed_at("w_raw0", w_at, PACK, D // 2), fresh("w_raw1", PACK, D // 2)]
         w_rows = W.rearrange("(p j) d -> p j d", j=PACK)
 
-        nc.sync.dma_start(bag_list[:], boffs)
         nc.sync.dma_start(gy_win[:], gy)
+        nc.sync.dma_start(bag_list[:], boffs)
         nc.sync.dma_start(idx_list[:], offs)
         nc.sync.dma_start(tables[0][:], vT[0:P, :])
         nc.sync.dma_start(slot_list[:], soffs)
@@ -65,7 +66,7 @@ def tile_attend_gfm_bi_kernel(tc, vT, W, dz, gy, offs, boffs, soffs, out):
         nc.sync.dma_start(w_raw[1][:], w_rows[:, :, D // 2 :])
 
         minus_one = fresh("minus_one", GY_ON_VECTOR // 2)
-        nc.vector.memset(minus_one[:], -1.0)
+        nc.gpsimd.memset(minus_one[:], -1.0)
         windows = [fresh("window%d" % t, T) for t in range(3)]
         for window in windows:
             nc.gpsimd.memset(window[:], 0.0)
@@ -90,10 +91,10 @@ def tile_attend_gfm_bi_kernel(tc, vT, W, dz, gy, offs, boffs, soffs, out):
         def gather_bags(engine, t, dst, lo, hi):
             gather(engine, dst[:, lo:hi], picked[t], slot_list, lo, hi)
 
-        def interleaved(grouped, raw):
+        def interleaved(grouped, raw, cols=slice(None)):
             return (
-                grouped[:].rearrange("p (c i) j -> p c j i", i=4),
-                raw[:].rearrange("p j (c i) -> p c j i", i=4),
+                grouped[:, cols, :].rearrange("p (c i) j -> p c j i", i=4),
+                raw[:, :, cols].rearrange("p j (c i) -> p c j i", i=4),
             )
 
         def quantise(grouped, name, fmt):
@@ -117,18 +118,20 @@ def tile_attend_gfm_bi_kernel(tc, vT, W, dz, gy, offs, boffs, soffs, out):
             )
             return acc
 
+        def two_rows(ap):
+            return ap.rearrange("p (r w) -> p r w", r=2)
+
         def add_pairs(dst, by_sample):
-            pairs = by_sample.rearrange("p (x j) -> p j x", j=2)
-            nc.vector.tensor_tensor(dst[:], pairs[:, 0, :], pairs[:, 1, :], ADD)
+            pairs = by_sample.rearrange("p (r w j) -> p j r w", r=2, j=2)
+            nc.vector.tensor_tensor(dst, pairs[:, 0], pairs[:, 1], ADD)
 
         def scale_by_gy(dst, sums):
-            nc.vector.tensor_tensor(dst[:], sums[:], gy_win[:], MULT)
+            nc.vector.tensor_tensor(dst, sums, two_rows(gy_win[:]), MULT)
 
         def make_e(dst, ds, scaled):
-            nc.vector.tensor_tensor(dst[:], ds[:], scaled[:], ADD)
+            nc.vector.tensor_tensor(two_rows(dst[:]), two_rows(ds[:]), scaled, ADD)
 
-        def finish(t, k, e, values, own):
-            lo, hi = k * PIECE, (k + 1) * PIECE
+        def finish(t, lo, hi, e, values, own):
             nc.vector.tensor_tensor(values, e[:].indirect(entries(bag_list, lo, hi)), own, ADD)
             nc.scalar.activation(windows[t][:].indirect(entries(idx_list, lo, hi)), values, COPY)
 
@@ -138,14 +141,14 @@ def tile_attend_gfm_bi_kernel(tc, vT, W, dz, gy, offs, boffs, soffs, out):
         def rows(t):
             return out[t * P : (t + 1) * P, :]
 
-        gy_twice = fresh("gy_twice", X, 2)
-        nc.scalar.copy(gy_twice[:], gy_win[:].unsqueeze(2).to_broadcast([P, X, 2]))
+        gy_twice = fresh("gy_twice", X // 2, 2)
+        nc.scalar.copy(gy_twice[:], gy_win[:, : X // 2].unsqueeze(2).to_broadcast([P, X // 2, 2]))
         for lo in (0, GY_ON_VECTOR // 2):
             hi = lo + GY_ON_VECTOR // 2
             nc.vector.tensor_tensor(neg_gy_c[:, lo:hi], gy_win[:].indirect(entries(bag_list, lo, hi)), minus_one[:], MULT)
         nc.scalar.activation(neg_gy_c[:, GY_ON_VECTOR:], gy_win[:].indirect(entries(bag_list, GY_ON_VECTOR, C)), COPY, scale=-1.0)
 
-        own0_at, own0_step, own2_at, own3_at = 640, 1408, 1024, 1920
+        own0_at, own0_step, own2_at = 640, 1408, 1024
         relay = fresh("relay", own0_at + 2 * own0_step)
         own0_rows = relay[:, own0_at:].rearrange("p (r w) -> p r w", r=2)[:, :, :HALF]
         own0 = [piece(relay, k % 2, own0_at + k // 2 * own0_step) for k in range(4)]
@@ -163,20 +166,21 @@ def tile_attend_gfm_bi_kernel(tc, vT, W, dz, gy, offs, boffs, soffs, out):
         for lo in (0, HALF):
             gather_bags("scalar", 1, by_sample1, lo, lo + HALF)
 
-        sums0 = placed_at("sums0", table_at[1], X)
+        sums0 = two_rows(placed_at("sums0", table_at[1], X)[:])
         add_pairs(sums0, by_sample0[:])
-        scaled0 = fresh("scaled0", X)
-        scale_by_gy(scaled0, sums0)
         dz_grouped = keep.tile([P, X, PACK], BF16, name="dz_grouped", align_bytes=64)
-        nc.vector.tensor_copy(*interleaved(dz_grouped, dz_raw))
+        for lo in (0, X // 2):
+            nc.vector.tensor_copy(*interleaved(dz_grouped, dz_raw, slice(lo, lo + X // 2)))
+        scaled0 = dz_raw[:, 0:2, : X // 2]
+        scale_by_gy(scaled0, sums0)
         dz_planes = quantise(dz_grouped, "dz", E5M2X4)
-        sums1 = placed_at("sums1", dz_at, X)
+        sums1 = dz_raw[:, 2:4, : X // 2]
         add_pairs(sums1, by_sample1[:])
         w_low = keep.tile([P, D // 2, PACK], BF16, name="w_low", align_bytes=64)
         nc.scalar.copy(*interleaved(w_low, w_raw[0]))
         w_planes = quantise(w_low, "w_low", E4M3X4)
         ds = [dense_gradient(t, w_planes, dz_planes) for t in range(2)]
-        scaled1 = placed_at("scaled1", w_at - X // 2, X)
+        scaled1 = two_rows(placed_at("scaled1", w_at - X // 2, X)[:])
         scale_by_gy(scaled1, sums1)
         own1 = placed_at("own1", w_at + C - PIECE, C)
         nc.vector.tensor_tensor(own1[:, :HALF], picked[1][:, :HALF], neg_gy_c[:, :HALF], MULT)
@@ -189,7 +193,7 @@ def tile_attend_gfm_bi_kernel(tc, vT, W, dz, gy, offs, boffs, soffs, out):
             gather_bags("scalar", 2, relay, k * PIECE, (k + 1) * PIECE)
         dv0_first = placed_at("dv0_first", table_at[2], HALF)
         for k in range(2):
-            finish(0, k, e0, piece(dv0_first, k), own0[k])
+            finish(0, k * PIECE, (k + 1) * PIECE, e0, piece(dv0_first, k), own0[k])
             gather_bags("scalar", 2, relay, (k + 2) * PIECE, (k + 3) * PIECE)
         own2 = relay[:, own2_at : own2_at + C]
         nc.gpsimd.tensor_tensor(own2, picked[2][:], neg_gy_c[:], MULT)
@@ -198,54 +202,52 @@ def tile_attend_gfm_bi_kernel(tc, vT, W, dz, gy, offs, boffs, soffs, out):
         make_e(e1, ds[1], scaled1)
         dv0_last = placed_at("dv0_last", table_at[3] + X, HALF)
         dv1 = fresh("dv1", C)
-        dv2 = fresh("dv2", C)
+        dv2 = fresh("dv2", 2 * THIRD)
 
         def finish1(k):
-            finish(1, k, e1, piece(dv1, k), piece(own1, k))
+            finish(1, k * PIECE, (k + 1) * PIECE, e1, piece(dv1, k), piece(own1, k))
 
-        finish(0, 2, e0, piece(dv0_last, 0), own0[2])
+        finish(0, 2 * PIECE, 3 * PIECE, e0, piece(dv0_last, 0), own0[2])
+        by_sample3 = fresh("by_sample3", C)
+        gather_bags("scalar", 3, by_sample3, HALF, HALF + PIECE)
         w_high = keep.tile([P, D // 2, PACK], BF16, name="w_high", align_bytes=64)
         nc.vector.tensor_copy(*interleaved(w_high, w_raw[1]))
         finish1(0)
+        gather_bags("scalar", 3, by_sample3, HALF + PIECE, C)
         w_planes = quantise(w_high, "w_high", E4M3X4)
         ds += [dense_gradient(t, w_planes, dz_planes) for t in (2, 3)]
-        sums2 = placed_at("sums2", table_at[3] + X + HALF, X)
+        sums2 = two_rows(placed_at("sums2", table_at[3] + X + HALF, X)[:])
         add_pairs(sums2, relay[:, :C])
-        finish(0, 3, e0, piece(dv0_last, 1), own0[3])
+        finish(0, 3 * PIECE, C, e0, piece(dv0_last, 1), own0[3])
         nc.sync.dma_start(rows(0), windows[0][:])
-        scaled2 = fresh("scaled2", X)
+        scaled2 = two_rows(fresh("scaled2", X)[:])
         scale_by_gy(scaled2, sums2)
         finish1(1)
         e2 = fresh("e2", X)
         make_e(e2, ds[2], scaled2)
 
-        def finish2(k):
-            finish(2, k, e2, piece(dv2, k), piece(relay, k, own2_at))
+        def finish2(lo, hi, values):
+            finish(2, lo, hi, e2, values, own2[:, lo:hi])
 
-        by_sample3 = fresh("by_sample3", C)
         gy_by_pair = gy_twice[:].rearrange("p x j -> p (x j)")
-
-        def gather_scaled_bags(lo, hi):
-            nc.vector.tensor_tensor(by_sample3[:, lo:hi], picked[3][:].indirect(entries(slot_list, lo, hi)), gy_by_pair[:, lo:hi], MULT)
-
-        gather_scaled_bags(0, HALF)
-        finish2(0)
-        gather_scaled_bags(HALF, C)
-        finish1(2)
-        scaled3 = fresh("scaled3", X)
+        nc.vector.tensor_tensor(by_sample3[:, :HALF], picked[3][:].indirect(entries(slot_list, 0, HALF)), gy_by_pair, MULT)
+        finish2(0, THIRD, dv2[:, :THIRD])
+        scaled3 = two_rows(fresh("scaled3", X)[:])
         add_pairs(scaled3, by_sample3[:])
-        finish2(1)
+        finish1(2)
+        nc.vector.tensor_tensor(scaled3[:, 1], scaled3[:, 1], gy_win[:, X // 2 :], MULT)
+        finish2(THIRD, 2 * THIRD, dv2[:, THIRD:])
         finish1(3)
         nc.sync.dma_start(rows(1), windows[1][:])
-        finish2(2)
-        e3 = placed_at("e3", table_at[3], X)
+        own3 = placed_at("own3", w_at + C - PIECE, C)
+        nc.gpsimd.tensor_tensor(own3[:], picked[3][:], neg_gy_c[:], MULT)
+        e3 = fresh("e3", X)
         make_e(e3, ds[3], scaled3)
-        finish2(3)
-        nc.scalar.dma_start(rows(2), windows[2][:])
-        own3 = relay[:, own3_at : own3_at + C]
-        nc.gpsimd.tensor_tensor(own3, picked[3][:], neg_gy_c[:], MULT)
         e3_by_slot = fresh("e3_by_slot", C)
         for lo, hi in ((0, 352), (352, 704), (704, C)):
             gather("vector", e3_by_slot[:, lo:hi], e3, bag_list, lo, hi)
-        nc.vector.tensor_tensor(windows[3][:].indirect(idx_list[:]), e3_by_slot[:], own3, ADD)
+        dv2_last = keep.tile([P, C - 2 * THIRD], F32, name="dv2_last", tag="picked3")
+        finish2(2 * THIRD, C, dv2_last[:])
+        nc.scalar.dma_start(rows(2), windows[2][:])
+        nc.vector.tensor_tensor(windows[3][:].indirect(idx_list[:]), e3_by_slot[:], own3[:], ADD)
         nc.sync.dma_start(rows(3), windows[3][:])

@@ -25,6 +25,7 @@ HALF = C // 2
 PIECE = C // 4
 THIRD = 320
 GY_ON_VECTOR = 640
+BAGS3_ON_VECTOR = C - 3 * P
 
 
 def tile_attend_gfm_bi_kernel(tc, vT, W, dz, gy, offs, boffs, soffs, out):
@@ -42,7 +43,11 @@ def tile_attend_gfm_bi_kernel(tc, vT, W, dz, gy, offs, boffs, soffs, out):
 
         table_at = {t: (t - 1) * T for t in (1, 2, 3)}
         dz_at = 3 * T
-        w_at = 4 * T + X
+        rounded_at = 4 * T
+        own0_at, own2_at, late_at = 640, 1024, 2048
+        own1_at = late_at + HALF
+        w_at = own1_at + C - P
+        relay = fresh("relay", w_at + C)
 
         bag_list = keep.tile([P, C // STRIPE], U16, name="bag_list")
         idx_list = keep.tile([P, C // STRIPE], U16, name="idx_list")
@@ -50,7 +55,7 @@ def tile_attend_gfm_bi_kernel(tc, vT, W, dz, gy, offs, boffs, soffs, out):
         gy_win = fresh("gy_win", X)
         tables = [fresh("table0", T)] + [placed_at("table%d" % t, table_at[t], T) for t in (1, 2, 3)]
         dz_raw = placed_at("dz_raw", dz_at, PACK, X)
-        w_raw = [placed_at("w_raw0", w_at, PACK, D // 2), fresh("w_raw1", PACK, D // 2)]
+        w_raw = [relay[:, w_at:].rearrange("p (j d) -> p j d", j=PACK), fresh("w_raw1", PACK, D // 2)[:]]
         w_rows = W.rearrange("(p j) d -> p j d", j=PACK)
 
         nc.sync.dma_start(gy_win[:], gy)
@@ -60,17 +65,16 @@ def tile_attend_gfm_bi_kernel(tc, vT, W, dz, gy, offs, boffs, soffs, out):
         nc.sync.dma_start(slot_list[:], soffs)
         nc.sync.dma_start(tables[1][:], vT[P : 2 * P, :])
         nc.sync.dma_start(dz_raw[:], dz.rearrange("(p j) x -> p j x", j=PACK))
-        nc.sync.dma_start(w_raw[0][:], w_rows[:, :, : D // 2])
+        nc.sync.dma_start(w_raw[0], w_rows[:, :, : D // 2])
         nc.sync.dma_start(tables[2][:], vT[2 * P : 3 * P, :])
         nc.sync.dma_start(tables[3][:], vT[3 * P :, :])
-        nc.sync.dma_start(w_raw[1][:], w_rows[:, :, D // 2 :])
+        nc.sync.dma_start(w_raw[1], w_rows[:, :, D // 2 :])
 
         minus_one = fresh("minus_one", GY_ON_VECTOR // 2)
         nc.gpsimd.memset(minus_one[:], -1.0)
-        windows = [fresh("window%d" % t, T) for t in range(3)]
+        windows = [fresh("window%d" % t, T) for t in range(2)]
         for window in windows:
             nc.gpsimd.memset(window[:], 0.0)
-        windows.append(windows[0])
 
         picked = [fresh("picked%d" % t, C) for t in range(D_TILES)]
         neg_gy_c = fresh("neg_gy_c", C)
@@ -118,18 +122,21 @@ def tile_attend_gfm_bi_kernel(tc, vT, W, dz, gy, offs, boffs, soffs, out):
             )
             return acc
 
-        def two_rows(ap):
-            return ap.rearrange("p (r w) -> p r w", r=2)
+        def four_rows(ap):
+            return ap.rearrange("p (r w) -> p r w", r=4)
 
         def add_pairs(dst, by_sample):
-            pairs = by_sample.rearrange("p (r w j) -> p j r w", r=2, j=2)
+            pairs = by_sample.rearrange("p r (w j) -> p j r w", j=2)
             nc.vector.tensor_tensor(dst, pairs[:, 0], pairs[:, 1], ADD)
 
         def scale_by_gy(dst, sums):
-            nc.vector.tensor_tensor(dst, sums, two_rows(gy_win[:]), MULT)
+            nc.vector.tensor_tensor(dst, sums, four_rows(gy_win[:]), MULT)
 
         def make_e(dst, ds, scaled):
-            nc.vector.tensor_tensor(two_rows(dst[:]), two_rows(ds[:]), scaled, ADD)
+            nc.vector.tensor_tensor(four_rows(dst[:]), four_rows(ds[:]), scaled, ADD)
+
+        def make_own(engine, dst, t, lo, hi):
+            engine.tensor_tensor(dst, picked[t][:, lo:hi], neg_gy_c[:, lo:hi], MULT)
 
         def finish(t, lo, hi, e, values, own):
             nc.vector.tensor_tensor(values, e[:].indirect(entries(bag_list, lo, hi)), own, ADD)
@@ -141,17 +148,16 @@ def tile_attend_gfm_bi_kernel(tc, vT, W, dz, gy, offs, boffs, soffs, out):
         def rows(t):
             return out[t * P : (t + 1) * P, :]
 
-        gy_twice = fresh("gy_twice", X // 2, 2)
-        nc.scalar.copy(gy_twice[:], gy_win[:, : X // 2].unsqueeze(2).to_broadcast([P, X // 2, 2]))
+        early = BAGS3_ON_VECTOR // 2
+        gy_twice = fresh("gy_twice", early, 2)
+        nc.scalar.copy(gy_twice[:], gy_win[:, :early].unsqueeze(2).to_broadcast([P, early, 2]))
         for lo in (0, GY_ON_VECTOR // 2):
             hi = lo + GY_ON_VECTOR // 2
             nc.vector.tensor_tensor(neg_gy_c[:, lo:hi], gy_win[:].indirect(entries(bag_list, lo, hi)), minus_one[:], MULT)
         nc.scalar.activation(neg_gy_c[:, GY_ON_VECTOR:], gy_win[:].indirect(entries(bag_list, GY_ON_VECTOR, C)), COPY, scale=-1.0)
 
-        own0_at, own0_step, own2_at = 640, 1408, 1024
-        relay = fresh("relay", own0_at + 2 * own0_step)
-        own0_rows = relay[:, own0_at:].rearrange("p (r w) -> p r w", r=2)[:, :, :HALF]
-        own0 = [piece(relay, k % 2, own0_at + k // 2 * own0_step) for k in range(4)]
+        own0 = [piece(relay, 0, own0_at), piece(relay, 1, own0_at), piece(relay, 0, late_at), piece(relay, 1, late_at)]
+        own0_rows = relay[:, own0_at : 2 * late_at - own0_at].rearrange("p (r w) -> p r w", r=2)[:, :, :HALF]
 
         shares = (("vector", 0, HALF), ("scalar", HALF, C))
         by_sample0 = fresh("by_sample0", C)
@@ -166,27 +172,28 @@ def tile_attend_gfm_bi_kernel(tc, vT, W, dz, gy, offs, boffs, soffs, out):
         for lo in (0, HALF):
             gather_bags("scalar", 1, by_sample1, lo, lo + HALF)
 
-        sums0 = two_rows(placed_at("sums0", table_at[1], X)[:])
-        add_pairs(sums0, by_sample0[:])
-        dz_grouped = keep.tile([P, X, PACK], BF16, name="dz_grouped", align_bytes=64)
+        sums0 = four_rows(placed_at("sums0", table_at[1], X)[:])
+        add_pairs(sums0, four_rows(by_sample0[:]))
+        dz_grouped = reuse.tile([P, X, PACK], BF16, name="dz_grouped", align_bytes=64, offset=WORD * rounded_at)
         for lo in (0, X // 2):
             nc.vector.tensor_copy(*interleaved(dz_grouped, dz_raw, slice(lo, lo + X // 2)))
-        scaled0 = dz_raw[:, 0:2, : X // 2]
+        scaled0 = dz_raw[:, :, :P]
         scale_by_gy(scaled0, sums0)
         dz_planes = quantise(dz_grouped, "dz", E5M2X4)
-        sums1 = dz_raw[:, 2:4, : X // 2]
-        add_pairs(sums1, by_sample1[:])
-        w_low = keep.tile([P, D // 2, PACK], BF16, name="w_low", align_bytes=64)
+        sums1 = dz_raw[:, :, P : 2 * P]
+        add_pairs(sums1, four_rows(by_sample1[:]))
+        w_low = reuse.tile([P, D // 2, PACK], BF16, name="w_low", align_bytes=64, offset=WORD * (rounded_at + C))
         nc.scalar.copy(*interleaved(w_low, w_raw[0]))
         w_planes = quantise(w_low, "w_low", E4M3X4)
         ds = [dense_gradient(t, w_planes, dz_planes) for t in range(2)]
-        scaled1 = two_rows(placed_at("scaled1", w_at - X // 2, X)[:])
-        scale_by_gy(scaled1, sums1)
-        own1 = placed_at("own1", w_at + C - PIECE, C)
-        nc.vector.tensor_tensor(own1[:, :HALF], picked[1][:, :HALF], neg_gy_c[:, :HALF], MULT)
+        windows += [placed_at("window2", rounded_at, T), windows[0]]
+        nc.gpsimd.memset(windows[2][:], 0.0)
+        own1 = relay[:, own1_at : own1_at + C]
+        make_own(nc.vector, own1, 1, 0, C)
         e0 = fresh("e0", X)
         make_e(e0, ds[0], scaled0)
-        nc.vector.tensor_tensor(own1[:, HALF:], picked[1][:, HALF:], neg_gy_c[:, HALF:], MULT)
+        scaled1 = w_raw[0][:, :, P:]
+        scale_by_gy(scaled1, sums1)
 
         gather_table("scalar", 2)
         for k in range(2):
@@ -196,7 +203,7 @@ def tile_attend_gfm_bi_kernel(tc, vT, W, dz, gy, offs, boffs, soffs, out):
             finish(0, k * PIECE, (k + 1) * PIECE, e0, piece(dv0_first, k), own0[k])
             gather_bags("scalar", 2, relay, (k + 2) * PIECE, (k + 3) * PIECE)
         own2 = relay[:, own2_at : own2_at + C]
-        nc.gpsimd.tensor_tensor(own2, picked[2][:], neg_gy_c[:], MULT)
+        make_own(nc.gpsimd, own2, 2, 0, C)
         gather_table("vector", 3)
         e1 = placed_at("e1", table_at[3], X)
         make_e(e1, ds[1], scaled1)
@@ -208,19 +215,24 @@ def tile_attend_gfm_bi_kernel(tc, vT, W, dz, gy, offs, boffs, soffs, out):
             finish(1, k * PIECE, (k + 1) * PIECE, e1, piece(dv1, k), piece(own1, k))
 
         finish(0, 2 * PIECE, 3 * PIECE, e0, piece(dv0_last, 0), own0[2])
-        by_sample3 = fresh("by_sample3", C)
-        gather_bags("scalar", 3, by_sample3, HALF, HALF + PIECE)
+        bags3_late = four_rows(relay[:, late_at : late_at + C])[:, :3, :P]
+
+        def gather_late_bags(k):
+            gather("scalar", bags3_late[:, k], picked[3], slot_list, BAGS3_ON_VECTOR + k * P, BAGS3_ON_VECTOR + (k + 1) * P)
+
+        gather_late_bags(0)
         w_high = keep.tile([P, D // 2, PACK], BF16, name="w_high", align_bytes=64)
         nc.vector.tensor_copy(*interleaved(w_high, w_raw[1]))
         finish1(0)
-        gather_bags("scalar", 3, by_sample3, HALF + PIECE, C)
+        gather_late_bags(2)
         w_planes = quantise(w_high, "w_high", E4M3X4)
         ds += [dense_gradient(t, w_planes, dz_planes) for t in (2, 3)]
-        sums2 = two_rows(placed_at("sums2", table_at[3] + X + HALF, X)[:])
-        add_pairs(sums2, relay[:, :C])
+        sums2 = four_rows(placed_at("sums2", table_at[3] + X + HALF, X)[:])
+        add_pairs(sums2, four_rows(relay[:, :C]))
         finish(0, 3 * PIECE, C, e0, piece(dv0_last, 1), own0[3])
+        gather_late_bags(1)
         nc.sync.dma_start(rows(0), windows[0][:])
-        scaled2 = two_rows(fresh("scaled2", X)[:])
+        scaled2 = four_rows(fresh("scaled2", X)[:])
         scale_by_gy(scaled2, sums2)
         finish1(1)
         e2 = fresh("e2", X)
@@ -230,24 +242,27 @@ def tile_attend_gfm_bi_kernel(tc, vT, W, dz, gy, offs, boffs, soffs, out):
             finish(2, lo, hi, e2, values, own2[:, lo:hi])
 
         gy_by_pair = gy_twice[:].rearrange("p x j -> p (x j)")
-        nc.vector.tensor_tensor(by_sample3[:, :HALF], picked[3][:].indirect(entries(slot_list, 0, HALF)), gy_by_pair, MULT)
+        bags3_scaled = fresh("bags3_scaled", BAGS3_ON_VECTOR)
+        nc.vector.tensor_tensor(bags3_scaled[:], picked[3][:].indirect(entries(slot_list, 0, BAGS3_ON_VECTOR)), gy_by_pair, MULT)
         finish2(0, THIRD, dv2[:, :THIRD])
-        scaled3 = two_rows(fresh("scaled3", X)[:])
-        add_pairs(scaled3, by_sample3[:])
+        scaled3 = fresh("scaled3", X)
+        add_pairs(four_rows(scaled3[:, :early]), four_rows(bags3_scaled[:]))
         finish1(2)
-        nc.vector.tensor_tensor(scaled3[:, 1], scaled3[:, 1], gy_win[:, X // 2 :], MULT)
+        sums3 = own2[:, : X - early]
+        add_pairs(sums3.rearrange("p (r w) -> p r w", r=3), bags3_late)
         finish2(THIRD, 2 * THIRD, dv2[:, THIRD:])
+        nc.vector.tensor_tensor(scaled3[:, early:], sums3, gy_win[:, early:], MULT)
         finish1(3)
         nc.sync.dma_start(rows(1), windows[1][:])
-        own3 = placed_at("own3", w_at + C - PIECE, C)
-        nc.gpsimd.tensor_tensor(own3[:], picked[3][:], neg_gy_c[:], MULT)
+        own3 = relay[:, w_at:]
+        make_own(nc.gpsimd, own3, 3, 0, C)
         e3 = fresh("e3", X)
-        make_e(e3, ds[3], scaled3)
+        make_e(e3, ds[3], four_rows(scaled3[:]))
         e3_by_slot = fresh("e3_by_slot", C)
         for lo, hi in ((0, 352), (352, 704), (704, C)):
             gather("vector", e3_by_slot[:, lo:hi], e3, bag_list, lo, hi)
         dv2_last = keep.tile([P, C - 2 * THIRD], F32, name="dv2_last", tag="picked3")
         finish2(2 * THIRD, C, dv2_last[:])
         nc.scalar.dma_start(rows(2), windows[2][:])
-        nc.vector.tensor_tensor(windows[3][:].indirect(idx_list[:]), e3_by_slot[:], own3[:], ADD)
+        nc.vector.tensor_tensor(windows[3][:].indirect(idx_list[:]), e3_by_slot[:], own3, ADD)
         nc.sync.dma_start(rows(3), windows[3][:])

@@ -25,7 +25,9 @@ HALF = C // 2
 PIECE = C // 4
 THIRD = 320
 GY_ON_VECTOR = 640
-BAGS3_ON_VECTOR = C - 3 * P
+BAGS3_PIECE = 160
+BAGS3_ON_VECTOR = C - 3 * BAGS3_PIECE
+W_ON_VECTOR = 64
 
 
 def tile_attend_gfm_bi_kernel(tc, vT, W, dz, gy, offs, boffs, soffs, out):
@@ -44,7 +46,7 @@ def tile_attend_gfm_bi_kernel(tc, vT, W, dz, gy, offs, boffs, soffs, out):
         table_at = {t: (t - 1) * T for t in (1, 2, 3)}
         dz_at = 3 * T
         rounded_at = 4 * T
-        own0_at, own2_at, late_at = 640, 1024, 2048
+        own0_at, own2_at, late_at = 640, 1056, 2048
         own1_at = late_at + HALF
         w_at = own1_at + C - P
         relay = fresh("relay", w_at + C)
@@ -180,10 +182,12 @@ def tile_attend_gfm_bi_kernel(tc, vT, W, dz, gy, offs, boffs, soffs, out):
         scaled0 = dz_raw[:, :, :P]
         scale_by_gy(scaled0, sums0)
         dz_planes = quantise(dz_grouped, "dz", E5M2X4)
+        w_low = reuse.tile([P, D // 2, PACK], BF16, name="w_low", align_bytes=64, offset=WORD * (rounded_at + C))
+        nc.vector.tensor_copy(*interleaved(w_low, w_raw[0], slice(P, P + W_ON_VECTOR)))
         sums1 = dz_raw[:, :, P : 2 * P]
         add_pairs(sums1, four_rows(by_sample1[:]))
-        w_low = reuse.tile([P, D // 2, PACK], BF16, name="w_low", align_bytes=64, offset=WORD * (rounded_at + C))
-        nc.scalar.copy(*interleaved(w_low, w_raw[0]))
+        nc.scalar.copy(*interleaved(w_low, w_raw[0], slice(0, P)))
+        nc.scalar.copy(*interleaved(w_low, w_raw[0], slice(P + W_ON_VECTOR, 2 * P)))
         w_planes = quantise(w_low, "w_low", E4M3X4)
         ds = [dense_gradient(t, w_planes, dz_planes) for t in range(2)]
         windows += [placed_at("window2", rounded_at, T), windows[0]]
@@ -198,27 +202,27 @@ def tile_attend_gfm_bi_kernel(tc, vT, W, dz, gy, offs, boffs, soffs, out):
         gather_table("scalar", 2)
         for k in range(2):
             gather_bags("scalar", 2, relay, k * PIECE, (k + 1) * PIECE)
-        dv0_first = placed_at("dv0_first", table_at[2], HALF)
+        dv0_first = placed_at("dv0_first", table_at[2], 3 * PIECE)
         for k in range(2):
             finish(0, k * PIECE, (k + 1) * PIECE, e0, piece(dv0_first, k), own0[k])
             gather_bags("scalar", 2, relay, (k + 2) * PIECE, (k + 3) * PIECE)
+        finish(0, 2 * PIECE, 3 * PIECE, e0, piece(dv0_first, 2), own0[2])
         own2 = relay[:, own2_at : own2_at + C]
         make_own(nc.gpsimd, own2, 2, 0, C)
         gather_table("vector", 3)
         e1 = placed_at("e1", table_at[3], X)
         make_e(e1, ds[1], scaled1)
-        dv0_last = placed_at("dv0_last", table_at[3] + X, HALF)
+        dv0_last = placed_at("dv0_last", table_at[3] + X, PIECE)
         dv1 = fresh("dv1", C)
         dv2 = fresh("dv2", 2 * THIRD)
 
         def finish1(k):
             finish(1, k * PIECE, (k + 1) * PIECE, e1, piece(dv1, k), piece(own1, k))
 
-        finish(0, 2 * PIECE, 3 * PIECE, e0, piece(dv0_last, 0), own0[2])
-        bags3_late = four_rows(relay[:, late_at : late_at + C])[:, :3, :P]
+        bags3_late = four_rows(relay[:, late_at : late_at + C])[:, :3, 32 : 32 + BAGS3_PIECE]
 
         def gather_late_bags(k):
-            gather("scalar", bags3_late[:, k], picked[3], slot_list, BAGS3_ON_VECTOR + k * P, BAGS3_ON_VECTOR + (k + 1) * P)
+            gather("scalar", bags3_late[:, k], picked[3], slot_list, BAGS3_ON_VECTOR + k * BAGS3_PIECE, BAGS3_ON_VECTOR + (k + 1) * BAGS3_PIECE)
 
         gather_late_bags(0)
         w_high = keep.tile([P, D // 2, PACK], BF16, name="w_high", align_bytes=64)
@@ -229,7 +233,7 @@ def tile_attend_gfm_bi_kernel(tc, vT, W, dz, gy, offs, boffs, soffs, out):
         ds += [dense_gradient(t, w_planes, dz_planes) for t in (2, 3)]
         sums2 = four_rows(placed_at("sums2", table_at[3] + X + HALF, X)[:])
         add_pairs(sums2, four_rows(relay[:, :C]))
-        finish(0, 3 * PIECE, C, e0, piece(dv0_last, 1), own0[3])
+        finish(0, 3 * PIECE, C, e0, dv0_last[:], own0[3])
         gather_late_bags(1)
         nc.sync.dma_start(rows(0), windows[0][:])
         scaled2 = four_rows(fresh("scaled2", X)[:])

@@ -56,6 +56,7 @@ def tile_attend_gfm_bi_kernel(tc, vT, W, dz, gy, offs, boffs, soffs, out):
         slot_list = keep.tile([P, C // STRIPE], U16, name="slot_list")
         gy_win = fresh("gy_win", X)
         tables = [fresh("table0", T)] + [placed_at("table%d" % t, table_at[t], T) for t in (1, 2, 3)]
+        picked = [fresh("picked0", C), fresh("picked1", C), placed_at("picked2", rounded_at, C), fresh("picked3", C)]
         dz_raw = placed_at("dz_raw", dz_at, PACK, X)
         w_raw = [relay[:, w_at:].rearrange("p (j d) -> p j d", j=PACK), fresh("w_raw1", PACK, D // 2)[:]]
         w_rows = W.rearrange("(p j) d -> p j d", j=PACK)
@@ -69,8 +70,8 @@ def tile_attend_gfm_bi_kernel(tc, vT, W, dz, gy, offs, boffs, soffs, out):
         nc.sync.dma_start(dz_raw[:], dz.rearrange("(p j) x -> p j x", j=PACK))
         nc.sync.dma_start(w_raw[0], w_rows[:, :, : D // 2])
         nc.sync.dma_start(tables[2][:], vT[2 * P : 3 * P, :])
-        nc.sync.dma_start(tables[3][:], vT[3 * P :, :])
         nc.sync.dma_start(w_raw[1], w_rows[:, :, D // 2 :])
+        nc.sync.dma_start(tables[3][:], vT[3 * P :, :])
 
         minus_one = fresh("minus_one", GY_ON_VECTOR // 2)
         nc.gpsimd.memset(minus_one[:], -1.0)
@@ -78,7 +79,6 @@ def tile_attend_gfm_bi_kernel(tc, vT, W, dz, gy, offs, boffs, soffs, out):
         for window in windows:
             nc.gpsimd.memset(window[:], 0.0)
 
-        picked = [fresh("picked%d" % t, C) for t in range(D_TILES)]
         neg_gy_c = fresh("neg_gy_c", C)
 
         def entries(listed, lo, hi):
@@ -176,13 +176,13 @@ def tile_attend_gfm_bi_kernel(tc, vT, W, dz, gy, offs, boffs, soffs, out):
 
         sums0 = four_rows(placed_at("sums0", table_at[1], X)[:])
         add_pairs(sums0, four_rows(by_sample0[:]))
-        dz_grouped = reuse.tile([P, X, PACK], BF16, name="dz_grouped", align_bytes=64, offset=WORD * rounded_at)
+        dz_grouped = reuse.tile([P, X, PACK], BF16, name="dz_grouped", align_bytes=64, offset=WORD * (rounded_at + T))
         for lo in (0, X // 2):
             nc.vector.tensor_copy(*interleaved(dz_grouped, dz_raw, slice(lo, lo + X // 2)))
         scaled0 = dz_raw[:, :, :P]
         scale_by_gy(scaled0, sums0)
         dz_planes = quantise(dz_grouped, "dz", E5M2X4)
-        w_low = reuse.tile([P, D // 2, PACK], BF16, name="w_low", align_bytes=64, offset=WORD * (rounded_at + C))
+        w_low = reuse.tile([P, D // 2, PACK], BF16, name="w_low", align_bytes=64, offset=WORD * (rounded_at + T + C))
         nc.vector.tensor_copy(*interleaved(w_low, w_raw[0], slice(P, P + W_ON_VECTOR)))
         sums1 = dz_raw[:, :, P : 2 * P]
         add_pairs(sums1, four_rows(by_sample1[:]))
@@ -190,8 +190,6 @@ def tile_attend_gfm_bi_kernel(tc, vT, W, dz, gy, offs, boffs, soffs, out):
         nc.scalar.copy(*interleaved(w_low, w_raw[0], slice(P + W_ON_VECTOR, 2 * P)))
         w_planes = quantise(w_low, "w_low", E4M3X4)
         ds = [dense_gradient(t, w_planes, dz_planes) for t in range(2)]
-        windows += [placed_at("window2", rounded_at, T), windows[0]]
-        nc.gpsimd.memset(windows[2][:], 0.0)
         own1 = relay[:, own1_at : own1_at + C]
         make_own(nc.vector, own1, 1, 0, C)
         e0 = fresh("e0", X)
@@ -203,15 +201,22 @@ def tile_attend_gfm_bi_kernel(tc, vT, W, dz, gy, offs, boffs, soffs, out):
         for k in range(2):
             gather_bags("scalar", 2, relay, k * PIECE, (k + 1) * PIECE)
         dv0_first = placed_at("dv0_first", table_at[2], 3 * PIECE)
-        for k in range(2):
-            finish(0, k * PIECE, (k + 1) * PIECE, e0, piece(dv0_first, k), own0[k])
-            gather_bags("scalar", 2, relay, (k + 2) * PIECE, (k + 3) * PIECE)
+        finish(0, 0, PIECE, e0, piece(dv0_first, 0), own0[0])
+        gather_bags("scalar", 2, relay, 2 * PIECE, 3 * PIECE)
+        w_high = reuse.tile([P, D // 2, PACK], BF16, name="w_high", align_bytes=64, offset=WORD * (table_at[2] + C))
+        nc.vector.tensor_copy(*interleaved(w_high, w_raw[1]))
+        finish(0, PIECE, 2 * PIECE, e0, piece(dv0_first, 1), own0[1])
+        gather_bags("scalar", 2, relay, 3 * PIECE, C)
+        w_planes = quantise(w_high, "w_high", E4M3X4)
+        ds += [dense_gradient(t, w_planes, dz_planes) for t in (2, 3)]
+        windows += [placed_at("window2", rounded_at, T), windows[0]]
         finish(0, 2 * PIECE, 3 * PIECE, e0, piece(dv0_first, 2), own0[2])
         own2 = relay[:, own2_at : own2_at + C]
         make_own(nc.gpsimd, own2, 2, 0, C)
-        gather_table("vector", 3)
-        e1 = placed_at("e1", table_at[3], X)
+        nc.gpsimd.memset(windows[2][:], 0.0)
+        e1 = fresh("e1", X)
         make_e(e1, ds[1], scaled1)
+        gather_table("vector", 3)
         dv0_last = placed_at("dv0_last", table_at[3] + X, PIECE)
         dv1 = fresh("dv1", C)
         dv2 = fresh("dv2", 2 * THIRD)
@@ -225,12 +230,8 @@ def tile_attend_gfm_bi_kernel(tc, vT, W, dz, gy, offs, boffs, soffs, out):
             gather("scalar", bags3_late[:, k], picked[3], slot_list, BAGS3_ON_VECTOR + k * BAGS3_PIECE, BAGS3_ON_VECTOR + (k + 1) * BAGS3_PIECE)
 
         gather_late_bags(0)
-        w_high = keep.tile([P, D // 2, PACK], BF16, name="w_high", align_bytes=64)
-        nc.vector.tensor_copy(*interleaved(w_high, w_raw[1]))
         finish1(0)
         gather_late_bags(2)
-        w_planes = quantise(w_high, "w_high", E4M3X4)
-        ds += [dense_gradient(t, w_planes, dz_planes) for t in (2, 3)]
         sums2 = four_rows(placed_at("sums2", table_at[3] + X + HALF, X)[:])
         add_pairs(sums2, four_rows(relay[:, :C]))
         finish(0, 3 * PIECE, C, e0, dv0_last[:], own0[3])
@@ -252,16 +253,17 @@ def tile_attend_gfm_bi_kernel(tc, vT, W, dz, gy, offs, boffs, soffs, out):
         scaled3 = fresh("scaled3", X)
         add_pairs(four_rows(scaled3[:, :early]), four_rows(bags3_scaled[:]))
         finish1(2)
+        finish2(THIRD, 2 * THIRD, dv2[:, THIRD:])
         sums3 = own2[:, : X - early]
         add_pairs(sums3.rearrange("p (r w) -> p r w", r=3), bags3_late)
-        finish2(THIRD, 2 * THIRD, dv2[:, THIRD:])
-        nc.vector.tensor_tensor(scaled3[:, early:], sums3, gy_win[:, early:], MULT)
         finish1(3)
         nc.sync.dma_start(rows(1), windows[1][:])
+        nc.vector.tensor_tensor(scaled3[:, early:], sums3, gy_win[:, early:], MULT)
         own3 = relay[:, w_at:]
         make_own(nc.gpsimd, own3, 3, 0, C)
-        e3 = fresh("e3", X)
-        make_e(e3, ds[3], four_rows(scaled3[:]))
+        e3 = keep.tile([P, X], F32, name="e3", tag="e1")
+        for part in (slice(0, early), slice(early, X)):
+            nc.vector.tensor_tensor(e3[:, part], ds[3][:, part], scaled3[:, part], ADD)
         e3_by_slot = fresh("e3_by_slot", C)
         for lo, hi in ((0, 352), (352, 704), (704, C)):
             gather("vector", e3_by_slot[:, lo:hi], e3, bag_list, lo, hi)

from contextlib import ExitStack

import concourse.mybir as mybir

D, M, X, C, T = 512, 512, 512, 1024, 2048
FLOPS = 2 * M * D * X

F32 = mybir.dt.float32
BF16 = mybir.dt.bfloat16
U32 = mybir.dt.uint32
U16 = mybir.dt.uint16
U8 = mybir.dt.uint8
E4M3X4 = mybir.dt.float8_e4m3fn_x4
E5M2X4 = mybir.dt.float8_e5m2_x4
COPY = mybir.ActivationFunctionType.Copy
ADD = mybir.AluOpType.add
MULT = mybir.AluOpType.mult

P = 128
PACK = 4
STRIPE = 16
WORD = 4
D_TILES = D // P
HALF = C // 2
PIECE = C // 4
THIRD = 320
GY_ON_VECTOR = 640
BAGS3_PIECE = 160
BAGS3_ON_VECTOR = C - 3 * BAGS3_PIECE
W_ON_VECTOR = 64


def tile_attend_gfm_bi_kernel(tc, vT, W, dz, gy, offs, boffs, soffs, out):
    nc = tc.nc
    with ExitStack() as ctx:
        keep = ctx.enter_context(tc.tile_pool(name="keep", bufs=1))
        reuse = ctx.enter_context(tc.tile_pool(name="reuse", bufs=1))
        psum = ctx.enter_context(tc.psum_pool(name="psum", bufs=1))

        def fresh(name, *shape):
            return keep.tile([P, *shape], F32, name=name)

        def placed_at(name, at, *shape):
            return reuse.tile([P, *shape], F32, name=name, offset=WORD * at)

        table_at = {t: (t - 1) * T for t in (1, 2, 3)}
        dz_at = 3 * T
        rounded_at = 4 * T
        own0_at, own2_at, late_at = 640, 1056, 2048
        own1_at = late_at + HALF
        w_at = own1_at + C - P
        relay = fresh("relay", w_at + C)

        bag_list = keep.tile([P, C // STRIPE], U16, name="bag_list")
        idx_list = keep.tile([P, C // STRIPE], U16, name="idx_list")
        slot_list = keep.tile([P, C // STRIPE], U16, name="slot_list")
        gy_win = fresh("gy_win", X)
        tables = [fresh("table0", T)] + [placed_at("table%d" % t, table_at[t], T) for t in (1, 2, 3)]
        picked = [fresh("picked0", C), fresh("picked1", C), placed_at("picked2", rounded_at, C), fresh("picked3", C)]
        dz_raw = placed_at("dz_raw", dz_at, PACK, X)
        w_raw = [relay[:, w_at:].rearrange("p (j d) -> p j d", j=PACK), fresh("w_raw1", PACK, D // 2)[:]]
        w_rows = W.rearrange("(p j) d -> p j d", j=PACK)

        nc.sync.dma_start(gy_win[:], gy)
        nc.sync.dma_start(bag_list[:], boffs)
        nc.sync.dma_start(idx_list[:], offs)
        nc.sync.dma_start(tables[0][:], vT[0:P, :])
        nc.sync.dma_start(slot_list[:], soffs)
        nc.sync.dma_start(tables[1][:], vT[P : 2 * P, :])
        nc.sync.dma_start(dz_raw[:], dz.rearrange("(p j) x -> p j x", j=PACK))
        nc.sync.dma_start(w_raw[0], w_rows[:, :, : D // 2])
        nc.sync.dma_start(tables[2][:], vT[2 * P : 3 * P, :])
        nc.sync.dma_start(w_raw[1], w_rows[:, :, D // 2 :])
        nc.sync.dma_start(tables[3][:], vT[3 * P :, :])

        minus_one = fresh("minus_one", GY_ON_VECTOR // 2)
        nc.gpsimd.memset(minus_one[:], -1.0)
        windows = [fresh("window%d" % t, T) for t in range(2)]
        for window in windows:
            nc.gpsimd.memset(window[:], 0.0)

        neg_gy_c = fresh("neg_gy_c", C)

        def entries(listed, lo, hi):
            return listed[:, lo // STRIPE : hi // STRIPE]

        def gather(engine, dst, window, listed, lo, hi):
            src = window[:].indirect(entries(listed, lo, hi))
            if engine == "vector":
                nc.vector.tensor_copy(dst, src)
            else:
                nc.scalar.activation(dst, src, COPY)

        def gather_table(engine, t, lo=0, hi=C):
            gather(engine, picked[t][:, lo:hi], tables[t], idx_list, lo, hi)

        def gather_bags(engine, t, dst, lo, hi):
            gather(engine, dst[:, lo:hi], picked[t], slot_list, lo, hi)

        def interleaved(grouped, raw, cols=slice(None)):
            return (
                grouped[:, cols, :].rearrange("p (c i) j -> p c j i", i=4),
                raw[:, :, cols].rearrange("p j (c i) -> p c j i", i=4),
            )

        def quantise(grouped, name, fmt):
            width = grouped.shape[1]
            codes = keep.tile([P, width], U32, name=name + "_codes", align_bytes=64)
            scales = keep.tile([P, width], U8, name=name + "_scales", align_bytes=64)
            nc.vector.quantize_mx(out=codes[:].bitcast(fmt), scales=scales[:], in_=grouped[:].rearrange("p w j -> p (w j)"))
            return codes, scales

        def dense_gradient(t, w_planes, dz_planes):
            acc = psum.tile([P, X], F32, name="ds%d" % t)
            cols = slice(t % 2 * P, (t % 2 + 1) * P)
            nc.tensor.matmul_mx(
                out=acc[:],
                lhsT=w_planes[0][:, cols].bitcast(E4M3X4),
                lhsT_scale=w_planes[1][:, cols],
                rhs=dz_planes[0][:].bitcast(E5M2X4),
                rhs_scale=dz_planes[1][:],
                start=True,
                stop=True,
            )
            return acc

        def four_rows(ap):
            return ap.rearrange("p (r w) -> p r w", r=4)

        def add_pairs(dst, by_sample):
            pairs = by_sample.rearrange("p r (w j) -> p j r w", j=2)
            nc.vector.tensor_tensor(dst, pairs[:, 0], pairs[:, 1], ADD)

        def scale_by_gy(dst, sums):
            nc.vector.tensor_tensor(dst, sums, four_rows(gy_win[:]), MULT)

        def make_e(dst, ds, scaled):
            nc.vector.tensor_tensor(four_rows(dst[:]), four_rows(ds[:]), scaled, ADD)

        def make_own(engine, dst, t, lo, hi):
            engine.tensor_tensor(dst, picked[t][:, lo:hi], neg_gy_c[:, lo:hi], MULT)

        def finish(t, lo, hi, e, values, own):
            nc.vector.tensor_tensor(values, e[:].indirect(entries(bag_list, lo, hi)), own, ADD)
            nc.scalar.activation(windows[t][:].indirect(entries(idx_list, lo, hi)), values, COPY)

        def piece(tile, k, first=0):
            return tile[:, first + k * PIECE : first + (k + 1) * PIECE]

        def rows(t):
            return out[t * P : (t + 1) * P, :]

        early = BAGS3_ON_VECTOR // 2
        gy_twice = fresh("gy_twice", early, 2)
        nc.scalar.copy(gy_twice[:], gy_win[:, :early].unsqueeze(2).to_broadcast([P, early, 2]))
        for lo in (0, GY_ON_VECTOR // 2):
            hi = lo + GY_ON_VECTOR // 2
            nc.vector.tensor_tensor(neg_gy_c[:, lo:hi], gy_win[:].indirect(entries(bag_list, lo, hi)), minus_one[:], MULT)
        nc.scalar.activation(neg_gy_c[:, GY_ON_VECTOR:], gy_win[:].indirect(entries(bag_list, GY_ON_VECTOR, C)), COPY, scale=-1.0)

        own0 = [piece(relay, 0, own0_at), piece(relay, 1, own0_at), piece(relay, 0, late_at), piece(relay, 1, late_at)]
        own0_rows = relay[:, own0_at : 2 * late_at - own0_at].rearrange("p (r w) -> p r w", r=2)[:, :, :HALF]

        shares = (("vector", 0, HALF), ("scalar", HALF, C))
        by_sample0 = fresh("by_sample0", C)
        for engine, lo, hi in shares:
            gather_table(engine, 0, lo, hi)
        nc.gpsimd.tensor_tensor(own0_rows, picked[0][:].rearrange("p (r w) -> p r w", r=2), neg_gy_c[:].rearrange("p (r w) -> p r w", r=2), MULT)
        for engine, lo, hi in shares:
            gather_bags(engine, 0, by_sample0, lo, hi)
        for engine, lo, hi in shares:
            gather_table(engine, 1, lo, hi)
        by_sample1 = fresh("by_sample1", C)
        for lo in (0, HALF):
            gather_bags("scalar", 1, by_sample1, lo, lo + HALF)

        sums0 = four_rows(placed_at("sums0", table_at[1], X)[:])
        add_pairs(sums0, four_rows(by_sample0[:]))
        dz_grouped = reuse.tile([P, X, PACK], BF16, name="dz_grouped", align_bytes=64, offset=WORD * (rounded_at + T))
        for lo in (0, X // 2):
            nc.vector.tensor_copy(*interleaved(dz_grouped, dz_raw, slice(lo, lo + X // 2)))
        scaled0 = dz_raw[:, :, :P]
        scale_by_gy(scaled0, sums0)
        dz_planes = quantise(dz_grouped, "dz", E5M2X4)
        w_low = reuse.tile([P, D // 2, PACK], BF16, name="w_low", align_bytes=64, offset=WORD * (rounded_at + T + C))
        nc.vector.tensor_copy(*interleaved(w_low, w_raw[0], slice(P, P + W_ON_VECTOR)))
        sums1 = dz_raw[:, :, P : 2 * P]
        add_pairs(sums1, four_rows(by_sample1[:]))
        nc.scalar.copy(*interleaved(w_low, w_raw[0], slice(0, P)))
        nc.scalar.copy(*interleaved(w_low, w_raw[0], slice(P + W_ON_VECTOR, 2 * P)))
        w_planes = quantise(w_low, "w_low", E4M3X4)
        ds = [dense_gradient(t, w_planes, dz_planes) for t in range(2)]
        own1 = relay[:, own1_at : own1_at + C]
        make_own(nc.vector, own1, 1, 0, C)
        e0 = fresh("e0", X)
        make_e(e0, ds[0], scaled0)
        scaled1 = w_raw[0][:, :, P:]
        scale_by_gy(scaled1, sums1)

        gather_table("scalar", 2)
        for k in range(2):
            gather_bags("scalar", 2, relay, k * PIECE, (k + 1) * PIECE)
        dv0_first = placed_at("dv0_first", table_at[2], 3 * PIECE)
        finish(0, 0, PIECE, e0, piece(dv0_first, 0), own0[0])
        gather_bags("scalar", 2, relay, 2 * PIECE, 3 * PIECE)
        w_high = reuse.tile([P, D // 2, PACK], BF16, name="w_high", align_bytes=64, offset=WORD * (table_at[2] + C))
        nc.vector.tensor_copy(*interleaved(w_high, w_raw[1]))
        finish(0, PIECE, 2 * PIECE, e0, piece(dv0_first, 1), own0[1])
        gather_bags("scalar", 2, relay, 3 * PIECE, C)
        w_planes = quantise(w_high, "w_high", E4M3X4)
        ds += [dense_gradient(t, w_planes, dz_planes) for t in (2, 3)]
        windows += [placed_at("window2", rounded_at, T), windows[0]]
        finish(0, 2 * PIECE, 3 * PIECE, e0, piece(dv0_first, 2), own0[2])
        own2 = relay[:, own2_at : own2_at + C]
        make_own(nc.gpsimd, own2, 2, 0, C)
        nc.gpsimd.memset(windows[2][:], 0.0)
        e1 = fresh("e1", X)
        make_e(e1, ds[1], scaled1)
        gather_table("vector", 3)
        dv0_last = placed_at("dv0_last", table_at[3] + X, PIECE)
        dv1 = fresh("dv1", C)
        dv2 = fresh("dv2", 2 * THIRD)

        def finish1(k):
            finish(1, k * PIECE, (k + 1) * PIECE, e1, piece(dv1, k), piece(own1, k))

        bags3_late = four_rows(relay[:, late_at : late_at + C])[:, :3, 32 : 32 + BAGS3_PIECE]

        def gather_late_bags(k):
            gather("scalar", bags3_late[:, k], picked[3], slot_list, BAGS3_ON_VECTOR + k * BAGS3_PIECE, BAGS3_ON_VECTOR + (k + 1) * BAGS3_PIECE)

        gather_late_bags(0)
        finish1(0)
        gather_late_bags(2)
        sums2 = four_rows(placed_at("sums2", table_at[3] + X + HALF, X)[:])
        add_pairs(sums2, four_rows(relay[:, :C]))
        finish(0, 3 * PIECE, C, e0, dv0_last[:], own0[3])
        gather_late_bags(1)
        nc.sync.dma_start(rows(0), windows[0][:])
        scaled2 = four_rows(fresh("scaled2", X)[:])
        scale_by_gy(scaled2, sums2)
        finish1(1)
        e2 = fresh("e2", X)
        make_e(e2, ds[2], scaled2)

        def finish2(lo, hi, values):
            finish(2, lo, hi, e2, values, own2[:, lo:hi])

        gy_by_pair = gy_twice[:].rearrange("p x j -> p (x j)")
        bags3_scaled = fresh("bags3_scaled", BAGS3_ON_VECTOR)
        nc.vector.tensor_tensor(bags3_scaled[:], picked[3][:].indirect(entries(slot_list, 0, BAGS3_ON_VECTOR)), gy_by_pair, MULT)
        finish2(0, THIRD, dv2[:, :THIRD])
        scaled3 = fresh("scaled3", X)
        add_pairs(four_rows(scaled3[:, :early]), four_rows(bags3_scaled[:]))
        finish1(2)
        finish2(THIRD, 2 * THIRD, dv2[:, THIRD:])
        sums3 = own2[:, : X - early]
        add_pairs(sums3.rearrange("p (r w) -> p r w", r=3), bags3_late)
        finish1(3)
        nc.sync.dma_start(rows(1), windows[1][:])
        nc.vector.tensor_tensor(scaled3[:, early:], sums3, gy_win[:, early:], MULT)
        own3 = relay[:, w_at:]
        make_own(nc.gpsimd, own3, 3, 0, C)
        e3 = keep.tile([P, X], F32, name="e3", tag="e1")
        for part in (slice(0, early), slice(early, X)):
            nc.vector.tensor_tensor(e3[:, part], ds[3][:, part], scaled3[:, part], ADD)
        e3_by_slot = fresh("e3_by_slot", C)
        for lo, hi in ((0, 352), (352, 704), (704, C)):
            gather("vector", e3_by_slot[:, lo:hi], e3, bag_list, lo, hi)
        dv2_last = keep.tile([P, C - 2 * THIRD], F32, name="dv2_last", tag="picked3")
        finish2(2 * THIRD, C, dv2_last[:])
        nc.scalar.dma_start(rows(2), windows[2][:])
        nc.vector.tensor_tensor(windows[3][:].indirect(idx_list[:]), e3_by_slot[:], own3, ADD)
        nc.sync.dma_start(rows(3), windows[3][:])
